import numpy as np
import ml_dtypes


def mxq(x, axis, fmt="e4m3"):
    dtype, down = {"e4m3": (ml_dtypes.float8_e4m3fn, 7), "e5m2": (ml_dtypes.float8_e5m2, 14)}[fmt]
    v = np.moveaxis(np.asarray(x, np.float32).astype(ml_dtypes.bfloat16).astype(np.float64), axis, -1)
    blocks = v.reshape(v.shape[:-1] + (-1, 32))
    amax = np.abs(blocks).max(-1, keepdims=True)
    byte = np.maximum(np.where(amax > 0, np.frexp(amax)[1] - 1 + 127, 0) - down, 1)
    scale = np.exp2(byte - 127.0)
    codes = (blocks / scale).astype(np.float32).astype(dtype).astype(np.float64)
    return np.moveaxis((codes * scale).reshape(v.shape), -1, axis)


WIDE = False


def mx_kscale(k):
    if not WIDE:
        return np.ones(k)
    levels = np.array([18, -18])
    if k % 512:
        return np.exp2(np.random.permutation(np.resize(levels, k // 32))).repeat(32)
    a = np.empty((k // 512, 16))
    for p in range(k // 512):
        a[p, :8] = np.random.permutation(np.resize(levels, 8))
        for g in range(8):
            far = levels[np.abs(levels - a[p, g]) >= 10]
            a[p, g + 8] = far[np.random.randint(len(far))]
    return np.exp2(a.ravel()).repeat(32)


def f64(x):
    return np.asarray(x).astype(np.float64)


def striped(idx):
    return np.tile(np.asarray(idx).reshape(-1, 16).T, (8, 1)).astype(np.uint16)


def unstriped(offs):
    return offs[:16].T.reshape(-1).astype(np.int64)


B, N, T, D, R, TU = 2, 512, 2048, 512, 512, 2048


def setup_inputs():
    n = np.random.standard_normal
    idx = np.random.permutation(T)[:B * N]
    uidx = np.random.permutation(TU)[:B * R]
    s = mx_kscale(D)[:, None]
    z = np.ones(TU)
    z[uidx] = mx_kscale(B * R)
    u = np.ones(T)
    u[idx] = mx_kscale(B * N)
    r = np.random.uniform(0.5, 2.0, T) * u
    ur = np.random.uniform(0.5, 2.0, TU) * z
    return {
        "uT": (n((D, TU)) * s / ur).astype(np.float32),
        "vT": (n((D, T)) * (1.00 / np.sqrt(D)) / s / r).astype(np.float32),
        "y": n((B, R, N)).astype(np.float32),
        "us": ur[uidx].reshape(B, R, 1).astype(np.float32),
        "ts": np.tile(r, (128, 1)).astype(np.float32),
        "offs": striped(idx),
        "uoffs": striped(uidx),
    }


def reference(uT, vT, y, us, ts, offs, uoffs):
    idx = unstriped(offs)
    pick = lambda x: x[:, idx].reshape(x.shape[0], B, N).transpose(1, 0, 2)
    uidx = unstriped(uoffs)
    w = pick(f64(vT))
    x = f64(uT)[:, uidx].reshape(D, B, R).transpose(1, 0, 2)
    a = mxq(x, 1, "e4m3").transpose(0, 2, 1) @ mxq(w, 1, "e4m3")
    sc = f64(us) * pick(f64(ts))[:, :1, :]
    a = a * sc
    g = (a - f64(y))
    h = sc * g
    du = mxq(w, 2, "e4m3") @ mxq(h, 2, "e5m2").transpose(0, 2, 1)
    gu = np.zeros((D, TU))
    gu[:, uidx] = du.transpose(1, 0, 2).reshape(D, B * R)
    return gu

@@ -1,0 +1,189 @@
+from contextlib import ExitStack
+
+import concourse.mybir as mybir
+from concourse.masks import make_identity
+
+B, N, T, D, R, TU = 2, 512, 2048, 512, 512, 2048
+FLOPS = 2 * 2 * B * N * R * D
+
+F32 = mybir.dt.float32
+BF16 = mybir.dt.bfloat16
+U32 = mybir.dt.uint32
+U16 = mybir.dt.uint16
+U8 = mybir.dt.uint8
+E4 = mybir.dt.float8_e4m3fn_x4
+E5 = mybir.dt.float8_e5m2_x4
+MULT = mybir.AluOpType.mult
+COPY = mybir.ActivationFunctionType.Copy
+SQUARE = mybir.ActivationFunctionType.Square
+
+P = 128
+PACK = 4
+LIST_COLS = N // 16
+
+CHUNKS = (
+    ((0, 512, 0), (512, 1024, 0), (1024, 2048, 256)),
+    ((0, 1024, 256), (1024, 2048, 256)),
+    ((0, 1024, 256), (1024, 2048, 256)),
+    ((0, 1024, 256), (1024, 1536, 128), (1536, 2048, 320)),
+)
+
+
+def tile_attend_gmf_sq_u_kernel(tc, uT, vT, y, us, ts, offs, uoffs, out):
+    nc = tc.nc
+    with ExitStack() as ctx:
+        keep = ctx.enter_context(tc.tile_pool(name="keep", bufs=1))
+        ring = ctx.enter_context(tc.tile_pool(name="ring", bufs=4))
+        psum = ctx.enter_context(tc.psum_pool(name="psum", bufs=2))
+
+        item_list = keep.tile([P, B * LIST_COLS], U16, name="item_list")
+        user_list = keep.tile([P, B * LIST_COLS], U16, name="user_list")
+        nc.sync.dma_start(item_list[:], offs)
+        nc.sync.dma_start(user_list[:], uoffs)
+
+        ts_table = keep.tile([P, T], F32, name="ts_table")
+        us_rows = keep.tile([P, P], F32, name="us_rows")
+        nc.vector.memset(ts_table[:], 0.0)
+        nc.gpsimd.memset(us_rows[:], 0.0)
+        nc.scalar.dma_start(ts_table[0:1, :], ts[0:1, :])
+        nc.scalar.dma_start(us_rows[0 : B * PACK, :], us.rearrange("b (c p) o -> (b c) (p o)", p=P))
+        ident = keep.tile([P, P], F32, name="ident")
+        make_identity(nc, ident[:])
+
+        windows = [keep.tile([P, TU], F32, name="window%d" % j) for j in range(PACK)]
+        for j in range(PACK):
+            nc.vector.memset(windows[j][:], 0.0)
+
+        pairs = []
+        raws = []
+        for n, (table, half) in enumerate(((vT, 0), (vT, 1), (uT, 0), (uT, 1))):
+            planes = table.rearrange("(p t) c -> p t c", t=PACK)[:, 2 * half : 2 * half + 2, :]
+            for c0, c1, share in CHUNKS[n]:
+                raw = keep.tile([P, 2, c1 - c0], F32, name="raw%d_%d" % (n, c0), tag="raw%d_%d" % (n, c0))
+                nc.sync.dma_start(raw[:], planes[:, :, c0:c1])
+                raws.append((n, c0, c1, share, raw))
+            pairs.append(keep.tile([P, T, 2], BF16, name="pair%d" % n, align_bytes=64))
+        for n, c0, c1, share, raw in raws:
+            cut = c1 - c0 - share
+            src = raw[:].rearrange("p e c -> p c e")
+            nc.scalar.activation(pairs[n][:, c0 : c0 + cut, :], src[:, 0:cut, :], COPY)
+            if share:
+                nc.vector.tensor_copy(pairs[n][:, c0 + cut : c1, :], src[:, cut:, :])
+        targets = []
+        for b, c0, c1, tag in ((0, 0, 2, "raw0_0"), (0, 2, 4, "raw0_512"), (1, 0, 4, "raw0_1024")):
+            tgt = keep.tile([P, c1 - c0, N], F32, name="y%d_%d" % (b, c0), tag=tag)
+            targets.append((tgt, y[b].rearrange("(c p) i -> p c i", p=P)[:, c0:c1, :]))
+        y_rows = [targets[0][0][:, 0, :], targets[0][0][:, 1, :], targets[1][0][:, 0, :], targets[1][0][:, 1, :]]
+        y_rows = y_rows + [targets[2][0][:, c, :] for c in range(PACK)]
+        for tgt, src in targets:
+            nc.sync.dma_start(tgt[:], src)
+        words = [pair[:].rearrange("p c e -> p (c e)").bitcast(U32) for pair in pairs]
+
+        us_bank = psum.tile([P, PACK, P], F32, name="us_bank", tag="turn")
+        nc.tensor.transpose(us_bank[:, 0, :], us_rows[:], ident[:])
+        us_neg = keep.tile([P, B * PACK], F32, name="us_neg")
+        us_sq = keep.tile([P, B * PACK], F32, name="us_sq")
+        nc.scalar.activation(us_neg[:], us_bank[:, 0, 0 : B * PACK], COPY, scale=-1.0)
+        nc.gpsimd.tensor_tensor(us_sq[:], us_neg[:], us_neg[:], MULT)
+
+        def quantise(name, src, fmt):
+            codes = keep.tile([P, N], U32, name=name + "_codes", align_bytes=64)
+            scales = keep.tile([P, N], U8, name=name + "_scales", align_bytes=64)
+            nc.vector.quantize_mx(codes[:].bitcast(fmt), scales[:], src)
+            return codes, scales
+
+        def item_scales(b):
+            picked = keep.tile([P, N], F32, name="ts_picked%d" % b)
+            nc.vector.tensor_copy(picked[:], ts_table[:].indirect(item_list[:, b * LIST_COLS : (b + 1) * LIST_COLS]))
+            bank = psum.tile([P, PACK, P], F32, name="ts_turned", tag="turn")
+            for t in range(PACK):
+                nc.tensor.transpose(bank[:, t, :], picked[:, t:N:PACK], ident[:])
+            cols = keep.tile([P, PACK], F32, name="ts_cols%d" % b)
+            nc.scalar.activation(cols[:], bank[:, :, 0], COPY)
+            spread = psum.tile([P, PACK, P], F32, name="ts_spread", tag="turn")
+            for t in range(PACK):
+                nc.tensor.transpose(spread[:, t, :], cols[:, t : t + 1].to_broadcast([P, P]), ident[:])
+            plain = keep.tile([P, P, PACK], F32, name="ts_plain%d" % b)
+            square = keep.tile([P, N], F32, name="ts_square%d" % b)
+            nc.scalar.activation(square[:], spread[:].rearrange("p t q -> p (t q)"), SQUARE)
+            nc.scalar.activation(plain[:], spread[:].rearrange("p t q -> p q t"), COPY)
+            return plain, square
+
+        def items(b):
+            picked = keep.tile([P, 2, N], U32, name="v_picked%d" % b)
+            for u in range(2):
+                nc.vector.tensor_copy(picked[:, u, :], words[u].indirect(item_list[:, b * LIST_COLS : (b + 1) * LIST_COLS]))
+            woven = keep.tile([P, N, 2], U32, name="v_woven%d" % b, align_bytes=64)
+            nc.scalar.copy(
+                woven[:].rearrange("p (t q) u -> p q t u", t=PACK),
+                picked[:].rearrange("p u (q t) -> p q t u", t=PACK),
+            )
+            flat = woven[:].rearrange("p c u -> p (c u)")
+            along_d = quantise("v%d" % b, flat.bitcast(BF16), E4)
+            return flat, along_d
+
+        def items_turned(b, flat):
+            turned = keep.tile([P, 2, 2, P, PACK], BF16, name="v_turned%d" % b, align_bytes=64)
+            for u in range(2):
+                bank = psum.tile([P, PACK, P], F32, name="v_bank", tag="turn")
+                for t in range(PACK):
+                    nc.tensor.transpose(bank[:, t, :], flat.bitcast(F32)[:, 2 * P * t + u : 2 * P * (t + 1) : 2], ident[:])
+                halves = bank[:].rearrange("p t m -> p (t m)").bitcast(BF16)
+                nc.scalar.copy(turned[:, u], halves.rearrange("p (t m e) -> p e m t", t=PACK, e=2))
+            return quantise("vt%d" % b, turned[:].rearrange("p u e m t -> p (u e m t)"), E4)
+
+        def users(b):
+            woven = keep.tile([P, R, 2], U32, name="u_woven%d" % b, align_bytes=64)
+            for u in range(2):
+                nc.vector.tensor_copy(woven[:, :, u], words[2 + u].indirect(user_list[:, b * LIST_COLS : (b + 1) * LIST_COLS]))
+            return quantise("u%d" % b, woven[:].rearrange("p c u -> p (c u)").bitcast(BF16), E4)
+
+        def gradient(b, u_mx, v_mx, ts_plain, ts_square):
+            h = keep.tile([P, R, PACK], BF16, name="h%d" % b, align_bytes=64)
+            for c in range(PACK):
+                rows = slice(c * P, (c + 1) * P)
+                col = slice(b * PACK + c, b * PACK + c + 1)
+                scores = psum.tile([P, N], F32, name="scores", tag="scores")
+                nc.tensor.matmul_mx(
+                    scores[:], lhsT=u_mx[0][:, rows].bitcast(E4), lhsT_scale=u_mx[1][:, rows],
+                    rhs=v_mx[0][:].bitcast(E4), rhs_scale=v_mx[1][:], start=True, stop=True,
+                )
+                model = ring.tile([P, N], F32, name="model", bufs=3)
+                nc.vector.scalar_tensor_tensor(model[:], scores[:], us_sq[:, col], ts_square[:], MULT, MULT)
+                target = ring.tile([P, PACK, P], F32, name="target")
+                nc.vector.scalar_tensor_tensor(
+                    target[:].rearrange("p t q -> p q t"),
+                    y_rows[b * PACK + c].rearrange("p (q t) -> p q t", t=PACK),
+                    us_neg[:, col], ts_plain[:], MULT, MULT,
+                )
+                bank = psum.tile([P, PACK, P], F32, name="h_bank", tag="h_bank")
+                for t in range(PACK):
+                    nc.tensor.matmul(bank[:, t, :], target[:, t, :], ident[:], start=True, stop=False, is_transpose=True)
+                    nc.tensor.matmul(bank[:, t, :], model[:, t * P : (t + 1) * P], ident[:], start=False, stop=True, is_transpose=True)
+                nc.scalar.copy(h[:, rows, :], bank[:].rearrange("p t r -> p r t"))
+            return quantise("h%d" % b, h[:].rearrange("p r t -> p (r t)"), E5)
+
+        def scatter(b, vt_mx, h_mx):
+            for j in range(PACK):
+                cols = slice(j * P, (j + 1) * P)
+                bank = psum.tile([P, R], F32, name="du_bank", tag="du_bank")
+                nc.tensor.matmul_mx(
+                    bank[:], lhsT=vt_mx[0][:, cols].bitcast(E4), lhsT_scale=vt_mx[1][:, cols],
+                    rhs=h_mx[0][:].bitcast(E5), rhs_scale=h_mx[1][:], start=True, stop=True,
+                )
+                du = ring.tile([P, R], F32, name="du", bufs=3)
+                nc.scalar.copy(du[:], bank[:])
+                nc.vector.tensor_copy(windows[j][:].indirect(user_list[:, b * LIST_COLS : (b + 1) * LIST_COLS]), du[:])
+                if b == B - 1:
+                    nc.sync.dma_start(out.rearrange("(m j) c -> m j c", j=PACK)[:, j, :], windows[j][:])
+
+        scales = [item_scales(b) for b in range(B)]
+        h_mx = []
+        vt_mx = []
+        for b in range(B):
+            flat, v_mx = items(b)
+            u_mx = users(b)
+            vt_mx.append(items_turned(b, flat))
+            h_mx.append(gradient(b, u_mx, v_mx, *scales[b]))
+        for b in range(B):
+            scatter(b, vt_mx[b], h_mx[b])

@@ -9,23 +9,26 @@ FLOPS = 2 * 2 * B * N * R * D
 F32 = mybir.dt.float32
 BF16 = mybir.dt.bfloat16
 U32 = mybir.dt.uint32
+I32 = mybir.dt.int32
 U16 = mybir.dt.uint16
 U8 = mybir.dt.uint8
 E4 = mybir.dt.float8_e4m3fn_x4
 E5 = mybir.dt.float8_e5m2_x4
 MULT = mybir.AluOpType.mult
-COPY = mybir.ActivationFunctionType.Copy
 SQUARE = mybir.ActivationFunctionType.Square
+COPY = mybir.ActivationFunctionType.Copy
 
 P = 128
 PACK = 4
 LIST_COLS = N // 16
+ALIGN = 256
 
-CHUNKS = (
-    ((0, 512, 0), (512, 1024, 0), (1024, 2048, 256)),
-    ((0, 1024, 256), (1024, 2048, 256)),
-    ((0, 1024, 256), (1024, 2048, 256)),
-    ((0, 1024, 256), (1024, 1536, 128), (1536, 2048, 320)),
+SMALL_SHARE, LARGE_SHARE = 384, 640
+LOADS = (
+    ((0, 1024, 0), (1024, 2048, LARGE_SHARE)),
+    ((0, 1024, SMALL_SHARE), (1024, 2048, LARGE_SHARE)),
+    ((0, 1024, 0), (1024, 2048, SMALL_SHARE)),
+    ((0, 1024, 0), (1024, 1536, SMALL_SHARE), (1536, 2048, SMALL_SHARE)),
 )
 
 
@@ -33,8 +36,16 @@ def tile_attend_gmf_sq_u_kernel(tc, uT, vT, y, us, ts, offs, uoffs, out):
     nc = tc.nc
     with ExitStack() as ctx:
         keep = ctx.enter_context(tc.tile_pool(name="keep", bufs=1))
-        ring = ctx.enter_context(tc.tile_pool(name="ring", bufs=4))
-        psum = ctx.enter_context(tc.psum_pool(name="psum", bufs=2))
+        psum = ctx.enter_context(tc.psum_pool(name="psum", bufs=1))
+
+        def shared(shape, dtype, name, tag):
+            return keep.tile(shape, dtype, name=name, tag=tag, align_bytes=ALIGN)
+
+        def bank_tile(shape, name, bank):
+            return psum.tile(shape, F32, name=name, tag="bank%d" % bank)
+
+        def entries(offsets, b):
+            return offsets[:, b * LIST_COLS : (b + 1) * LIST_COLS]
 
         item_list = keep.tile([P, B * LIST_COLS], U16, name="item_list")
         user_list = keep.tile([P, B * LIST_COLS], U16, name="user_list")
@@ -43,147 +54,208 @@ def tile_attend_gmf_sq_u_kernel(tc, uT, vT, y, us, ts, offs, uoffs, out):
 
         ts_table = keep.tile([P, T], F32, name="ts_table")
         us_rows = keep.tile([P, P], F32, name="us_rows")
-        nc.vector.memset(ts_table[:], 0.0)
-        nc.gpsimd.memset(us_rows[:], 0.0)
-        nc.scalar.dma_start(ts_table[0:1, :], ts[0:1, :])
-        nc.scalar.dma_start(us_rows[0 : B * PACK, :], us.rearrange("b (c p) o -> (b c) (p o)", p=P))
+        ts_first = shared([1, T], F32, "ts_first", "pair3")
+        nc.sync.dma_start(ts_first[:], ts[0:1, :])
+        nc.vector.memset(us_rows[:], 0.0)
+        nc.vector.memset(ts_table[:].bitcast(I32), 0)
+        nc.vector.tensor_copy(ts_table[0:1, :], ts_first[:])
+        nc.sync.dma_start(us_rows[0 : B * PACK, :], us.rearrange("b (c p) o -> (b c) (p o)", p=P))
         ident = keep.tile([P, P], F32, name="ident")
         make_identity(nc, ident[:])
 
-        windows = [keep.tile([P, TU], F32, name="window%d" % j) for j in range(PACK)]
-        for j in range(PACK):
-            nc.vector.memset(windows[j][:], 0.0)
+        windows = [keep.tile([P, TU], F32, name="window0")]
+        nc.vector.memset(windows[0][:].bitcast(I32), 0)
 
-        pairs = []
-        raws = []
-        for n, (table, half) in enumerate(((vT, 0), (vT, 1), (uT, 0), (uT, 1))):
-            planes = table.rearrange("(p t) c -> p t c", t=PACK)[:, 2 * half : 2 * half + 2, :]
-            for c0, c1, share in CHUNKS[n]:
-                raw = keep.tile([P, 2, c1 - c0], F32, name="raw%d_%d" % (n, c0), tag="raw%d_%d" % (n, c0))
+        pair_tables = []
+        loaded = []
+        for n, (table, u) in enumerate(((vT, 0), (vT, 1), (uT, 0), (uT, 1))):
+            planes = table.rearrange("(p t) c -> p t c", t=PACK)[:, 2 * u : 2 * u + 2, :]
+            for c0, c1, share in LOADS[n]:
+                raw = shared([P, 2, c1 - c0], F32, "raw%d_%d" % (n, c0), "raw%d_%d" % (n, c0))
                 nc.sync.dma_start(raw[:], planes[:, :, c0:c1])
-                raws.append((n, c0, c1, share, raw))
-            pairs.append(keep.tile([P, T, 2], BF16, name="pair%d" % n, align_bytes=64))
-        for n, c0, c1, share, raw in raws:
-            cut = c1 - c0 - share
-            src = raw[:].rearrange("p e c -> p c e")
-            nc.scalar.activation(pairs[n][:, c0 : c0 + cut, :], src[:, 0:cut, :], COPY)
-            if share:
-                nc.vector.tensor_copy(pairs[n][:, c0 + cut : c1, :], src[:, cut:, :])
-        targets = []
-        for b, c0, c1, tag in ((0, 0, 2, "raw0_0"), (0, 2, 4, "raw0_512"), (1, 0, 4, "raw0_1024")):
-            tgt = keep.tile([P, c1 - c0, N], F32, name="y%d_%d" % (b, c0), tag=tag)
-            targets.append((tgt, y[b].rearrange("(c p) i -> p c i", p=P)[:, c0:c1, :]))
-        y_rows = [targets[0][0][:, 0, :], targets[0][0][:, 1, :], targets[1][0][:, 0, :], targets[1][0][:, 1, :]]
-        y_rows = y_rows + [targets[2][0][:, c, :] for c in range(PACK)]
-        for tgt, src in targets:
-            nc.sync.dma_start(tgt[:], src)
-        words = [pair[:].rearrange("p c e -> p (c e)").bitcast(U32) for pair in pairs]
+                loaded.append((n, c0, c1, share, raw))
+            pair_tables.append(shared([P, T, 2], BF16, "pair%d" % n, "pair%d" % n))
+        pair_words = [pair[:].rearrange("p c e -> p (c e)").bitcast(U32) for pair in pair_tables]
+        item_words, user_words = pair_words[0:2], pair_words[2:4]
 
-        us_bank = psum.tile([P, PACK, P], F32, name="us_bank", tag="turn")
+        def quantise(name, src, fmt, parts):
+            codes = shared([P, N], U32, name + "_codes", name + "_codes")
+            plane = shared([P, N], U8, name + "_scales", name + "_scales")
+            step = N // parts
+            for c0 in range(0, N, step):
+                cols = slice(c0, c0 + step)
+                nc.vector.quantize_mx(codes[:, cols].bitcast(fmt), plane[:, cols], src[:, PACK * c0 : PACK * (c0 + step)])
+            return codes, plane
+
+        def item_scales(b, turn_bank, spread_bank):
+            picked = keep.tile([P, N], F32, name="ts_picked%d" % b)
+            nc.vector.tensor_copy(picked[:], ts_table[:].indirect(entries(item_list, b)))
+            turned = bank_tile([P, PACK, P], "ts_turned", turn_bank)
+            for t in range(PACK):
+                nc.tensor.transpose(turned[:, t, :], picked[:, t:N:PACK], ident[:])
+            cols = keep.tile([P, PACK], F32, name="ts_cols%d" % b)
+            nc.scalar.activation(cols[:], turned[:, :, 0], COPY)
+            spread = bank_tile([P, PACK, P], "ts_spread", spread_bank)
+            for t in range(PACK):
+                nc.tensor.transpose(spread[:, t, :], cols[:, t : t + 1].to_broadcast([P, P]), ident[:])
+            return cols, spread[:].rearrange("p t q -> p (t q)")
+
+        def pick(name, words, offsets, b):
+            picked = keep.tile([P, 2, N], U32, name=name)
+            for u in range(2):
+                nc.vector.tensor_copy(picked[:, u, :], words[u].indirect(entries(offsets, b)))
+            return picked
+
+        def dealing_views(woven, picked):
+            return (
+                woven[:].rearrange("p (t q) u -> p q t u", t=PACK),
+                picked[:].rearrange("p u (q t) -> p q t u", t=PACK),
+            )
+
+        def as_values(woven):
+            return woven[:].rearrange("p c u -> p (c u)").bitcast(BF16)
+
+        def items_along_slots(b, woven, tag, banks):
+            words = woven[:].rearrange("p c u -> p (c u)").bitcast(F32)
+            turned = shared([P, 2, 2, P, PACK], BF16, "v_turned%d" % b, tag)
+            for u in range(2):
+                bank = bank_tile([P, PACK, P], "v_bank", banks[u])
+                for t in range(PACK):
+                    nc.tensor.transpose(bank[:, t, :], words[:, 2 * P * t + u : 2 * P * (t + 1) : 2], ident[:])
+                halves = bank[:].rearrange("p t m -> p (t m)").bitcast(BF16)
+                nc.scalar.copy(turned[:, u], halves.rearrange("p (t m e) -> p e m t", t=PACK, e=2))
+            return quantise("vt%d" % b, turned[:].rearrange("p u e m t -> p (u e m t)"), E4, 1)
+
+        def target_terms(b, tag):
+            target = shared([P, PACK, PACK, P], F32, "target%d" % b, tag)
+            for c in range(PACK):
+                nc.scalar.activation(
+                    target[:, c].rearrange("p t q -> p q t"),
+                    y_rows[b * PACK + c].rearrange("p (q t) -> p q t", t=PACK),
+                    COPY,
+                    scale=us_neg[:, b * PACK + c : b * PACK + c + 1],
+                )
+            return target
+
+        def score_term(b, c, u_mx, v_mx, ts_row, model, bank):
+            rows = slice(c * P, (c + 1) * P)
+            scores = bank_tile([P, N], "scores", bank)
+            nc.tensor.matmul_mx(
+                scores[:], lhsT=u_mx[0][:, rows].bitcast(E4), lhsT_scale=u_mx[1][:, rows],
+                rhs=v_mx[0][:].bitcast(E4), rhs_scale=v_mx[1][:], start=True, stop=True,
+            )
+            nc.vector.scalar_tensor_tensor(
+                model[:, c, :], scores[:], us_sq[:, b * PACK + c : b * PACK + c + 1], ts_row[:], MULT, MULT
+            )
+
+        def turn_and_add(dst, model, target, c, t):
+            nc.tensor.matmul(dst, target[:, c, t, :], ident[:], start=True, stop=False, is_transpose=True)
+            nc.tensor.matmul(dst, model[:, c, t * P : (t + 1) * P], ident[:], start=False, stop=True, is_transpose=True)
+
+        def product(b, j, vt_mx, h_mx, tag, bank):
+            cols = slice(j * P, (j + 1) * P)
+            sums = bank_tile([P, R], "du_bank", bank)
+            nc.tensor.matmul_mx(
+                sums[:], lhsT=vt_mx[0][:, cols].bitcast(E4), lhsT_scale=vt_mx[1][:, cols],
+                rhs=h_mx[0][:].bitcast(E5), rhs_scale=h_mx[1][:], start=True, stop=True,
+            )
+            du = shared([P, R], F32, "du%d_%d" % (b, j), tag)
+            nc.scalar.copy(du[:], sums[:])
+            return du
+
+        us_bank = bank_tile([P, PACK, P], "us_bank", 6)
         nc.tensor.transpose(us_bank[:, 0, :], us_rows[:], ident[:])
         us_neg = keep.tile([P, B * PACK], F32, name="us_neg")
         us_sq = keep.tile([P, B * PACK], F32, name="us_sq")
         nc.scalar.activation(us_neg[:], us_bank[:, 0, 0 : B * PACK], COPY, scale=-1.0)
         nc.gpsimd.tensor_tensor(us_sq[:], us_neg[:], us_neg[:], MULT)
+        ts_spread0 = item_scales(0, 4, 2)[1]
+        ts_cols1, ts_spread1 = item_scales(1, 5, 3)
 
-        def quantise(name, src, fmt):
-            codes = keep.tile([P, N], U32, name=name + "_codes", align_bytes=64)
-            scales = keep.tile([P, N], U8, name=name + "_scales", align_bytes=64)
-            nc.vector.quantize_mx(codes[:].bitcast(fmt), scales[:], src)
-            return codes, scales
+        for n, c0, c1, share, raw in loaded:
+            cut = c1 - c0 - share
+            side_by_side = raw[:].rearrange("p e c -> p c e")
+            nc.scalar.activation(pair_tables[n][:, c0 : c0 + cut, :], side_by_side[:, 0:cut, :], COPY)
+            if share:
+                nc.vector.tensor_copy(pair_tables[n][:, c0 + cut : c1, :], side_by_side[:, cut:, :])
 
-        def item_scales(b):
-            picked = keep.tile([P, N], F32, name="ts_picked%d" % b)
-            nc.vector.tensor_copy(picked[:], ts_table[:].indirect(item_list[:, b * LIST_COLS : (b + 1) * LIST_COLS]))
-            bank = psum.tile([P, PACK, P], F32, name="ts_turned", tag="turn")
+        ts_square0 = keep.tile([P, N], F32, name="ts_square0")
+        ts_row0 = keep.tile([P, N], F32, name="ts_row0")
+        ts_row1 = keep.tile([P, N], F32, name="ts_row1")
+        nc.scalar.activation(ts_square0[:], ts_spread0, SQUARE)
+        nc.scalar.copy(ts_row0[:], ts_spread0)
+        nc.scalar.copy(ts_row1[:], ts_spread1)
+
+        y_rows = []
+        for b, c0, c1, tag in ((0, 0, 2, "y0_first"), (0, 2, 4, "y0_second"), (1, 0, 4, "raw0_1024")):
+            rows_in = shared([P, c1 - c0, N], F32, "y%d_%d" % (b, c0), tag)
+            nc.sync.dma_start(rows_in[:], y[b].rearrange("(c p) i -> p c i", p=P)[:, c0:c1, :])
+            y_rows.extend([rows_in[:, c, :] for c in range(c1 - c0)])
+
+        v_picked0 = pick("v_picked0", item_words, item_list, 0)
+        v_woven0 = shared([P, N, 2], U32, "v_woven0", "v_woven0")
+        dst, src = dealing_views(v_woven0, v_picked0)
+        for t0 in (0, 2):
+            nc.vector.tensor_copy(dst[:, :, t0 : t0 + 2, :].bitcast(I32), src[:, :, t0 : t0 + 2, :].bitcast(I32))
+        v_mx0 = quantise("v0", as_values(v_woven0), E4, 1)
+
+        u_woven0 = shared([P, R, 2], U32, "u_woven0", "u_woven0")
+        for u in range(2):
+            nc.vector.tensor_copy(u_woven0[:, :, u], user_words[u].indirect(entries(user_list, 0)))
+        u_mx0 = quantise("u0", as_values(u_woven0), E4, 1)
+
+        model0 = shared([P, PACK, N], F32, "model0", "raw1_0")
+        target0 = target_terms(0, "raw2_0")
+        for c, bank in enumerate((0, 1, 6, 7)):
+            score_term(0, c, u_mx0, v_mx0, ts_square0, model0, bank)
+            term = target0[:, c].rearrange("p t q -> p (t q)")
+            nc.vector.tensor_tensor(term, term, ts_row0[:], MULT)
+        h0 = shared([P, R, PACK], BF16, "h0", "h0")
+        for c, bank in enumerate((2, 3, 0, 1)):
+            sums = bank_tile([P, PACK, P], "h_bank", bank)
             for t in range(PACK):
-                nc.tensor.transpose(bank[:, t, :], picked[:, t:N:PACK], ident[:])
-            cols = keep.tile([P, PACK], F32, name="ts_cols%d" % b)
-            nc.scalar.activation(cols[:], bank[:, :, 0], COPY)
-            spread = psum.tile([P, PACK, P], F32, name="ts_spread", tag="turn")
-            for t in range(PACK):
-                nc.tensor.transpose(spread[:, t, :], cols[:, t : t + 1].to_broadcast([P, P]), ident[:])
-            plain = keep.tile([P, P, PACK], F32, name="ts_plain%d" % b)
-            square = keep.tile([P, N], F32, name="ts_square%d" % b)
-            nc.scalar.activation(square[:], spread[:].rearrange("p t q -> p (t q)"), SQUARE)
-            nc.scalar.activation(plain[:], spread[:].rearrange("p t q -> p q t"), COPY)
-            return plain, square
+                turn_and_add(sums[:, t, :], model0, target0, c, t)
+            nc.scalar.copy(h0[:, c * P : (c + 1) * P, :], sums[:].rearrange("p t r -> p r t"))
+        vt_mx0 = items_along_slots(0, v_woven0, "raw2_1024", (4, 5))
+        h_mx0 = quantise("h0", h0[:].rearrange("p r t -> p (r t)"), E5, 2)
+        du0 = [product(0, j, vt_mx0, h_mx0, "du0_%d" % j, 6 + j % 2) for j in range(PACK - 1)]
 
-        def items(b):
-            picked = keep.tile([P, 2, N], U32, name="v_picked%d" % b)
-            for u in range(2):
-                nc.vector.tensor_copy(picked[:, u, :], words[u].indirect(item_list[:, b * LIST_COLS : (b + 1) * LIST_COLS]))
-            woven = keep.tile([P, N, 2], U32, name="v_woven%d" % b, align_bytes=64)
-            nc.scalar.copy(
-                woven[:].rearrange("p (t q) u -> p q t u", t=PACK),
-                picked[:].rearrange("p u (q t) -> p q t u", t=PACK),
-            )
-            flat = woven[:].rearrange("p c u -> p (c u)")
-            along_d = quantise("v%d" % b, flat.bitcast(BF16), E4)
-            return flat, along_d
+        u_picked1 = pick("u_picked1", user_words, user_list, 1)
+        v_picked1 = pick("v_picked1", item_words, item_list, 1)
+        v_woven1 = shared([P, N, 2], U32, "v_woven1", "raw3_1024")
+        nc.scalar.copy(*dealing_views(v_woven1, v_picked1))
+        v_mx1 = quantise("v1", as_values(v_woven1), E4, 1)
+        u_woven1 = shared([P, R, 2], U32, "u_woven1", "u_woven1")
+        nc.scalar.copy(u_woven1[:], u_picked1[:].rearrange("p u c -> p c u"))
+        u_mx1 = quantise("u1", as_values(u_woven1), E4, 1)
 
-        def items_turned(b, flat):
-            turned = keep.tile([P, 2, 2, P, PACK], BF16, name="v_turned%d" % b, align_bytes=64)
-            for u in range(2):
-                bank = psum.tile([P, PACK, P], F32, name="v_bank", tag="turn")
-                for t in range(PACK):
-                    nc.tensor.transpose(bank[:, t, :], flat.bitcast(F32)[:, 2 * P * t + u : 2 * P * (t + 1) : 2], ident[:])
-                halves = bank[:].rearrange("p t m -> p (t m)").bitcast(BF16)
-                nc.scalar.copy(turned[:, u], halves.rearrange("p (t m e) -> p e m t", t=PACK, e=2))
-            return quantise("vt%d" % b, turned[:].rearrange("p u e m t -> p (u e m t)"), E4)
-
-        def users(b):
-            woven = keep.tile([P, R, 2], U32, name="u_woven%d" % b, align_bytes=64)
-            for u in range(2):
-                nc.vector.tensor_copy(woven[:, :, u], words[2 + u].indirect(user_list[:, b * LIST_COLS : (b + 1) * LIST_COLS]))
-            return quantise("u%d" % b, woven[:].rearrange("p c u -> p (c u)").bitcast(BF16), E4)
-
-        def gradient(b, u_mx, v_mx, ts_plain, ts_square):
-            h = keep.tile([P, R, PACK], BF16, name="h%d" % b, align_bytes=64)
+        model1 = shared([P, PACK, N], F32, "model1", "raw1_1024")
+        for c, bank in enumerate((4, 5, 2, 3)):
+            score_term(1, c, u_mx1, v_mx1, ts_row1, model1, bank)
+        target1 = target_terms(1, "target1")
+        vt_mx1 = items_along_slots(1, v_woven1, "v_turned1", (2, 3))
+        h1 = shared([P, R, PACK], BF16, "h1", "h1")
+        places1 = shared([P, PACK, R], BF16, "places1", "places1")
+        for t, bank in enumerate((2, 3, 0, 1)):
+            sums = bank_tile([P, PACK, P], "h_bank", bank)
             for c in range(PACK):
-                rows = slice(c * P, (c + 1) * P)
-                col = slice(b * PACK + c, b * PACK + c + 1)
-                scores = psum.tile([P, N], F32, name="scores", tag="scores")
-                nc.tensor.matmul_mx(
-                    scores[:], lhsT=u_mx[0][:, rows].bitcast(E4), lhsT_scale=u_mx[1][:, rows],
-                    rhs=v_mx[0][:].bitcast(E4), rhs_scale=v_mx[1][:], start=True, stop=True,
-                )
-                model = ring.tile([P, N], F32, name="model", bufs=3)
-                nc.vector.scalar_tensor_tensor(model[:], scores[:], us_sq[:, col], ts_square[:], MULT, MULT)
-                target = ring.tile([P, PACK, P], F32, name="target")
-                nc.vector.scalar_tensor_tensor(
-                    target[:].rearrange("p t q -> p q t"),
-                    y_rows[b * PACK + c].rearrange("p (q t) -> p q t", t=PACK),
-                    us_neg[:, col], ts_plain[:], MULT, MULT,
-                )
-                bank = psum.tile([P, PACK, P], F32, name="h_bank", tag="h_bank")
-                for t in range(PACK):
-                    nc.tensor.matmul(bank[:, t, :], target[:, t, :], ident[:], start=True, stop=False, is_transpose=True)
-                    nc.tensor.matmul(bank[:, t, :], model[:, t * P : (t + 1) * P], ident[:], start=False, stop=True, is_transpose=True)
-                nc.scalar.copy(h[:, rows, :], bank[:].rearrange("p t r -> p r t"))
-            return quantise("h%d" % b, h[:].rearrange("p r t -> p (r t)"), E5)
+                turn_and_add(sums[:, c, :], model1, target1, c, t)
+            nc.scalar.activation(places1[:, t, :], sums[:].rearrange("p c r -> p (c r)"), COPY, scale=ts_cols1[:, t : t + 1])
+        nc.scalar.copy(
+            h1[:].rearrange("p (g i) t -> p g t i", i=PACK), places1[:].rearrange("p t (g i) -> p g t i", i=PACK)
+        )
+        h_mx1 = quantise("h1", h1[:].rearrange("p r t -> p (r t)"), E5, 1)
+        du0.append(product(0, PACK - 1, vt_mx0, h_mx0, "places1", 3))
 
-        def scatter(b, vt_mx, h_mx):
-            for j in range(PACK):
-                cols = slice(j * P, (j + 1) * P)
-                bank = psum.tile([P, R], F32, name="du_bank", tag="du_bank")
-                nc.tensor.matmul_mx(
-                    bank[:], lhsT=vt_mx[0][:, cols].bitcast(E4), lhsT_scale=vt_mx[1][:, cols],
-                    rhs=h_mx[0][:].bitcast(E5), rhs_scale=h_mx[1][:], start=True, stop=True,
-                )
-                du = ring.tile([P, R], F32, name="du", bufs=3)
-                nc.scalar.copy(du[:], bank[:])
-                nc.vector.tensor_copy(windows[j][:].indirect(user_list[:, b * LIST_COLS : (b + 1) * LIST_COLS]), du[:])
-                if b == B - 1:
-                    nc.sync.dma_start(out.rearrange("(m j) c -> m j c", j=PACK)[:, j, :], windows[j][:])
+        for j, tag in enumerate(("u_woven0", "u_woven1", "raw1_1024")):
+            window = shared([P, TU], F32, "window%d" % (j + 1), tag)
+            for c0 in range(0, TU, N):
+                nc.gpsimd.memset(window[:, c0 : c0 + N], 0.0)
+            windows.append(window)
 
-        scales = [item_scales(b) for b in range(B)]
-        h_mx = []
-        vt_mx = []
-        for b in range(B):
-            flat, v_mx = items(b)
-            u_mx = users(b)
-            vt_mx.append(items_turned(b, flat))
-            h_mx.append(gradient(b, u_mx, v_mx, *scales[b]))
-        for b in range(B):
-            scatter(b, vt_mx[b], h_mx[b])
+        for j in range(PACK):
+            nc.vector.tensor_copy(windows[j][:].indirect(entries(user_list, 0)), du0[j][:])
+        du1 = [product(1, j, vt_mx1, h_mx1, tag, 6 + j % 2) for j, tag in enumerate(("pair0", "pair1", "pair2", "h0"))]
+        for j in range(PACK):
+            nc.vector.tensor_copy(windows[j][:].indirect(entries(user_list, 1)), du1[j][:])
+            nc.sync.dma_start(out.rearrange("(m j) c -> m j c", j=PACK)[:, j, :], windows[j][:])

@@ -23,10 +23,10 @@ PACK = 4
 LIST_COLS = N // 16
 ALIGN = 256
 
-SMALL_SHARE, LARGE_SHARE = 384, 640
+SMALL_SHARE, HALF_SHARE, LARGE_SHARE = 384, 512, 640
 LOADS = (
-    ((0, 1024, 0), (1024, 2048, LARGE_SHARE)),
-    ((0, 1024, SMALL_SHARE), (1024, 2048, LARGE_SHARE)),
+    ((0, 1024, 0), (1024, 2048, HALF_SHARE)),
+    ((0, 1024, HALF_SHARE), (1024, 2048, LARGE_SHARE)),
     ((0, 1024, 0), (1024, 2048, SMALL_SHARE)),
     ((0, 1024, 0), (1024, 1536, SMALL_SHARE), (1536, 2048, SMALL_SHARE)),
 )
@@ -126,16 +126,8 @@ def tile_attend_gmf_sq_u_kernel(tc, uT, vT, y, us, ts, offs, uoffs, out):
                 nc.scalar.copy(turned[:, u], halves.rearrange("p (t m e) -> p e m t", t=PACK, e=2))
             return quantise("vt%d" % b, turned[:].rearrange("p u e m t -> p (u e m t)"), E4, 1)
 
-        def target_terms(b, tag):
-            target = shared([P, PACK, PACK, P], F32, "target%d" % b, tag)
-            for c in range(PACK):
-                nc.scalar.activation(
-                    target[:, c].rearrange("p t q -> p q t"),
-                    y_rows[b * PACK + c].rearrange("p (q t) -> p q t", t=PACK),
-                    COPY,
-                    scale=us_neg[:, b * PACK + c : b * PACK + c + 1],
-                )
-            return target
+        def dealt_targets(target, b, c):
+            return target[:, c].rearrange("p t q -> p q t"), y_rows[b * PACK + c].rearrange("p (q t) -> p q t", t=PACK)
 
         def score_term(b, c, u_mx, v_mx, ts_row, model, bank):
             rows = slice(c * P, (c + 1) * P)
@@ -180,10 +172,10 @@ def tile_attend_gmf_sq_u_kernel(tc, uT, vT, y, us, ts, offs, uoffs, out):
                 nc.vector.tensor_copy(pair_tables[n][:, c0 + cut : c1, :], side_by_side[:, cut:, :])
 
         ts_square0 = keep.tile([P, N], F32, name="ts_square0")
-        ts_row0 = keep.tile([P, N], F32, name="ts_row0")
+        ts_plain0 = keep.tile([P, P, PACK], F32, name="ts_plain0")
         ts_row1 = keep.tile([P, N], F32, name="ts_row1")
         nc.scalar.activation(ts_square0[:], ts_spread0, SQUARE)
-        nc.scalar.copy(ts_row0[:], ts_spread0)
+        nc.scalar.copy(ts_plain0[:], ts_spread0.rearrange("p (t q) -> p q t", t=PACK))
         nc.scalar.copy(ts_row1[:], ts_spread1)
 
         y_rows = []
@@ -203,26 +195,25 @@ def tile_attend_gmf_sq_u_kernel(tc, uT, vT, y, us, ts, offs, uoffs, out):
         for u in range(2):
             nc.vector.tensor_copy(u_woven0[:, :, u], user_words[u].indirect(entries(user_list, 0)))
         u_mx0 = quantise("u0", as_values(u_woven0), E4, 1)
+        u_picked1 = pick("u_picked1", user_words, user_list, 1)
 
         model0 = shared([P, PACK, N], F32, "model0", "raw1_0")
-        target0 = target_terms(0, "raw2_0")
+        target0 = shared([P, PACK, PACK, P], F32, "target0", "raw2_0")
         for c, bank in enumerate((0, 1, 6, 7)):
             score_term(0, c, u_mx0, v_mx0, ts_square0, model0, bank)
-            term = target0[:, c].rearrange("p t q -> p (t q)")
-            nc.vector.tensor_tensor(term, term, ts_row0[:], MULT)
+            nc.vector.scalar_tensor_tensor(*dealt_targets(target0, 0, c), us_neg[:, c : c + 1], ts_plain0[:], MULT, MULT)
         h0 = shared([P, R, PACK], BF16, "h0", "h0")
         for c, bank in enumerate((2, 3, 0, 1)):
             sums = bank_tile([P, PACK, P], "h_bank", bank)
             for t in range(PACK):
                 turn_and_add(sums[:, t, :], model0, target0, c, t)
             nc.scalar.copy(h0[:, c * P : (c + 1) * P, :], sums[:].rearrange("p t r -> p r t"))
-        vt_mx0 = items_along_slots(0, v_woven0, "raw2_1024", (4, 5))
+        vt_mx0 = items_along_slots(0, v_woven0, "raw3_0", (4, 5))
         h_mx0 = quantise("h0", h0[:].rearrange("p r t -> p (r t)"), E5, 2)
         du0 = [product(0, j, vt_mx0, h_mx0, "du0_%d" % j, 6 + j % 2) for j in range(PACK - 1)]
 
-        u_picked1 = pick("u_picked1", user_words, user_list, 1)
         v_picked1 = pick("v_picked1", item_words, item_list, 1)
-        v_woven1 = shared([P, N, 2], U32, "v_woven1", "raw3_1024")
+        v_woven1 = shared([P, N, 2], U32, "v_woven1", "raw3_1536")
         nc.scalar.copy(*dealing_views(v_woven1, v_picked1))
         v_mx1 = quantise("v1", as_values(v_woven1), E4, 1)
         u_woven1 = shared([P, R, 2], U32, "u_woven1", "u_woven1")
@@ -232,8 +223,10 @@ def tile_attend_gmf_sq_u_kernel(tc, uT, vT, y, us, ts, offs, uoffs, out):
         model1 = shared([P, PACK, N], F32, "model1", "raw1_1024")
         for c, bank in enumerate((4, 5, 2, 3)):
             score_term(1, c, u_mx1, v_mx1, ts_row1, model1, bank)
-        target1 = target_terms(1, "target1")
-        vt_mx1 = items_along_slots(1, v_woven1, "v_turned1", (2, 3))
+        target1 = shared([P, PACK, PACK, P], F32, "target1", "target1")
+        for c in range(PACK):
+            nc.scalar.activation(*dealt_targets(target1, 1, c), COPY, scale=us_neg[:, PACK + c : PACK + c + 1])
+        vt_mx1 = items_along_slots(1, v_woven1, "v_turned1", (6, 7))
         h1 = shared([P, R, PACK], BF16, "h1", "h1")
         places1 = shared([P, PACK, R], BF16, "places1", "places1")
         for t, bank in enumerate((2, 3, 0, 1)):
@@ -241,13 +234,11 @@ def tile_attend_gmf_sq_u_kernel(tc, uT, vT, y, us, ts, offs, uoffs, out):
             for c in range(PACK):
                 turn_and_add(sums[:, c, :], model1, target1, c, t)
             nc.scalar.activation(places1[:, t, :], sums[:].rearrange("p c r -> p (c r)"), COPY, scale=ts_cols1[:, t : t + 1])
-        nc.scalar.copy(
-            h1[:].rearrange("p (g i) t -> p g t i", i=PACK), places1[:].rearrange("p t (g i) -> p g t i", i=PACK)
-        )
+        nc.scalar.copy(h1[:], places1[:].rearrange("p t r -> p r t"))
         h_mx1 = quantise("h1", h1[:].rearrange("p r t -> p (r t)"), E5, 1)
         du0.append(product(0, PACK - 1, vt_mx0, h_mx0, "places1", 3))
 
-        for j, tag in enumerate(("u_woven0", "u_woven1", "raw1_1024")):
+        for j, tag in enumerate(("u_woven0", "h0", "raw1_1024")):
             window = shared([P, TU], F32, "window%d" % (j + 1), tag)
             for c0 in range(0, TU, N):
                 nc.gpsimd.memset(window[:, c0 : c0 + N], 0.0)
@@ -255,7 +246,7 @@ def tile_attend_gmf_sq_u_kernel(tc, uT, vT, y, us, ts, offs, uoffs, out):
 
         for j in range(PACK):
             nc.vector.tensor_copy(windows[j][:].indirect(entries(user_list, 0)), du0[j][:])
-        du1 = [product(1, j, vt_mx1, h_mx1, tag, 6 + j % 2) for j, tag in enumerate(("pair0", "pair1", "pair2", "h0"))]
+        du1 = [product(1, j, vt_mx1, h_mx1, tag, 6 + j % 2) for j, tag in enumerate(("pair0", "pair1", "pair2", "pair3"))]
         for j in range(PACK):
             nc.vector.tensor_copy(windows[j][:].indirect(entries(user_list, 1)), du1[j][:])
             nc.sync.dma_start(out.rearrange("(m j) c -> m j c", j=PACK)[:, j, :], windows[j][:])

@@ -23,12 +23,11 @@ PACK = 4
 LIST_COLS = N // 16
 ALIGN = 256
 
-SMALL_SHARE, HALF_SHARE, LARGE_SHARE = 384, 512, 640
 LOADS = (
-    ((0, 1024, 0), (1024, 2048, HALF_SHARE)),
-    ((0, 1024, HALF_SHARE), (1024, 2048, LARGE_SHARE)),
-    ((0, 1024, 0), (1024, 2048, SMALL_SHARE)),
-    ((0, 1024, 0), (1024, 1536, SMALL_SHARE), (1536, 2048, SMALL_SHARE)),
+    ((0, 1024, 0), (1024, 2048, 640)),
+    ((0, 1024, 512), (1024, 2048, 640)),
+    ((0, 1024, 0), (1024, 2048, 704)),
+    ((0, 1024, 256), (1024, 1664, 320), (1664, 2048, 384)),
 )
 
 
@@ -38,8 +37,8 @@ def tile_attend_gmf_sq_u_kernel(tc, uT, vT, y, us, ts, offs, uoffs, out):
         keep = ctx.enter_context(tc.tile_pool(name="keep", bufs=1))
         psum = ctx.enter_context(tc.psum_pool(name="psum", bufs=1))
 
-        def shared(shape, dtype, name, tag):
-            return keep.tile(shape, dtype, name=name, tag=tag, align_bytes=ALIGN)
+        def sb(shape, dtype, name, tag=None):
+            return keep.tile(shape, dtype, name=name, tag=tag or name, align_bytes=ALIGN)
 
         def bank_tile(shape, name, bank):
             return psum.tile(shape, F32, name=name, tag="bank%d" % bank)
@@ -52,201 +51,229 @@ def tile_attend_gmf_sq_u_kernel(tc, uT, vT, y, us, ts, offs, uoffs, out):
         nc.sync.dma_start(item_list[:], offs)
         nc.sync.dma_start(user_list[:], uoffs)
 
-        ts_table = keep.tile([P, T], F32, name="ts_table")
-        us_rows = keep.tile([P, P], F32, name="us_rows")
-        ts_first = shared([1, T], F32, "ts_first", "pair3")
+        us_rows = sb([P, P], F32, "us_rows")
+        ts_table = sb([P, T], F32, "ts_table")
+        ts_first = sb([1, T], F32, "ts_first")
         nc.sync.dma_start(ts_first[:], ts[0:1, :])
         nc.vector.memset(us_rows[:], 0.0)
         nc.vector.memset(ts_table[:].bitcast(I32), 0)
         nc.vector.tensor_copy(ts_table[0:1, :], ts_first[:])
         nc.sync.dma_start(us_rows[0 : B * PACK, :], us.rearrange("b (c p) o -> (b c) (p o)", p=P))
-        ident = keep.tile([P, P], F32, name="ident")
+        ts_picked = sb([P, B, N], F32, "ts_picked")
+        ts_dealt = ts_picked[:].bitcast(U32).rearrange("p b (t q) -> p b q t", t=PACK)
+        nc.vector.tensor_copy(ts_dealt, ts_table[:].bitcast(U32).indirect(item_list[:]))
+        ident = sb([P, P], F32, "ident")
         make_identity(nc, ident[:])
 
-        windows = [keep.tile([P, TU], F32, name="window0")]
-        nc.vector.memset(windows[0][:].bitcast(I32), 0)
+        windows = []
+
+        def clear_window(tag):
+            window = sb([P, TU], F32, "window%d" % len(windows), tag)
+            for c0 in range(0, TU, N):
+                nc.gpsimd.memset(window[:, c0 : c0 + N], 0.0)
+            windows.append(window)
+
+        clear_window("ts_first")
 
         pair_tables = []
         loaded = []
         for n, (table, u) in enumerate(((vT, 0), (vT, 1), (uT, 0), (uT, 1))):
             planes = table.rearrange("(p t) c -> p t c", t=PACK)[:, 2 * u : 2 * u + 2, :]
             for c0, c1, share in LOADS[n]:
-                raw = shared([P, 2, c1 - c0], F32, "raw%d_%d" % (n, c0), "raw%d_%d" % (n, c0))
+                raw = sb([P, 2, c1 - c0], F32, "raw%d_%d" % (n, c0))
                 nc.sync.dma_start(raw[:], planes[:, :, c0:c1])
                 loaded.append((n, c0, c1, share, raw))
-            pair_tables.append(shared([P, T, 2], BF16, "pair%d" % n, "pair%d" % n))
+            pair_tables.append(sb([P, T, 2], BF16, "pair%d" % n))
         pair_words = [pair[:].rearrange("p c e -> p (c e)").bitcast(U32) for pair in pair_tables]
         item_words, user_words = pair_words[0:2], pair_words[2:4]
+        y_rows = []
+        for b, c0, c1 in ((0, 0, 1), (0, 1, 2), (0, 2, 4), (1, 0, 4)):
+            rows_in = sb([P, c1 - c0, N], F32, "y%d_%d" % (b, c0))
+            nc.sync.dma_start(rows_in[:], y[b].rearrange("(c p) i -> p c i", p=P)[:, c0:c1, :])
+            y_rows.extend([rows_in[:, c, :] for c in range(c1 - c0)])
 
-        def quantise(name, src, fmt, parts):
-            codes = shared([P, N], U32, name + "_codes", name + "_codes")
-            plane = shared([P, N], U8, name + "_scales", name + "_scales")
-            step = N // parts
-            for c0 in range(0, N, step):
-                cols = slice(c0, c0 + step)
-                nc.vector.quantize_mx(codes[:, cols].bitcast(fmt), plane[:, cols], src[:, PACK * c0 : PACK * (c0 + step)])
-            return codes, plane
+        def round_table(n):
+            for m, c0, c1, share, raw in loaded:
+                if m == n:
+                    cut = c1 - c0 - share
+                    side_by_side = raw[:].rearrange("p e c -> p c e")
+                    if cut:
+                        nc.scalar.activation(pair_tables[n][:, c0 : c0 + cut, :], side_by_side[:, 0:cut, :], COPY)
+                    if share:
+                        nc.vector.tensor_copy(pair_tables[n][:, c0 + cut : c1, :], side_by_side[:, cut:, :])
 
-        def item_scales(b, turn_bank, spread_bank):
-            picked = keep.tile([P, N], F32, name="ts_picked%d" % b)
-            nc.vector.tensor_copy(picked[:], ts_table[:].indirect(entries(item_list, b)))
-            turned = bank_tile([P, PACK, P], "ts_turned", turn_bank)
-            for t in range(PACK):
-                nc.tensor.transpose(turned[:, t, :], picked[:, t:N:PACK], ident[:])
-            cols = keep.tile([P, PACK], F32, name="ts_cols%d" % b)
-            nc.scalar.activation(cols[:], turned[:, :, 0], COPY)
-            spread = bank_tile([P, PACK, P], "ts_spread", spread_bank)
-            for t in range(PACK):
-                nc.tensor.transpose(spread[:, t, :], cols[:, t : t + 1].to_broadcast([P, P]), ident[:])
-            return cols, spread[:].rearrange("p t q -> p (t q)")
+        def mx_tiles(name, tag=None):
+            return sb([P, N], U32, name + "_codes", tag), sb([P, N], U8, name + "_scales")
 
-        def pick(name, words, offsets, b):
-            picked = keep.tile([P, 2, N], U32, name=name)
-            for u in range(2):
-                nc.vector.tensor_copy(picked[:, u, :], words[u].indirect(entries(offsets, b)))
-            return picked
-
-        def dealing_views(woven, picked):
-            return (
-                woven[:].rearrange("p (t q) u -> p q t u", t=PACK),
-                picked[:].rearrange("p u (q t) -> p q t u", t=PACK),
-            )
+        def quantise(mx, src, fmt, c0, c1):
+            nc.vector.quantize_mx(mx[0][:, c0:c1].bitcast(fmt), mx[1][:, c0:c1], src)
 
         def as_values(woven):
             return woven[:].rearrange("p c u -> p (c u)").bitcast(BF16)
 
-        def items_along_slots(b, woven, tag, banks):
-            words = woven[:].rearrange("p c u -> p (c u)").bitcast(F32)
-            turned = shared([P, 2, 2, P, PACK], BF16, "v_turned%d" % b, tag)
-            for u in range(2):
-                bank = bank_tile([P, PACK, P], "v_bank", banks[u])
-                for t in range(PACK):
-                    nc.tensor.transpose(bank[:, t, :], words[:, 2 * P * t + u : 2 * P * (t + 1) : 2], ident[:])
-                halves = bank[:].rearrange("p t m -> p (t m)").bitcast(BF16)
-                nc.scalar.copy(turned[:, u], halves.rearrange("p (t m e) -> p e m t", t=PACK, e=2))
-            return quantise("vt%d" % b, turned[:].rearrange("p u e m t -> p (u e m t)"), E4, 1)
+        v_picked = sb([P, 2, B, N], U32, "v_picked")
+
+        def pick_items(u):
+            dealt = v_picked[:, u].rearrange("p b (t q) -> p b q t", t=PACK)
+            nc.vector.tensor_copy(dealt, item_words[u].indirect(item_list[:]))
+
+        def turn_items(b, u, bank, laid):
+            words = v_picked[:, u, b, :].bitcast(F32)
+            turned = bank_tile([P, PACK, P], "v_bank", bank)
+            for t in range(PACK):
+                nc.tensor.transpose(turned[:, t, :], words[:, t * P : (t + 1) * P], ident[:])
+            halves = turned[:].rearrange("p t m -> p (t m)").bitcast(BF16)
+            nc.scalar.copy(laid.rearrange("p (e m t) -> p e m t", t=PACK, e=2), halves.rearrange("p (t m e) -> p e m t", t=PACK, e=2))
+
+        def items_mx(b, values):
+            woven = values.bitcast(I32).rearrange("p (c u) -> p c u", u=2)
+            nc.vector.tensor_copy(woven, v_picked[:, :, b, :].rearrange("p u c -> p c u").bitcast(I32))
+            mx = mx_tiles("v%d" % b)
+            quantise(mx, values, E4, 0, N)
+            return mx
+
+        def users_mx(b, picked):
+            woven = sb([P, R, 2], U32, "u_woven%d" % b)
+            nc.scalar.copy(woven[:], picked[:].rearrange("p u c -> p c u"))
+            mx = mx_tiles("u%d" % b)
+            quantise(mx, as_values(woven), E4, 0, R)
+            return mx
 
         def dealt_targets(target, b, c):
             return target[:, c].rearrange("p t q -> p q t"), y_rows[b * PACK + c].rearrange("p (q t) -> p q t", t=PACK)
 
-        def score_term(b, c, u_mx, v_mx, ts_row, model, bank):
+        def score_term(b, c, u_mx, ts_row, model, bank):
             rows = slice(c * P, (c + 1) * P)
             scores = bank_tile([P, N], "scores", bank)
             nc.tensor.matmul_mx(
                 scores[:], lhsT=u_mx[0][:, rows].bitcast(E4), lhsT_scale=u_mx[1][:, rows],
-                rhs=v_mx[0][:].bitcast(E4), rhs_scale=v_mx[1][:], start=True, stop=True,
+                rhs=v_mx[b][0][:].bitcast(E4), rhs_scale=v_mx[b][1][:], start=True, stop=True,
             )
             nc.vector.scalar_tensor_tensor(
-                model[:, c, :], scores[:], us_sq[:, b * PACK + c : b * PACK + c + 1], ts_row[:], MULT, MULT
+                model[:, c].rearrange("p t q -> p (t q)"), scores[:], us_sq[:, b * PACK + c : b * PACK + c + 1], ts_row[:], MULT, MULT
             )
 
-        def turn_and_add(dst, model, target, c, t):
-            nc.tensor.matmul(dst, target[:, c, t, :], ident[:], start=True, stop=False, is_transpose=True)
-            nc.tensor.matmul(dst, model[:, c, t * P : (t + 1) * P], ident[:], start=False, stop=True, is_transpose=True)
+        def turn_onto(dst, src, start, stop):
+            nc.tensor.matmul(dst, src, ident[:], start=start, stop=stop, is_transpose=True)
 
-        def product(b, j, vt_mx, h_mx, tag, bank):
+        def product(b, j, vt_mx, h_mx, bank, tag=None):
             cols = slice(j * P, (j + 1) * P)
             sums = bank_tile([P, R], "du_bank", bank)
             nc.tensor.matmul_mx(
                 sums[:], lhsT=vt_mx[0][:, cols].bitcast(E4), lhsT_scale=vt_mx[1][:, cols],
                 rhs=h_mx[0][:].bitcast(E5), rhs_scale=h_mx[1][:], start=True, stop=True,
             )
-            du = shared([P, R], F32, "du%d_%d" % (b, j), tag)
+            du = sb([P, R], F32, "du%d_%d" % (b, j), tag)
             nc.scalar.copy(du[:], sums[:])
             return du
 
-        us_bank = bank_tile([P, PACK, P], "us_bank", 6)
+        round_table(0)
+        pick_items(0)
+        clear_window("raw0_0")
+
+        us_bank = bank_tile([P, PACK, P], "us_bank", 3)
         nc.tensor.transpose(us_bank[:, 0, :], us_rows[:], ident[:])
-        us_neg = keep.tile([P, B * PACK], F32, name="us_neg")
-        us_sq = keep.tile([P, B * PACK], F32, name="us_sq")
+        us_neg = sb([P, B * PACK], F32, "us_neg")
+        us_sq = sb([P, B * PACK], F32, "us_sq")
         nc.scalar.activation(us_neg[:], us_bank[:, 0, 0 : B * PACK], COPY, scale=-1.0)
-        nc.gpsimd.tensor_tensor(us_sq[:], us_neg[:], us_neg[:], MULT)
-        ts_spread0 = item_scales(0, 4, 2)[1]
-        ts_cols1, ts_spread1 = item_scales(1, 5, 3)
-
-        for n, c0, c1, share, raw in loaded:
-            cut = c1 - c0 - share
-            side_by_side = raw[:].rearrange("p e c -> p c e")
-            nc.scalar.activation(pair_tables[n][:, c0 : c0 + cut, :], side_by_side[:, 0:cut, :], COPY)
-            if share:
-                nc.vector.tensor_copy(pair_tables[n][:, c0 + cut : c1, :], side_by_side[:, cut:, :])
-
-        ts_square0 = keep.tile([P, N], F32, name="ts_square0")
-        ts_plain0 = keep.tile([P, P, PACK], F32, name="ts_plain0")
-        ts_row1 = keep.tile([P, N], F32, name="ts_row1")
-        nc.scalar.activation(ts_square0[:], ts_spread0, SQUARE)
-        nc.scalar.copy(ts_plain0[:], ts_spread0.rearrange("p (t q) -> p q t", t=PACK))
-        nc.scalar.copy(ts_row1[:], ts_spread1)
-
-        y_rows = []
-        for b, c0, c1, tag in ((0, 0, 2, "y0_first"), (0, 2, 4, "y0_second"), (1, 0, 4, "raw0_1024")):
-            rows_in = shared([P, c1 - c0, N], F32, "y%d_%d" % (b, c0), tag)
-            nc.sync.dma_start(rows_in[:], y[b].rearrange("(c p) i -> p c i", p=P)[:, c0:c1, :])
-            y_rows.extend([rows_in[:, c, :] for c in range(c1 - c0)])
-
-        v_picked0 = pick("v_picked0", item_words, item_list, 0)
-        v_woven0 = shared([P, N, 2], U32, "v_woven0", "v_woven0")
-        dst, src = dealing_views(v_woven0, v_picked0)
-        for t0 in (0, 2):
-            nc.vector.tensor_copy(dst[:, :, t0 : t0 + 2, :].bitcast(I32), src[:, :, t0 : t0 + 2, :].bitcast(I32))
-        v_mx0 = quantise("v0", as_values(v_woven0), E4, 1)
-
-        u_woven0 = shared([P, R, 2], U32, "u_woven0", "u_woven0")
-        for u in range(2):
-            nc.vector.tensor_copy(u_woven0[:, :, u], user_words[u].indirect(entries(user_list, 0)))
-        u_mx0 = quantise("u0", as_values(u_woven0), E4, 1)
-        u_picked1 = pick("u_picked1", user_words, user_list, 1)
-
-        model0 = shared([P, PACK, N], F32, "model0", "raw1_0")
-        target0 = shared([P, PACK, PACK, P], F32, "target0", "raw2_0")
-        for c, bank in enumerate((0, 1, 6, 7)):
-            score_term(0, c, u_mx0, v_mx0, ts_square0, model0, bank)
-            nc.vector.scalar_tensor_tensor(*dealt_targets(target0, 0, c), us_neg[:, c : c + 1], ts_plain0[:], MULT, MULT)
-        h0 = shared([P, R, PACK], BF16, "h0", "h0")
-        for c, bank in enumerate((2, 3, 0, 1)):
-            sums = bank_tile([P, PACK, P], "h_bank", bank)
+        nc.scalar.activation(us_sq[:], us_bank[:, 0, 0 : B * PACK], SQUARE)
+        ts_cols, ts_spread = [], []
+        ts_cols_all = sb([P, B, PACK], F32, "ts_cols", "raw0_1024")
+        for b in range(B):
+            turned = bank_tile([P, PACK, P], "ts_turned", 1 + b)
             for t in range(PACK):
-                turn_and_add(sums[:, t, :], model0, target0, c, t)
-            nc.scalar.copy(h0[:, c * P : (c + 1) * P, :], sums[:].rearrange("p t r -> p r t"))
-        vt_mx0 = items_along_slots(0, v_woven0, "raw3_0", (4, 5))
-        h_mx0 = quantise("h0", h0[:].rearrange("p r t -> p (r t)"), E5, 2)
-        du0 = [product(0, j, vt_mx0, h_mx0, "du0_%d" % j, 6 + j % 2) for j in range(PACK - 1)]
+                nc.tensor.transpose(turned[:, t, :], ts_picked[:, b, t * P : (t + 1) * P], ident[:])
+            cols = ts_cols_all[:, b, :]
+            nc.scalar.activation(cols, turned[:, :, 0], COPY)
+            spread = bank_tile([P, PACK, P], "ts_spread", (0, 3)[b])
+            for t in range(PACK):
+                nc.tensor.transpose(spread[:, t, :], cols[:, t : t + 1].to_broadcast([P, P]), ident[:])
+            ts_cols.append(cols)
+            ts_spread.append(spread)
 
-        v_picked1 = pick("v_picked1", item_words, item_list, 1)
-        v_woven1 = shared([P, N, 2], U32, "v_woven1", "raw3_1536")
-        nc.scalar.copy(*dealing_views(v_woven1, v_picked1))
-        v_mx1 = quantise("v1", as_values(v_woven1), E4, 1)
-        u_woven1 = shared([P, R, 2], U32, "u_woven1", "u_woven1")
-        nc.scalar.copy(u_woven1[:], u_picked1[:].rearrange("p u c -> p c u"))
-        u_mx1 = quantise("u1", as_values(u_woven1), E4, 1)
+        round_table(1)
+        pick_items(1)
+        round_table(2)
+        v_woven0 = sb([P, PACK * N], BF16, "v_woven0")
+        v_mx = [items_mx(0, v_woven0[:])]
+        u_picked0 = sb([P, 2, R], U32, "u_picked0")
+        nc.vector.tensor_copy(u_picked0[:, 0, :], user_words[0].indirect(entries(user_list, 0)))
+        round_table(3)
+        nc.vector.tensor_copy(u_picked0[:, 1, :], user_words[1].indirect(entries(user_list, 0)))
+        u_mx0 = users_mx(0, u_picked0)
+        behind_users = sb([P, 6 * N], BF16, "behind_users", "raw2_1024")
+        v_mx.append(items_mx(1, behind_users[:, 0 : PACK * N]))
 
-        model1 = shared([P, PACK, N], F32, "model1", "raw1_1024")
-        for c, bank in enumerate((4, 5, 2, 3)):
-            score_term(1, c, u_mx1, v_mx1, ts_row1, model1, bank)
-        target1 = shared([P, PACK, PACK, P], F32, "target1", "target1")
+        ts_square0 = sb([P, N], F32, "ts_square0")
+        ts_row1 = sb([P, N], F32, "ts_row1")
+        nc.scalar.activation(ts_square0[:], ts_spread[0][:].rearrange("p t q -> p (t q)"), SQUARE)
+        nc.scalar.copy(ts_row1[:], ts_spread[1][:].rearrange("p t q -> p (t q)"))
+
+        vt_mx0 = mx_tiles("vt0")
+        v_turned0 = sb([P, 2 * N], BF16, "v_turned0", "raw1_1024")
+        for u, laid in enumerate((v_turned0[:], behind_users[:, PACK * N :])):
+            turn_items(0, u, 4 + u, laid)
+            quantise(vt_mx0, laid, E4, 2 * P * u, 2 * P * (u + 1))
+        v_turned1 = sb([P, PACK * N], BF16, "v_turned1", "raw3_1024")
+        for u in range(2):
+            turn_items(1, u, 6 + u, v_turned1[:, 2 * N * u : 2 * N * (u + 1)])
+
+        model0 = sb([P, PACK, PACK, P], F32, "model0", "pair0")
+        target0 = sb([P, PACK, PACK, P], F32, "target0", "raw3_1664")
+        ts_listed0 = ts_spread[0][:].rearrange("p t q -> p q t")
+        h_banks = []
+        for c in range(PACK):
+            nc.vector.scalar_tensor_tensor(*dealt_targets(target0, 0, c), us_neg[:, c : c + 1], ts_listed0, MULT, MULT)
+        for c, bank in enumerate((1, 2, 3, 0)):
+            score_term(0, c, u_mx0, ts_square0, model0, bank)
+        for c in range(PACK):
+            sums = bank_tile([P, PACK, P], "h_bank", 4 + c)
+            for t in range(PACK):
+                turn_onto(sums[:, t, :], target0[:, c, t, :], t == 0, False)
+            h_banks.append(sums)
+        clear_window("raw3_1664")
+        target1 = sb([P, PACK, PACK, P], F32, "target1", "pair1")
         for c in range(PACK):
             nc.scalar.activation(*dealt_targets(target1, 1, c), COPY, scale=us_neg[:, PACK + c : PACK + c + 1])
-        vt_mx1 = items_along_slots(1, v_woven1, "v_turned1", (6, 7))
-        h1 = shared([P, R, PACK], BF16, "h1", "h1")
-        places1 = shared([P, PACK, R], BF16, "places1", "places1")
-        for t, bank in enumerate((2, 3, 0, 1)):
-            sums = bank_tile([P, PACK, P], "h_bank", bank)
-            for c in range(PACK):
-                turn_and_add(sums[:, c, :], model1, target1, c, t)
-            nc.scalar.activation(places1[:, t, :], sums[:].rearrange("p c r -> p (c r)"), COPY, scale=ts_cols1[:, t : t + 1])
-        nc.scalar.copy(h1[:], places1[:].rearrange("p t r -> p r t"))
-        h_mx1 = quantise("h1", h1[:].rearrange("p r t -> p (r t)"), E5, 1)
-        du0.append(product(0, PACK - 1, vt_mx0, h_mx0, "places1", 3))
+        u_picked1 = sb([P, 2, R], U32, "u_picked1", "u_woven0")
+        for u in range(2):
+            nc.vector.tensor_copy(u_picked1[:, u, :], user_words[u].indirect(entries(user_list, 1)))
+        u_mx1 = users_mx(1, u_picked1)
+        h0 = sb([P, R, PACK], BF16, "h0", "y1_0")
+        h_mx0 = mx_tiles("h0")
+        for c in range(PACK):
+            for t in range(PACK):
+                turn_onto(h_banks[c][:, t, :], model0[:, c, t, :], False, t == PACK - 1)
+            nc.scalar.copy(h0[:, c * P : (c + 1) * P, :], h_banks[c][:].rearrange("p t r -> p r t"))
+        for c0, c1 in ((0, 256), (256, 384), (384, 512)):
+            quantise(h_mx0, h0[:, c0:c1, :].rearrange("p r t -> p (r t)"), E5, c0, c1)
+        du0 = [product(0, j, vt_mx0, h_mx0, 4 + j) for j in range(PACK - 1)]
 
-        for j, tag in enumerate(("u_woven0", "h0", "raw1_1024")):
-            window = shared([P, TU], F32, "window%d" % (j + 1), tag)
-            for c0 in range(0, TU, N):
-                nc.gpsimd.memset(window[:, c0 : c0 + N], 0.0)
-            windows.append(window)
+        vt_mx1 = mx_tiles("vt1", "u_woven1")
+        quantise(vt_mx1, v_turned1[:], E4, 0, D)
+        model1 = sb([P, PACK, PACK, P], F32, "model1", "y1_0")
+        for c in range(PACK):
+            score_term(1, c, u_mx1, ts_row1, model1, c)
+        place_banks = [bank_tile([P, PACK, P], "place_bank", bank) for bank in (4, 5, 6, 3)]
+        for t in range(PACK):
+            for c in range(PACK):
+                turn_onto(place_banks[t][:, c, :], target1[:, c, t, :], c == 0, False)
+        for c in range(PACK):
+            for t in range(PACK):
+                turn_onto(place_banks[t][:, c, :], model1[:, c, t, :], False, c == PACK - 1)
+        clear_window("y1_0")
+        h1 = sb([P, R, PACK], BF16, "h1")
+        places1 = sb([P, PACK, R], BF16, "places1")
+        for t in range(PACK):
+            nc.scalar.activation(places1[:, t, :], place_banks[t][:].rearrange("p c r -> p (c r)"), COPY, scale=ts_cols[1][:, t : t + 1])
+        nc.scalar.copy(h1[:], places1[:].rearrange("p t r -> p r t"))
+        h_mx1 = mx_tiles("h1")
+        quantise(h_mx1, h1[:].rearrange("p r t -> p (r t)"), E5, 0, R)
+        du0.append(product(0, PACK - 1, vt_mx0, h_mx0, 7, "places1"))
 
         for j in range(PACK):
             nc.vector.tensor_copy(windows[j][:].indirect(entries(user_list, 0)), du0[j][:])
-        du1 = [product(1, j, vt_mx1, h_mx1, tag, 6 + j % 2) for j, tag in enumerate(("pair0", "pair1", "pair2", "pair3"))]
+        du1 = [product(1, j, vt_mx1, h_mx1, 1 + j % 2) for j in range(PACK)]
         for j in range(PACK):
             nc.vector.tensor_copy(windows[j][:].indirect(entries(user_list, 1)), du1[j][:])
             nc.sync.dma_start(out.rearrange("(m j) c -> m j c", j=PACK)[:, j, :], windows[j][:])

@@ -139,8 +139,8 @@ def tile_attend_gmf_sq_u_kernel(tc, uT, vT, y, us, ts, offs, uoffs, out):
             quantise(mx, as_values(woven), E4, 0, R)
             return mx
 
-        def dealt_targets(target, b, c):
-            return target[:, c].rearrange("p t q -> p q t"), y_rows[b * PACK + c].rearrange("p (q t) -> p q t", t=PACK)
+        def paired(b, c):
+            return y_rows[b * PACK + c].rearrange("p (q v e) -> p v q e", v=2, e=2)
 
         def score_term(b, c, u_mx, ts_row, model, bank):
             rows = slice(c * P, (c + 1) * P)
@@ -219,27 +219,26 @@ def tile_attend_gmf_sq_u_kernel(tc, uT, vT, y, us, ts, offs, uoffs, out):
             turn_items(1, u, 6 + u, v_turned1[:, 2 * N * u : 2 * N * (u + 1)])
 
         model0 = sb([P, PACK, PACK, P], F32, "model0", "pair0")
-        target0 = sb([P, PACK, PACK, P], F32, "target0", "raw3_1664")
-        ts_listed0 = ts_spread[0][:].rearrange("p t q -> p q t")
+        target0 = sb([P, PACK, 2, P, 2], F32, "target0", "raw3_1664")
+        ts_paired0 = ts_spread[0][:].rearrange("p (v e) q -> p v q e", e=2)
         h_banks = []
         for c in range(PACK):
-            nc.vector.scalar_tensor_tensor(*dealt_targets(target0, 0, c), us_neg[:, c : c + 1], ts_listed0, MULT, MULT)
+            for v in range(2):
+                nc.vector.scalar_tensor_tensor(
+                    target0[:, c, v], paired(0, c)[:, v], us_neg[:, c : c + 1], ts_paired0[:, v], MULT, MULT
+                )
         for c, bank in enumerate((1, 2, 3, 0)):
             score_term(0, c, u_mx0, ts_square0, model0, bank)
         for c in range(PACK):
             sums = bank_tile([P, PACK, P], "h_bank", 4 + c)
             for t in range(PACK):
-                turn_onto(sums[:, t, :], target0[:, c, t, :], t == 0, False)
+                turn_onto(sums[:, t, :], target0[:, c, t // 2, :, t % 2], t == 0, False)
             h_banks.append(sums)
-        clear_window("raw3_1664")
-        target1 = sb([P, PACK, PACK, P], F32, "target1", "pair1")
-        for c in range(PACK):
-            nc.scalar.activation(*dealt_targets(target1, 1, c), COPY, scale=us_neg[:, PACK + c : PACK + c + 1])
         u_picked1 = sb([P, 2, R], U32, "u_picked1", "u_woven0")
         for u in range(2):
             nc.vector.tensor_copy(u_picked1[:, u, :], user_words[u].indirect(entries(user_list, 1)))
         u_mx1 = users_mx(1, u_picked1)
-        h0 = sb([P, R, PACK], BF16, "h0", "y1_0")
+        h0 = sb([P, R, PACK], BF16, "h0")
         h_mx0 = mx_tiles("h0")
         for c in range(PACK):
             for t in range(PACK):
@@ -247,21 +246,23 @@ def tile_attend_gmf_sq_u_kernel(tc, uT, vT, y, us, ts, offs, uoffs, out):
             nc.scalar.copy(h0[:, c * P : (c + 1) * P, :], h_banks[c][:].rearrange("p t r -> p r t"))
         for c0, c1 in ((0, 256), (256, 384), (384, 512)):
             quantise(h_mx0, h0[:, c0:c1, :].rearrange("p r t -> p (r t)"), E5, c0, c1)
-        du0 = [product(0, j, vt_mx0, h_mx0, 4 + j) for j in range(PACK - 1)]
+        du0 = [product(0, j, vt_mx0, h_mx0, 4 + j, ("raw2_0", None, None)[j]) for j in range(PACK - 1)]
 
         vt_mx1 = mx_tiles("vt1", "u_woven1")
         quantise(vt_mx1, v_turned1[:], E4, 0, D)
-        model1 = sb([P, PACK, PACK, P], F32, "model1", "y1_0")
+        model1 = sb([P, PACK, PACK, P], F32, "model1", "h0")
         for c in range(PACK):
             score_term(1, c, u_mx1, ts_row1, model1, c)
+        target1 = sb([P, PACK, 2, P, 2], F32, "target1", "pair1")
+        for c in range(PACK):
+            nc.scalar.activation(target1[:, c], paired(1, c), COPY, scale=us_neg[:, PACK + c : PACK + c + 1])
         place_banks = [bank_tile([P, PACK, P], "place_bank", bank) for bank in (4, 5, 6, 3)]
         for t in range(PACK):
             for c in range(PACK):
-                turn_onto(place_banks[t][:, c, :], target1[:, c, t, :], c == 0, False)
+                turn_onto(place_banks[t][:, c, :], target1[:, c, t // 2, :, t % 2], c == 0, False)
         for c in range(PACK):
             for t in range(PACK):
                 turn_onto(place_banks[t][:, c, :], model1[:, c, t, :], False, c == PACK - 1)
-        clear_window("y1_0")
         h1 = sb([P, R, PACK], BF16, "h1")
         places1 = sb([P, PACK, R], BF16, "places1")
         for t in range(PACK):
@@ -271,7 +272,10 @@ def tile_attend_gmf_sq_u_kernel(tc, uT, vT, y, us, ts, offs, uoffs, out):
         quantise(h_mx1, h1[:].rearrange("p r t -> p (r t)"), E5, 0, R)
         du0.append(product(0, PACK - 1, vt_mx0, h_mx0, 7, "places1"))
 
-        for j in range(PACK):
+        nc.vector.tensor_copy(windows[0][:].indirect(entries(user_list, 0)), du0[0][:])
+        clear_window("raw2_0")
+        clear_window("h0")
+        for j in range(1, PACK):
             nc.vector.tensor_copy(windows[j][:].indirect(entries(user_list, 0)), du0[j][:])
         du1 = [product(1, j, vt_mx1, h_mx1, 1 + j % 2) for j in range(PACK)]
         for j in range(PACK):

@@ -26,8 +26,8 @@ ALIGN = 256
 LOADS = (
     ((0, 1024, 0), (1024, 2048, 640)),
     ((0, 1024, 512), (1024, 2048, 640)),
-    ((0, 1024, 0), (1024, 2048, 704)),
-    ((0, 1024, 256), (1024, 1664, 320), (1664, 2048, 384)),
+    ((0, 1024, 0), (1024, 2048, 640)),
+    ((0, 1024, 0), (1024, 1664, 384), (1664, 2048, 384)),
 )
 
 
@@ -132,26 +132,27 @@ def tile_attend_gmf_sq_u_kernel(tc, uT, vT, y, us, ts, offs, uoffs, out):
             quantise(mx, values, E4, 0, N)
             return mx
 
-        def users_mx(b, picked):
+        def weave_users(b):
             woven = sb([P, R, 2], U32, "u_woven%d" % b)
-            nc.scalar.copy(woven[:], picked[:].rearrange("p u c -> p c u"))
-            mx = mx_tiles("u%d" % b)
+            nc.scalar.copy(woven[:], u_picked[:, :, b, :].rearrange("p u c -> p c u"))
+            return woven
+
+        def quantise_users(b, woven, tag=None):
+            mx = mx_tiles("u%d" % b, tag)
             quantise(mx, as_values(woven), E4, 0, R)
             return mx
 
-        def paired(b, c):
-            return y_rows[b * PACK + c].rearrange("p (q v e) -> p v q e", v=2, e=2)
+        def dealt_targets(target, b, c):
+            return target[:, c].rearrange("p t q -> p q t"), y_rows[b * PACK + c].rearrange("p (q t) -> p q t", t=PACK)
 
-        def score_term(b, c, u_mx, ts_row, model, bank):
+        def score(b, c, u_mx, bank):
             rows = slice(c * P, (c + 1) * P)
             scores = bank_tile([P, N], "scores", bank)
             nc.tensor.matmul_mx(
                 scores[:], lhsT=u_mx[0][:, rows].bitcast(E4), lhsT_scale=u_mx[1][:, rows],
                 rhs=v_mx[b][0][:].bitcast(E4), rhs_scale=v_mx[b][1][:], start=True, stop=True,
             )
-            nc.vector.scalar_tensor_tensor(
-                model[:, c].rearrange("p t q -> p (t q)"), scores[:], us_sq[:, b * PACK + c : b * PACK + c + 1], ts_row[:], MULT, MULT
-            )
+            return scores
 
         def turn_onto(dst, src, start, stop):
             nc.tensor.matmul(dst, src, ident[:], start=start, stop=stop, is_transpose=True)
@@ -191,93 +192,103 @@ def tile_attend_gmf_sq_u_kernel(tc, uT, vT, y, us, ts, offs, uoffs, out):
             ts_cols.append(cols)
             ts_spread.append(spread)
 
+        ts_square0 = sb([P, N], F32, "ts_square0")
+        ts_row1 = sb([P, N], F32, "ts_row1")
         round_table(1)
+        nc.scalar.activation(ts_square0[:], ts_spread[0][:].rearrange("p t q -> p (t q)"), SQUARE)
+        nc.scalar.copy(ts_row1[:], ts_spread[1][:].rearrange("p t q -> p (t q)"))
         pick_items(1)
         round_table(2)
         v_woven0 = sb([P, PACK * N], BF16, "v_woven0")
         v_mx = [items_mx(0, v_woven0[:])]
-        u_picked0 = sb([P, 2, R], U32, "u_picked0")
-        nc.vector.tensor_copy(u_picked0[:, 0, :], user_words[0].indirect(entries(user_list, 0)))
+        u_picked = sb([P, 2, B, R], U32, "u_picked")
+        nc.vector.tensor_copy(u_picked[:, 0].rearrange("p b c -> p (b c)"), user_words[0].indirect(user_list[:]))
         round_table(3)
-        nc.vector.tensor_copy(u_picked0[:, 1, :], user_words[1].indirect(entries(user_list, 0)))
-        u_mx0 = users_mx(0, u_picked0)
-        behind_users = sb([P, 6 * N], BF16, "behind_users", "raw2_1024")
-        v_mx.append(items_mx(1, behind_users[:, 0 : PACK * N]))
+        for b in range(B):
+            nc.vector.tensor_copy(u_picked[:, 1, b, :], user_words[1].indirect(entries(user_list, b)))
+        u_mx0 = quantise_users(0, weave_users(0))
+        u_woven1 = weave_users(1)
 
-        ts_square0 = sb([P, N], F32, "ts_square0")
-        ts_row1 = sb([P, N], F32, "ts_row1")
-        nc.scalar.activation(ts_square0[:], ts_spread[0][:].rearrange("p t q -> p (t q)"), SQUARE)
-        nc.scalar.copy(ts_row1[:], ts_spread[1][:].rearrange("p t q -> p (t q)"))
 
         vt_mx0 = mx_tiles("vt0")
-        v_turned0 = sb([P, 2 * N], BF16, "v_turned0", "raw1_1024")
-        for u, laid in enumerate((v_turned0[:], behind_users[:, PACK * N :])):
-            turn_items(0, u, 4 + u, laid)
-            quantise(vt_mx0, laid, E4, 2 * P * u, 2 * P * (u + 1))
-        v_turned1 = sb([P, PACK * N], BF16, "v_turned1", "raw3_1024")
+        for u, tag in enumerate(("raw1_1024", "raw2_1024")):
+            laid = sb([P, 2 * N], BF16, "v_turned0_%d" % u, tag)
+            turn_items(0, u, 4 + u, laid[:])
+            quantise(vt_mx0, laid[:], E4, 2 * P * u, 2 * P * (u + 1))
+        behind_tables = sb([P, PACK, N], F32, "behind_tables", "raw3_1024")
+        v_turned1 = behind_tables[:, 0:2, :].rearrange("p u c -> p (u c)").bitcast(BF16)
+        v_woven1 = behind_tables[:, 2:PACK, :].rearrange("p u c -> p (u c)")
         for u in range(2):
             turn_items(1, u, 6 + u, v_turned1[:, 2 * N * u : 2 * N * (u + 1)])
+        nc.scalar.copy(v_woven1.bitcast(U32).rearrange("p (c u) -> p c u", u=2), v_picked[:, :, 1, :].rearrange("p u c -> p c u"))
 
-        model0 = sb([P, PACK, PACK, P], F32, "model0", "pair0")
-        target0 = sb([P, PACK, 2, P, 2], F32, "target0", "raw3_1664")
-        ts_paired0 = ts_spread[0][:].rearrange("p (v e) q -> p v q e", e=2)
+        clear_window("raw3_1664")
+        model0 = sb([P, PACK, PACK, P], F32, "model0", "raw2_0")
+        target0 = sb([P, PACK, PACK, P], F32, "target0", "u_woven0")
+        ts_listed0 = ts_spread[0][:].rearrange("p t q -> p q t")
         h_banks = []
         for c in range(PACK):
-            for v in range(2):
-                nc.vector.scalar_tensor_tensor(
-                    target0[:, c, v], paired(0, c)[:, v], us_neg[:, c : c + 1], ts_paired0[:, v], MULT, MULT
-                )
+            nc.vector.scalar_tensor_tensor(*dealt_targets(target0, 0, c), us_neg[:, c : c + 1], ts_listed0, MULT, MULT)
         for c, bank in enumerate((1, 2, 3, 0)):
-            score_term(0, c, u_mx0, ts_square0, model0, bank)
+            scores = score(0, c, u_mx0, bank)
+            nc.vector.scalar_tensor_tensor(
+                model0[:, c].rearrange("p t q -> p (t q)"), scores[:], us_sq[:, c : c + 1], ts_square0[:], MULT, MULT
+            )
         for c in range(PACK):
             sums = bank_tile([P, PACK, P], "h_bank", 4 + c)
             for t in range(PACK):
-                turn_onto(sums[:, t, :], target0[:, c, t // 2, :, t % 2], t == 0, False)
+                turn_onto(sums[:, t, :], target0[:, c, t, :], t == 0, False)
             h_banks.append(sums)
-        u_picked1 = sb([P, 2, R], U32, "u_picked1", "u_woven0")
-        for u in range(2):
-            nc.vector.tensor_copy(u_picked1[:, u, :], user_words[u].indirect(entries(user_list, 1)))
-        u_mx1 = users_mx(1, u_picked1)
-        h0 = sb([P, R, PACK], BF16, "h0")
+        v_mx.append(mx_tiles("v1"))
+        quantise(v_mx[1], v_woven1.bitcast(BF16), E4, 0, N)
+        u_mx1 = quantise_users(1, u_woven1, "y0_2")
         h_mx0 = mx_tiles("h0")
-        for c in range(PACK):
-            for t in range(PACK):
-                turn_onto(h_banks[c][:, t, :], model0[:, c, t, :], False, t == PACK - 1)
-            nc.scalar.copy(h0[:, c * P : (c + 1) * P, :], h_banks[c][:].rearrange("p t r -> p r t"))
-        for c0, c1 in ((0, 256), (256, 384), (384, 512)):
-            quantise(h_mx0, h0[:, c0:c1, :].rearrange("p r t -> p (r t)"), E5, c0, c1)
-        du0 = [product(0, j, vt_mx0, h_mx0, 4 + j, ("raw2_0", None, None)[j]) for j in range(PACK - 1)]
+        for c0, c1 in ((0, 2), (2, 3), (3, 4)):
+            h0 = sb([P, (c1 - c0) * P, PACK], BF16, "h0_%d" % c0)
+            for c in range(c0, c1):
+                for t in range(PACK):
+                    turn_onto(h_banks[c][:, t, :], model0[:, c, t, :], False, t == PACK - 1)
+                nc.scalar.copy(h0[:, (c - c0) * P : (c - c0 + 1) * P, :], h_banks[c][:].rearrange("p t r -> p r t"))
+            quantise(h_mx0, h0[:].rearrange("p r t -> p (r t)"), E5, c0 * P, c1 * P)
+        du0 = [product(0, 0, vt_mx0, h_mx0, 4)]
 
-        vt_mx1 = mx_tiles("vt1", "u_woven1")
-        quantise(vt_mx1, v_turned1[:], E4, 0, D)
-        model1 = sb([P, PACK, PACK, P], F32, "model1", "h0")
+        vt_mx1 = mx_tiles("vt1", "h0_2")
+        quantise(vt_mx1, v_turned1, E4, 0, D)
+        model1 = [sb([P, 2, PACK, P], F32, "model1_%d" % half, ("h0_3", "raw1_0")[half]) for half in range(2)]
+        scaled1 = sb([P, 2, N], F32, "scaled1", "h0_0")
         for c in range(PACK):
-            score_term(1, c, u_mx1, ts_row1, model1, c)
-        target1 = sb([P, PACK, 2, P, 2], F32, "target1", "pair1")
+            scores = score(1, c, u_mx1, (1, 2, 4, 0)[c])
+            row = model1[c // 2][:, c % 2].rearrange("p t q -> p (t q)")
+            if c < 2:
+                nc.vector.scalar_tensor_tensor(row, scores[:], us_sq[:, PACK + c : PACK + c + 1], ts_row1[:], MULT, MULT)
+            else:
+                nc.scalar.activation(scaled1[:, c % 2, :], scores[:], COPY, scale=us_sq[:, PACK + c : PACK + c + 1])
+                nc.gpsimd.tensor_tensor(row, scaled1[:, c % 2, :], ts_row1[:], MULT)
+        du0.extend([product(0, j, vt_mx0, h_mx0, 4 + j) for j in (1, 2)])
+        target1 = sb([P, PACK, PACK, P], F32, "target1", "pair1")
         for c in range(PACK):
-            nc.scalar.activation(target1[:, c], paired(1, c), COPY, scale=us_neg[:, PACK + c : PACK + c + 1])
-        place_banks = [bank_tile([P, PACK, P], "place_bank", bank) for bank in (4, 5, 6, 3)]
+            nc.scalar.activation(*dealt_targets(target1, 1, c), COPY, scale=us_neg[:, PACK + c : PACK + c + 1])
+        place_banks = [bank_tile([P, PACK, P], "place_bank", bank) for bank in (7, 3, 1, 2)]
         for t in range(PACK):
             for c in range(PACK):
-                turn_onto(place_banks[t][:, c, :], target1[:, c, t // 2, :, t % 2], c == 0, False)
+                turn_onto(place_banks[t][:, c, :], target1[:, c, t, :], c == 0, False)
         for c in range(PACK):
             for t in range(PACK):
-                turn_onto(place_banks[t][:, c, :], model1[:, c, t, :], False, c == PACK - 1)
-        h1 = sb([P, R, PACK], BF16, "h1")
+                turn_onto(place_banks[t][:, c, :], model1[c // 2][:, c % 2, t, :], False, c == PACK - 1)
+        h1 = sb([P, R, PACK], BF16, "h1", "ts_table")
         places1 = sb([P, PACK, R], BF16, "places1")
         for t in range(PACK):
             nc.scalar.activation(places1[:, t, :], place_banks[t][:].rearrange("p c r -> p (c r)"), COPY, scale=ts_cols[1][:, t : t + 1])
         nc.scalar.copy(h1[:], places1[:].rearrange("p t r -> p r t"))
         h_mx1 = mx_tiles("h1")
         quantise(h_mx1, h1[:].rearrange("p r t -> p (r t)"), E5, 0, R)
-        du0.append(product(0, PACK - 1, vt_mx0, h_mx0, 7, "places1"))
+        du0.append(product(0, PACK - 1, vt_mx0, h_mx0, 4, "places1"))
 
         nc.vector.tensor_copy(windows[0][:].indirect(entries(user_list, 0)), du0[0][:])
-        clear_window("raw2_0")
-        clear_window("h0")
+        clear_window("h0_0")
         for j in range(1, PACK):
             nc.vector.tensor_copy(windows[j][:].indirect(entries(user_list, 0)), du0[j][:])
-        du1 = [product(1, j, vt_mx1, h_mx1, 1 + j % 2) for j in range(PACK)]
+        du1 = [product(1, j, vt_mx1, h_mx1, 5 + j % 2, tag) for j, tag in enumerate(("pair0", "pair2", "pair3", "v_picked"))]
         for j in range(PACK):
             nc.vector.tensor_copy(windows[j][:].indirect(entries(user_list, 1)), du1[j][:])
             nc.sync.dma_start(out.rearrange("(m j) c -> m j c", j=PACK)[:, j, :], windows[j][:])

@@ -26,8 +26,8 @@ ALIGN = 256
 LOADS = (
     ((0, 1024, 0), (1024, 2048, 640)),
     ((0, 1024, 512), (1024, 2048, 640)),
-    ((0, 1024, 0), (1024, 2048, 640)),
-    ((0, 1024, 0), (1024, 1664, 384), (1664, 2048, 384)),
+    ((0, 1024, 256), (1024, 2048, 640)),
+    ((0, 1024, 0), (1024, 1664, 512), (1664, 2048, 384)),
 )
 
 
@@ -49,7 +49,6 @@ def tile_attend_gmf_sq_u_kernel(tc, uT, vT, y, us, ts, offs, uoffs, out):
         item_list = keep.tile([P, B * LIST_COLS], U16, name="item_list")
         user_list = keep.tile([P, B * LIST_COLS], U16, name="user_list")
         nc.sync.dma_start(item_list[:], offs)
-        nc.sync.dma_start(user_list[:], uoffs)
 
         us_rows = sb([P, P], F32, "us_rows")
         ts_table = sb([P, T], F32, "ts_table")
@@ -69,8 +68,8 @@ def tile_attend_gmf_sq_u_kernel(tc, uT, vT, y, us, ts, offs, uoffs, out):
 
         def clear_window(tag):
             window = sb([P, TU], F32, "window%d" % len(windows), tag)
-            for c0 in range(0, TU, N):
-                nc.gpsimd.memset(window[:, c0 : c0 + N], 0.0)
+            for c0 in range(0, TU, TU // 2):
+                nc.gpsimd.memset(window[:, c0 : c0 + TU // 2], 0.0)
             windows.append(window)
 
         clear_window("ts_first")
@@ -84,6 +83,8 @@ def tile_attend_gmf_sq_u_kernel(tc, uT, vT, y, us, ts, offs, uoffs, out):
                 nc.sync.dma_start(raw[:], planes[:, :, c0:c1])
                 loaded.append((n, c0, c1, share, raw))
             pair_tables.append(sb([P, T, 2], BF16, "pair%d" % n))
+            if n == 0:
+                nc.sync.dma_start(user_list[:], uoffs)
         pair_words = [pair[:].rearrange("p c e -> p (c e)").bitcast(U32) for pair in pair_tables]
         item_words, user_words = pair_words[0:2], pair_words[2:4]
         y_rows = []
@@ -105,6 +106,9 @@ def tile_attend_gmf_sq_u_kernel(tc, uT, vT, y, us, ts, offs, uoffs, out):
         def mx_tiles(name, tag=None):
             return sb([P, N], U32, name + "_codes", tag), sb([P, N], U8, name + "_scales")
 
+        def half_tiles(name, tag=None):
+            return sb([P, 2 * P], U32, name + "_codes", tag), sb([P, 2 * P], U8, name + "_scales")
+
         def quantise(mx, src, fmt, c0, c1):
             nc.vector.quantize_mx(mx[0][:, c0:c1].bitcast(fmt), mx[1][:, c0:c1], src)
 
@@ -125,12 +129,9 @@ def tile_attend_gmf_sq_u_kernel(tc, uT, vT, y, us, ts, offs, uoffs, out):
             halves = turned[:].rearrange("p t m -> p (t m)").bitcast(BF16)
             nc.scalar.copy(laid.rearrange("p (e m t) -> p e m t", t=PACK, e=2), halves.rearrange("p (t m e) -> p e m t", t=PACK, e=2))
 
-        def items_mx(b, values):
+        def weave_items(b, values):
             woven = values.bitcast(I32).rearrange("p (c u) -> p c u", u=2)
             nc.vector.tensor_copy(woven, v_picked[:, :, b, :].rearrange("p u c -> p c u").bitcast(I32))
-            mx = mx_tiles("v%d" % b)
-            quantise(mx, values, E4, 0, N)
-            return mx
 
         def weave_users(b):
             woven = sb([P, R, 2], U32, "u_woven%d" % b)
@@ -143,7 +144,7 @@ def tile_attend_gmf_sq_u_kernel(tc, uT, vT, y, us, ts, offs, uoffs, out):
             return mx
 
         def dealt_targets(target, b, c):
-            return target[:, c].rearrange("p t q -> p q t"), y_rows[b * PACK + c].rearrange("p (q t) -> p q t", t=PACK)
+            return target.rearrange("p t q -> p q t"), y_rows[b * PACK + c].rearrange("p (q t) -> p q t", t=PACK)
 
         def score(b, c, u_mx, bank):
             rows = slice(c * P, (c + 1) * P)
@@ -158,7 +159,8 @@ def tile_attend_gmf_sq_u_kernel(tc, uT, vT, y, us, ts, offs, uoffs, out):
             nc.tensor.matmul(dst, src, ident[:], start=start, stop=stop, is_transpose=True)
 
         def product(b, j, vt_mx, h_mx, bank, tag=None):
-            cols = slice(j * P, (j + 1) * P)
+            place = j % 2 if b == 0 else j
+            cols = slice(place * P, (place + 1) * P)
             sums = bank_tile([P, R], "du_bank", bank)
             nc.tensor.matmul_mx(
                 sums[:], lhsT=vt_mx[0][:, cols].bitcast(E4), lhsT_scale=vt_mx[1][:, cols],
@@ -192,89 +194,99 @@ def tile_attend_gmf_sq_u_kernel(tc, uT, vT, y, us, ts, offs, uoffs, out):
             ts_cols.append(cols)
             ts_spread.append(spread)
 
-        ts_square0 = sb([P, N], F32, "ts_square0")
+        ts_row0 = sb([P, N], F32, "ts_row0")
         ts_row1 = sb([P, N], F32, "ts_row1")
         round_table(1)
-        nc.scalar.activation(ts_square0[:], ts_spread[0][:].rearrange("p t q -> p (t q)"), SQUARE)
+        nc.scalar.copy(ts_row0[:], ts_spread[0][:].rearrange("p t q -> p (t q)"))
         nc.scalar.copy(ts_row1[:], ts_spread[1][:].rearrange("p t q -> p (t q)"))
         pick_items(1)
         round_table(2)
         v_woven0 = sb([P, PACK * N], BF16, "v_woven0")
-        v_mx = [items_mx(0, v_woven0[:])]
+        weave_items(0, v_woven0[:])
+        v_mx = [mx_tiles("v0")]
+        quantise(v_mx[0], v_woven0[:], E4, 0, N)
         u_picked = sb([P, 2, B, R], U32, "u_picked")
         nc.vector.tensor_copy(u_picked[:, 0].rearrange("p b c -> p (b c)"), user_words[0].indirect(user_list[:]))
         round_table(3)
         for b in range(B):
             nc.vector.tensor_copy(u_picked[:, 1, b, :], user_words[1].indirect(entries(user_list, b)))
         u_mx0 = quantise_users(0, weave_users(0))
-        u_woven1 = weave_users(1)
 
 
-        vt_mx0 = mx_tiles("vt0")
-        for u, tag in enumerate(("raw1_1024", "raw2_1024")):
-            laid = sb([P, 2 * N], BF16, "v_turned0_%d" % u, tag)
-            turn_items(0, u, 4 + u, laid[:])
-            quantise(vt_mx0, laid[:], E4, 2 * P * u, 2 * P * (u + 1))
-        behind_tables = sb([P, PACK, N], F32, "behind_tables", "raw3_1024")
-        v_turned1 = behind_tables[:, 0:2, :].rearrange("p u c -> p (u c)").bitcast(BF16)
-        v_woven1 = behind_tables[:, 2:PACK, :].rearrange("p u c -> p (u c)")
-        for u in range(2):
-            turn_items(1, u, 6 + u, v_turned1[:, 2 * N * u : 2 * N * (u + 1)])
-        nc.scalar.copy(v_woven1.bitcast(U32).rearrange("p (c u) -> p c u", u=2), v_picked[:, :, 1, :].rearrange("p u c -> p c u"))
+        vt_mx0 = [half_tiles("vt0_0")]
+        first_pairs = sb([P, B, 2 * N], BF16, "first_pairs", "raw1_1024")
+        behind_users = sb([P, 6 * N], BF16, "behind_users", "raw2_1024")
+        last_pair0, v_woven1 = behind_users[:, 0 : 2 * N], behind_users[:, 2 * N :]
+        weave_items(1, v_woven1)
+        for u, laid in enumerate((first_pairs[:, 0, :], last_pair0)):
+            turn_items(0, u, 4 + u, laid)
+        quantise(vt_mx0[0], first_pairs[:, 0, :], E4, 0, 2 * P)
+        turn_items(1, 0, 6, first_pairs[:, 1, :])
 
         clear_window("raw3_1664")
         model0 = sb([P, PACK, PACK, P], F32, "model0", "raw2_0")
-        target0 = sb([P, PACK, PACK, P], F32, "target0", "u_woven0")
-        ts_listed0 = ts_spread[0][:].rearrange("p t q -> p q t")
-        h_banks = []
-        for c in range(PACK):
-            nc.vector.scalar_tensor_tensor(*dealt_targets(target0, 0, c), us_neg[:, c : c + 1], ts_listed0, MULT, MULT)
-        for c, bank in enumerate((1, 2, 3, 0)):
-            scores = score(0, c, u_mx0, bank)
-            nc.vector.scalar_tensor_tensor(
-                model0[:, c].rearrange("p t q -> p (t q)"), scores[:], us_sq[:, c : c + 1], ts_square0[:], MULT, MULT
-            )
-        for c in range(PACK):
-            sums = bank_tile([P, PACK, P], "h_bank", 4 + c)
-            for t in range(PACK):
-                turn_onto(sums[:, t, :], target0[:, c, t, :], t == 0, False)
-            h_banks.append(sums)
-        v_mx.append(mx_tiles("v1"))
-        quantise(v_mx[1], v_woven1.bitcast(BF16), E4, 0, N)
-        u_mx1 = quantise_users(1, u_woven1, "y0_2")
+        target0 = [sb([P, 2, PACK, P], F32, "target0_%d" % half, ("raw3_1024", "pair3")[half]) for half in range(2)]
+        for c in range(2):
+            nc.scalar.activation(*dealt_targets(target0[0][:, c], 0, c), COPY, scale=us_neg[:, c : c + 1])
+        u_woven1 = weave_users(1)
+        for c in range(2, PACK):
+            nc.scalar.activation(*dealt_targets(target0[1][:, c - 2], 0, c), COPY, scale=us_neg[:, c : c + 1])
+        last_pair1 = sb([P, 2 * N], BF16, "last_pair1", "y0_2")
+        turn_items(1, 1, 7, last_pair1[:])
+        v_mx.append(mx_tiles("v1", "u_woven0"))
+        quantise(v_mx[1], v_woven1, E4, 0, N)
+        u_mx1 = quantise_users(1, u_woven1)
+        score_banks = [score(0, c, u_mx0, c) for c in range(PACK)]
+        h_banks = [bank_tile([P, PACK, P], "h_bank", 4 + c) for c in range(PACK)]
         h_mx0 = mx_tiles("h0")
-        for c0, c1 in ((0, 2), (2, 3), (3, 4)):
-            h0 = sb([P, (c1 - c0) * P, PACK], BF16, "h0_%d" % c0)
-            for c in range(c0, c1):
-                for t in range(PACK):
-                    turn_onto(h_banks[c][:, t, :], model0[:, c, t, :], False, t == PACK - 1)
-                nc.scalar.copy(h0[:, (c - c0) * P : (c - c0 + 1) * P, :], h_banks[c][:].rearrange("p t r -> p r t"))
-            quantise(h_mx0, h0[:].rearrange("p r t -> p (r t)"), E5, c0 * P, c1 * P)
-        du0 = [product(0, 0, vt_mx0, h_mx0, 4)]
+        h0 = [sb([P, rows, PACK], BF16, "h0_%d" % c0) for c0, rows in ((0, 2 * P), (2, 2 * P))]
+        h0_rows = [h0[c // 2][:, c % 2 * P : (c % 2 + 1) * P, :] for c in range(PACK)]
+        ts_places0 = ts_cols[0].unsqueeze(1).to_broadcast([P, P, PACK])
 
-        vt_mx1 = mx_tiles("vt1", "h0_2")
-        quantise(vt_mx1, v_turned1, E4, 0, D)
-        model1 = [sb([P, 2, PACK, P], F32, "model1_%d" % half, ("h0_3", "raw1_0")[half]) for half in range(2)]
-        scaled1 = sb([P, 2, N], F32, "scaled1", "h0_0")
+        def model_rows0(c):
+            nc.vector.scalar_tensor_tensor(
+                model0[:, c].rearrange("p t q -> p (t q)"), score_banks[c][:], us_sq[:, c : c + 1], ts_row0[:], MULT, MULT
+            )
+            for t in range(PACK):
+                turn_onto(h_banks[c][:, t, :], target0[c // 2][:, c % 2, t, :], t == 0, False)
+            for t in range(PACK):
+                turn_onto(h_banks[c][:, t, :], model0[:, c, t, :], False, t == PACK - 1)
+
         for c in range(PACK):
-            scores = score(1, c, u_mx1, (1, 2, 4, 0)[c])
-            row = model1[c // 2][:, c % 2].rearrange("p t q -> p (t q)")
-            if c < 2:
-                nc.vector.scalar_tensor_tensor(row, scores[:], us_sq[:, PACK + c : PACK + c + 1], ts_row1[:], MULT, MULT)
+            model_rows0(c)
+        for c in range(PACK):
+            nc.vector.tensor_tensor(h0_rows[c], h_banks[c][:].rearrange("p t r -> p r t"), ts_places0, MULT)
+        for part, (c0, c1) in enumerate(((0, 2), (2, 4))):
+            quantise(h_mx0, h0[part][:].rearrange("p r t -> p (r t)"), E5, c0 * P, c1 * P)
+        du0 = [product(0, 0, vt_mx0[0], h_mx0, 4)]
+
+        vt_mx1 = mx_tiles("vt1", "h0_0")
+        for u, laid in enumerate((first_pairs[:, 1, :], last_pair1[:])):
+            quantise(vt_mx1, laid, E4, 2 * P * u, 2 * P * (u + 1))
+        vt_mx0.append(half_tiles("vt0_1", "h0_2"))
+        quantise(vt_mx0[1], last_pair0, E4, 0, 2 * P)
+        model1 = [sb([P, rows, PACK, P], F32, "model1_%d" % c0, tag) for c0, rows, tag in ((0, 1, "y0_2"), (1, 3, "raw2_1024"))]
+        model1_rows = [model1[0][:, 0]] + [model1[1][:, c] for c in range(PACK - 1)]
+        scaled1 = sb([P, PACK - 1, N], F32, "scaled1", "raw1_0")
+        for c in range(PACK):
+            scores = score(1, c, u_mx1, c)
+            row = model1_rows[c].rearrange("p t q -> p (t q)")
+            if c == 0:
+                nc.vector.scalar_tensor_tensor(row, scores[:], us_sq[:, PACK : PACK + 1], ts_row1[:], MULT, MULT)
             else:
-                nc.scalar.activation(scaled1[:, c % 2, :], scores[:], COPY, scale=us_sq[:, PACK + c : PACK + c + 1])
-                nc.gpsimd.tensor_tensor(row, scaled1[:, c % 2, :], ts_row1[:], MULT)
-        du0.extend([product(0, j, vt_mx0, h_mx0, 4 + j) for j in (1, 2)])
+                nc.scalar.activation(scaled1[:, c - 1, :], scores[:], COPY, scale=us_sq[:, PACK + c : PACK + c + 1])
+                nc.gpsimd.tensor_tensor(row, scaled1[:, c - 1, :], ts_row1[:], MULT)
+        du0.extend([product(0, j, vt_mx0[j // 2], h_mx0, 4 + j) for j in (1, 2)])
         target1 = sb([P, PACK, PACK, P], F32, "target1", "pair1")
         for c in range(PACK):
-            nc.scalar.activation(*dealt_targets(target1, 1, c), COPY, scale=us_neg[:, PACK + c : PACK + c + 1])
-        place_banks = [bank_tile([P, PACK, P], "place_bank", bank) for bank in (7, 3, 1, 2)]
+            nc.scalar.activation(*dealt_targets(target1[:, c], 1, c), COPY, scale=us_neg[:, PACK + c : PACK + c + 1])
+        place_banks = [bank_tile([P, PACK, P], "place_bank", bank) for bank in (7, 0, 4, 5)]
         for t in range(PACK):
             for c in range(PACK):
                 turn_onto(place_banks[t][:, c, :], target1[:, c, t, :], c == 0, False)
         for c in range(PACK):
             for t in range(PACK):
-                turn_onto(place_banks[t][:, c, :], model1[c // 2][:, c % 2, t, :], False, c == PACK - 1)
+                turn_onto(place_banks[t][:, c, :], model1_rows[c][:, t, :], False, c == PACK - 1)
         h1 = sb([P, R, PACK], BF16, "h1", "ts_table")
         places1 = sb([P, PACK, R], BF16, "places1")
         for t in range(PACK):
@@ -282,13 +294,13 @@ def tile_attend_gmf_sq_u_kernel(tc, uT, vT, y, us, ts, offs, uoffs, out):
         nc.scalar.copy(h1[:], places1[:].rearrange("p t r -> p r t"))
         h_mx1 = mx_tiles("h1")
         quantise(h_mx1, h1[:].rearrange("p r t -> p (r t)"), E5, 0, R)
-        du0.append(product(0, PACK - 1, vt_mx0, h_mx0, 4, "places1"))
+        du0.append(product(0, PACK - 1, vt_mx0[1], h_mx0, 6, "places1"))
 
         nc.vector.tensor_copy(windows[0][:].indirect(entries(user_list, 0)), du0[0][:])
-        clear_window("h0_0")
+        clear_window("raw2_1024")
         for j in range(1, PACK):
             nc.vector.tensor_copy(windows[j][:].indirect(entries(user_list, 0)), du0[j][:])
-        du1 = [product(1, j, vt_mx1, h_mx1, 5 + j % 2, tag) for j, tag in enumerate(("pair0", "pair2", "pair3", "v_picked"))]
+        du1 = [product(1, j, vt_mx1, h_mx1, 1 + j % 2, tag) for j, tag in enumerate(("pair0", "pair2", "raw3_0", "v_picked"))]
         for j in range(PACK):
             nc.vector.tensor_copy(windows[j][:].indirect(entries(user_list, 1)), du1[j][:])
             nc.sync.dma_start(out.rearrange("(m j) c -> m j c", j=PACK)[:, j, :], windows[j][:])

@@ -24,8 +24,8 @@ LIST_COLS = N // 16
 ALIGN = 256
 
 LOADS = (
-    ((0, 1024, 0), (1024, 2048, 640)),
-    ((0, 1024, 512), (1024, 2048, 640)),
+    ((0, 1024, 0), (1024, 1408, 0), (1408, 2048, 640)),
+    ((0, 1024, 256), (1024, 2048, 640)),
     ((0, 1024, 256), (1024, 2048, 640)),
     ((0, 1024, 0), (1024, 1664, 512), (1664, 2048, 384)),
 )
@@ -59,8 +59,9 @@ def tile_attend_gmf_sq_u_kernel(tc, uT, vT, y, us, ts, offs, uoffs, out):
         nc.vector.tensor_copy(ts_table[0:1, :], ts_first[:])
         nc.sync.dma_start(us_rows[0 : B * PACK, :], us.rearrange("b (c p) o -> (b c) (p o)", p=P))
         ts_picked = sb([P, B, N], F32, "ts_picked")
-        ts_dealt = ts_picked[:].bitcast(U32).rearrange("p b (t q) -> p b q t", t=PACK)
-        nc.vector.tensor_copy(ts_dealt, ts_table[:].bitcast(U32).indirect(item_list[:]))
+        for b in range(B):
+            ts_dealt = ts_picked[:, b, :].bitcast(U32).rearrange("p (t q) -> p q t", t=PACK)
+            nc.vector.tensor_copy(ts_dealt, ts_table[:].bitcast(U32).indirect(entries(item_list, b)))
         ident = sb([P, P], F32, "ident")
         make_identity(nc, ident[:])
 
@@ -172,7 +173,7 @@ def tile_attend_gmf_sq_u_kernel(tc, uT, vT, y, us, ts, offs, uoffs, out):
 
         round_table(0)
         pick_items(0)
-        clear_window("raw0_0")
+        clear_window("raw0_1408")
 
         us_bank = bank_tile([P, PACK, P], "us_bank", 3)
         nc.tensor.transpose(us_bank[:, 0, :], us_rows[:], ident[:])
@@ -181,24 +182,28 @@ def tile_attend_gmf_sq_u_kernel(tc, uT, vT, y, us, ts, offs, uoffs, out):
         nc.scalar.activation(us_neg[:], us_bank[:, 0, 0 : B * PACK], COPY, scale=-1.0)
         nc.scalar.activation(us_sq[:], us_bank[:, 0, 0 : B * PACK], SQUARE)
         ts_cols, ts_spread = [], []
-        ts_cols_all = sb([P, B, PACK], F32, "ts_cols", "raw0_1024")
+        ts_cols0 = sb([P, PACK], F32, "ts_cols0")
+        ts_held = sb([P, 2 * N + 8], F32, "ts_held", "raw0_1024")
+        ts_row0, ts_row1 = ts_held[:, 0:N], ts_held[:, N : 2 * N]
         for b in range(B):
             turned = bank_tile([P, PACK, P], "ts_turned", 1 + b)
             for t in range(PACK):
                 nc.tensor.transpose(turned[:, t, :], ts_picked[:, b, t * P : (t + 1) * P], ident[:])
-            cols = ts_cols_all[:, b, :]
-            nc.scalar.activation(cols, turned[:, :, 0], COPY)
+            if b == 0:
+                cols = ts_cols0[:]
+                nc.vector.tensor_copy(cols, turned[:, :, 0])
+            else:
+                cols = ts_held[:, 2 * N : 2 * N + PACK]
+                nc.scalar.activation(cols, turned[:, :, 0], COPY)
             spread = bank_tile([P, PACK, P], "ts_spread", (0, 3)[b])
             for t in range(PACK):
                 nc.tensor.transpose(spread[:, t, :], cols[:, t : t + 1].to_broadcast([P, P]), ident[:])
             ts_cols.append(cols)
             ts_spread.append(spread)
 
-        ts_row0 = sb([P, N], F32, "ts_row0")
-        ts_row1 = sb([P, N], F32, "ts_row1")
         round_table(1)
-        nc.scalar.copy(ts_row0[:], ts_spread[0][:].rearrange("p t q -> p (t q)"))
-        nc.scalar.copy(ts_row1[:], ts_spread[1][:].rearrange("p t q -> p (t q)"))
+        nc.scalar.copy(ts_row0, ts_spread[0][:].rearrange("p t q -> p (t q)"))
+        nc.scalar.copy(ts_row1, ts_spread[1][:].rearrange("p t q -> p (t q)"))
         pick_items(1)
         round_table(2)
         v_woven0 = sb([P, PACK * N], BF16, "v_woven0")
@@ -245,7 +250,7 @@ def tile_attend_gmf_sq_u_kernel(tc, uT, vT, y, us, ts, offs, uoffs, out):
 
         def model_rows0(c):
             nc.vector.scalar_tensor_tensor(
-                model0[:, c].rearrange("p t q -> p (t q)"), score_banks[c][:], us_sq[:, c : c + 1], ts_row0[:], MULT, MULT
+                model0[:, c].rearrange("p t q -> p (t q)"), score_banks[c][:], us_sq[:, c : c + 1], ts_row0, MULT, MULT
             )
             for t in range(PACK):
                 turn_onto(h_banks[c][:, t, :], target0[c // 2][:, c % 2, t, :], t == 0, False)
@@ -267,15 +272,15 @@ def tile_attend_gmf_sq_u_kernel(tc, uT, vT, y, us, ts, offs, uoffs, out):
         quantise(vt_mx0[1], last_pair0, E4, 0, 2 * P)
         model1 = [sb([P, rows, PACK, P], F32, "model1_%d" % c0, tag) for c0, rows, tag in ((0, 1, "y0_2"), (1, 3, "raw2_1024"))]
         model1_rows = [model1[0][:, 0]] + [model1[1][:, c] for c in range(PACK - 1)]
-        scaled1 = sb([P, PACK - 1, N], F32, "scaled1", "raw1_0")
+        scaled1 = sb([P, PACK - 1, N], F32, "scaled1", "pair0")
         for c in range(PACK):
             scores = score(1, c, u_mx1, c)
             row = model1_rows[c].rearrange("p t q -> p (t q)")
             if c == 0:
-                nc.vector.scalar_tensor_tensor(row, scores[:], us_sq[:, PACK : PACK + 1], ts_row1[:], MULT, MULT)
+                nc.vector.scalar_tensor_tensor(row, scores[:], us_sq[:, PACK : PACK + 1], ts_row1, MULT, MULT)
             else:
                 nc.scalar.activation(scaled1[:, c - 1, :], scores[:], COPY, scale=us_sq[:, PACK + c : PACK + c + 1])
-                nc.gpsimd.tensor_tensor(row, scaled1[:, c - 1, :], ts_row1[:], MULT)
+                nc.gpsimd.tensor_tensor(row, scaled1[:, c - 1, :], ts_row1, MULT)
         du0.extend([product(0, j, vt_mx0[j // 2], h_mx0, 4 + j) for j in (1, 2)])
         target1 = sb([P, PACK, PACK, P], F32, "target1", "pair1")
         for c in range(PACK):
@@ -300,7 +305,7 @@ def tile_attend_gmf_sq_u_kernel(tc, uT, vT, y, us, ts, offs, uoffs, out):
         clear_window("raw2_1024")
         for j in range(1, PACK):
             nc.vector.tensor_copy(windows[j][:].indirect(entries(user_list, 0)), du0[j][:])
-        du1 = [product(1, j, vt_mx1, h_mx1, 1 + j % 2, tag) for j, tag in enumerate(("pair0", "pair2", "raw3_0", "v_picked"))]
+        du1 = [product(1, j, vt_mx1, h_mx1, 1 + j % 2, tag) for j, tag in enumerate(("ts_picked", "pair2", "raw3_0", "v_picked"))]
         for j in range(PACK):
             nc.vector.tensor_copy(windows[j][:].indirect(entries(user_list, 1)), du1[j][:])
             nc.sync.dma_start(out.rearrange("(m j) c -> m j c", j=PACK)[:, j, :], windows[j][:])

@@ -213,9 +213,14 @@ def tile_attend_gmf_sq_u_kernel(tc, uT, vT, y, us, ts, offs, uoffs, out):
         u_picked = sb([P, 2, B, R], U32, "u_picked")
         nc.vector.tensor_copy(u_picked[:, 0].rearrange("p b c -> p (b c)"), user_words[0].indirect(user_list[:]))
         round_table(3)
-        for b in range(B):
-            nc.vector.tensor_copy(u_picked[:, 1, b, :], user_words[1].indirect(entries(user_list, b)))
-        u_mx0 = quantise_users(0, weave_users(0))
+        u_woven0 = sb([P, R, 2], U32, "u_woven0")
+        u_mx0 = mx_tiles("u0")
+        for c0 in range(0, R, R // 2):
+            c1 = c0 + R // 2
+            nc.vector.tensor_copy(u_picked[:, 1, 0, c0:c1], user_words[1].indirect(user_list[:, c0 // 16 : c1 // 16]))
+            nc.scalar.copy(u_woven0[:, c0:c1, :], u_picked[:, :, 0, c0:c1].rearrange("p u c -> p c u"))
+            quantise(u_mx0, as_values(u_woven0)[:, PACK * c0 : PACK * c1], E4, c0, c1)
+        nc.vector.tensor_copy(u_picked[:, 1, 1, :], user_words[1].indirect(entries(user_list, 1)))
 
 
         vt_mx0 = [half_tiles("vt0_0")]
@@ -230,17 +235,16 @@ def tile_attend_gmf_sq_u_kernel(tc, uT, vT, y, us, ts, offs, uoffs, out):
 
         clear_window("raw3_1664")
         model0 = sb([P, PACK, PACK, P], F32, "model0", "raw2_0")
-        target0 = [sb([P, 2, PACK, P], F32, "target0_%d" % half, ("raw3_1024", "pair3")[half]) for half in range(2)]
+        target0 = [sb([P, 2, PACK, P], F32, "target0_%d" % half, ("raw3_1024", None)[half]) for half in range(2)]
         for c in range(2):
             nc.scalar.activation(*dealt_targets(target0[0][:, c], 0, c), COPY, scale=us_neg[:, c : c + 1])
-        u_woven1 = weave_users(1)
         for c in range(2, PACK):
             nc.scalar.activation(*dealt_targets(target0[1][:, c - 2], 0, c), COPY, scale=us_neg[:, c : c + 1])
+        u_woven1 = weave_users(1)
         last_pair1 = sb([P, 2 * N], BF16, "last_pair1", "y0_2")
         turn_items(1, 1, 7, last_pair1[:])
         v_mx.append(mx_tiles("v1", "u_woven0"))
         quantise(v_mx[1], v_woven1, E4, 0, N)
-        u_mx1 = quantise_users(1, u_woven1)
         score_banks = [score(0, c, u_mx0, c) for c in range(PACK)]
         h_banks = [bank_tile([P, PACK, P], "h_bank", 4 + c) for c in range(PACK)]
         h_mx0 = mx_tiles("h0")
@@ -259,6 +263,7 @@ def tile_attend_gmf_sq_u_kernel(tc, uT, vT, y, us, ts, offs, uoffs, out):
 
         for c in range(PACK):
             model_rows0(c)
+        u_mx1 = quantise_users(1, u_woven1)
         for c in range(PACK):
             nc.vector.tensor_tensor(h0_rows[c], h_banks[c][:].rearrange("p t r -> p r t"), ts_places0, MULT)
         for part, (c0, c1) in enumerate(((0, 2), (2, 4))):
@@ -272,7 +277,7 @@ def tile_attend_gmf_sq_u_kernel(tc, uT, vT, y, us, ts, offs, uoffs, out):
         quantise(vt_mx0[1], last_pair0, E4, 0, 2 * P)
         model1 = [sb([P, rows, PACK, P], F32, "model1_%d" % c0, tag) for c0, rows, tag in ((0, 1, "y0_2"), (1, 3, "raw2_1024"))]
         model1_rows = [model1[0][:, 0]] + [model1[1][:, c] for c in range(PACK - 1)]
-        scaled1 = sb([P, PACK - 1, N], F32, "scaled1", "pair0")
+        scaled1 = sb([P, PACK - 1, N], F32, "scaled1", "raw1_0")
         for c in range(PACK):
             scores = score(1, c, u_mx1, c)
             row = model1_rows[c].rearrange("p t q -> p (t q)")

@@ -213,24 +213,23 @@ def tile_attend_gmf_sq_u_kernel(tc, uT, vT, y, us, ts, offs, uoffs, out):
         u_picked = sb([P, 2, B, R], U32, "u_picked")
         nc.vector.tensor_copy(u_picked[:, 0].rearrange("p b c -> p (b c)"), user_words[0].indirect(user_list[:]))
         round_table(3)
-        u_woven0 = sb([P, R, 2], U32, "u_woven0")
         u_mx0 = mx_tiles("u0")
         for c0 in range(0, R, R // 2):
             c1 = c0 + R // 2
             nc.vector.tensor_copy(u_picked[:, 1, 0, c0:c1], user_words[1].indirect(user_list[:, c0 // 16 : c1 // 16]))
-            nc.scalar.copy(u_woven0[:, c0:c1, :], u_picked[:, :, 0, c0:c1].rearrange("p u c -> p c u"))
-            quantise(u_mx0, as_values(u_woven0)[:, PACK * c0 : PACK * c1], E4, c0, c1)
+            woven = sb([P, R // 2, 2], U32, "u_woven0_%d" % c0)
+            nc.scalar.copy(woven[:], u_picked[:, :, 0, c0:c1].rearrange("p u c -> p c u"))
+            quantise(u_mx0, as_values(woven), E4, c0, c1)
         nc.vector.tensor_copy(u_picked[:, 1, 1, :], user_words[1].indirect(entries(user_list, 1)))
 
 
-        vt_mx0 = [half_tiles("vt0_0")]
+        vt_mx0 = [half_tiles("vt0_0", "u_woven0_256")]
         first_pairs = sb([P, B, 2 * N], BF16, "first_pairs", "raw1_1024")
         behind_users = sb([P, 6 * N], BF16, "behind_users", "raw2_1024")
         last_pair0, v_woven1 = behind_users[:, 0 : 2 * N], behind_users[:, 2 * N :]
         weave_items(1, v_woven1)
         for u, laid in enumerate((first_pairs[:, 0, :], last_pair0)):
             turn_items(0, u, 4 + u, laid)
-        quantise(vt_mx0[0], first_pairs[:, 0, :], E4, 0, 2 * P)
         turn_items(1, 0, 6, first_pairs[:, 1, :])
 
         clear_window("raw3_1664")
@@ -243,8 +242,9 @@ def tile_attend_gmf_sq_u_kernel(tc, uT, vT, y, us, ts, offs, uoffs, out):
         u_woven1 = weave_users(1)
         last_pair1 = sb([P, 2 * N], BF16, "last_pair1", "y0_2")
         turn_items(1, 1, 7, last_pair1[:])
-        v_mx.append(mx_tiles("v1", "u_woven0"))
+        v_mx.append(mx_tiles("v1", "u_woven0_0"))
         quantise(v_mx[1], v_woven1, E4, 0, N)
+        quantise(vt_mx0[0], first_pairs[:, 0, :], E4, 0, 2 * P)
         score_banks = [score(0, c, u_mx0, c) for c in range(PACK)]
         h_banks = [bank_tile([P, PACK, P], "h_bank", 4 + c) for c in range(PACK)]
         h_mx0 = mx_tiles("h0")

@@ -20,15 +20,10 @@ COPY = mybir.ActivationFunctionType.Copy
 
 P = 128
 PACK = 4
-LIST_COLS = N // 16
+UNIT = 256
+UNITS = B * R // UNIT
+BLOCKS = UNIT // P
 ALIGN = 256
-
-LOADS = (
-    ((0, 1024, 0), (1024, 1408, 0), (1408, 2048, 640)),
-    ((0, 1024, 256), (1024, 2048, 640)),
-    ((0, 1024, 256), (1024, 2048, 640)),
-    ((0, 1024, 0), (1024, 1664, 512), (1664, 2048, 384)),
-)
 
 
 def tile_attend_gmf_sq_u_kernel(tc, uT, vT, y, us, ts, offs, uoffs, out):
@@ -43,274 +38,295 @@ def tile_attend_gmf_sq_u_kernel(tc, uT, vT, y, us, ts, offs, uoffs, out):
         def bank_tile(shape, name, bank):
             return psum.tile(shape, F32, name=name, tag="bank%d" % bank)
 
-        def entries(offsets, b):
-            return offsets[:, b * LIST_COLS : (b + 1) * LIST_COLS]
+        def entries(offsets, e0, e1):
+            return offsets[:, e0 // 16 : e1 // 16]
 
-        item_list = keep.tile([P, B * LIST_COLS], U16, name="item_list")
-        user_list = keep.tile([P, B * LIST_COLS], U16, name="user_list")
-        nc.sync.dma_start(item_list[:], offs)
+        def load_plane(table, j, name):
+            plane = sb([P, T], F32, name)
+            nc.sync.dma_start(plane[:], table.rearrange("(p j) c -> p j c", j=PACK)[:, j, :])
+            return plane
 
-        us_rows = sb([P, P], F32, "us_rows")
-        ts_table = sb([P, T], F32, "ts_table")
-        ts_first = sb([1, T], F32, "ts_first")
-        nc.sync.dma_start(ts_first[:], ts[0:1, :])
-        nc.vector.memset(us_rows[:], 0.0)
-        nc.vector.memset(ts_table[:].bitcast(I32), 0)
-        nc.vector.tensor_copy(ts_table[0:1, :], ts_first[:])
-        nc.sync.dma_start(us_rows[0 : B * PACK, :], us.rearrange("b (c p) o -> (b c) (p o)", p=P))
-        ts_picked = sb([P, B, N], F32, "ts_picked")
-        for b in range(B):
-            ts_dealt = ts_picked[:, b, :].bitcast(U32).rearrange("p (t q) -> p q t", t=PACK)
-            nc.vector.tensor_copy(ts_dealt, ts_table[:].bitcast(U32).indirect(entries(item_list, b)))
-        ident = sb([P, P], F32, "ident")
-        make_identity(nc, ident[:])
+        def gather(engine, dst, plane, offsets):
+            if engine is nc.vector:
+                nc.vector.tensor_copy(dst, plane[:].indirect(offsets))
+            else:
+                nc.scalar.activation(dst, plane[:].indirect(offsets), COPY)
 
-        windows = []
+        def mx_tiles(name, width, tag=None):
+            return sb([P, width], U32, name + "_codes", tag), sb([P, width], U8, name + "_scales")
 
-        def clear_window(tag):
-            window = sb([P, TU], F32, "window%d" % len(windows), tag)
-            for c0 in range(0, TU, TU // 2):
-                nc.gpsimd.memset(window[:, c0 : c0 + TU // 2], 0.0)
-            windows.append(window)
-
-        clear_window("ts_first")
-
-        pair_tables = []
-        loaded = []
-        for n, (table, u) in enumerate(((vT, 0), (vT, 1), (uT, 0), (uT, 1))):
-            planes = table.rearrange("(p t) c -> p t c", t=PACK)[:, 2 * u : 2 * u + 2, :]
-            for c0, c1, share in LOADS[n]:
-                raw = sb([P, 2, c1 - c0], F32, "raw%d_%d" % (n, c0))
-                nc.sync.dma_start(raw[:], planes[:, :, c0:c1])
-                loaded.append((n, c0, c1, share, raw))
-            pair_tables.append(sb([P, T, 2], BF16, "pair%d" % n))
-            if n == 0:
-                nc.sync.dma_start(user_list[:], uoffs)
-        pair_words = [pair[:].rearrange("p c e -> p (c e)").bitcast(U32) for pair in pair_tables]
-        item_words, user_words = pair_words[0:2], pair_words[2:4]
-        y_rows = []
-        for b, c0, c1 in ((0, 0, 1), (0, 1, 2), (0, 2, 4), (1, 0, 4)):
-            rows_in = sb([P, c1 - c0, N], F32, "y%d_%d" % (b, c0))
-            nc.sync.dma_start(rows_in[:], y[b].rearrange("(c p) i -> p c i", p=P)[:, c0:c1, :])
-            y_rows.extend([rows_in[:, c, :] for c in range(c1 - c0)])
-
-        def round_table(n):
-            for m, c0, c1, share, raw in loaded:
-                if m == n:
-                    cut = c1 - c0 - share
-                    side_by_side = raw[:].rearrange("p e c -> p c e")
-                    if cut:
-                        nc.scalar.activation(pair_tables[n][:, c0 : c0 + cut, :], side_by_side[:, 0:cut, :], COPY)
-                    if share:
-                        nc.vector.tensor_copy(pair_tables[n][:, c0 + cut : c1, :], side_by_side[:, cut:, :])
-
-        def mx_tiles(name, tag=None):
-            return sb([P, N], U32, name + "_codes", tag), sb([P, N], U8, name + "_scales")
-
-        def half_tiles(name, tag=None):
-            return sb([P, 2 * P], U32, name + "_codes", tag), sb([P, 2 * P], U8, name + "_scales")
-
-        def quantise(mx, src, fmt, c0, c1):
-            nc.vector.quantize_mx(mx[0][:, c0:c1].bitcast(fmt), mx[1][:, c0:c1], src)
-
-        def as_values(woven):
-            return woven[:].rearrange("p c u -> p (c u)").bitcast(BF16)
-
-        v_picked = sb([P, 2, B, N], U32, "v_picked")
-
-        def pick_items(u):
-            dealt = v_picked[:, u].rearrange("p b (t q) -> p b q t", t=PACK)
-            nc.vector.tensor_copy(dealt, item_words[u].indirect(item_list[:]))
-
-        def turn_items(b, u, bank, laid):
-            words = v_picked[:, u, b, :].bitcast(F32)
-            turned = bank_tile([P, PACK, P], "v_bank", bank)
-            for t in range(PACK):
-                nc.tensor.transpose(turned[:, t, :], words[:, t * P : (t + 1) * P], ident[:])
-            halves = turned[:].rearrange("p t m -> p (t m)").bitcast(BF16)
-            nc.scalar.copy(laid.rearrange("p (e m t) -> p e m t", t=PACK, e=2), halves.rearrange("p (t m e) -> p e m t", t=PACK, e=2))
-
-        def weave_items(b, values):
-            woven = values.bitcast(I32).rearrange("p (c u) -> p c u", u=2)
-            nc.vector.tensor_copy(woven, v_picked[:, :, b, :].rearrange("p u c -> p c u").bitcast(I32))
-
-        def weave_users(b):
-            woven = sb([P, R, 2], U32, "u_woven%d" % b)
-            nc.scalar.copy(woven[:], u_picked[:, :, b, :].rearrange("p u c -> p c u"))
-            return woven
-
-        def quantise_users(b, woven, tag=None):
-            mx = mx_tiles("u%d" % b, tag)
-            quantise(mx, as_values(woven), E4, 0, R)
-            return mx
-
-        def dealt_targets(target, b, c):
-            return target.rearrange("p t q -> p q t"), y_rows[b * PACK + c].rearrange("p (q t) -> p q t", t=PACK)
-
-        def score(b, c, u_mx, bank):
-            rows = slice(c * P, (c + 1) * P)
-            scores = bank_tile([P, N], "scores", bank)
-            nc.tensor.matmul_mx(
-                scores[:], lhsT=u_mx[0][:, rows].bitcast(E4), lhsT_scale=u_mx[1][:, rows],
-                rhs=v_mx[b][0][:].bitcast(E4), rhs_scale=v_mx[b][1][:], start=True, stop=True,
-            )
-            return scores
+        def quantise(mx, src, fmt):
+            nc.vector.quantize_mx(mx[0][:].bitcast(fmt), mx[1][:], src)
 
         def turn_onto(dst, src, start, stop):
             nc.tensor.matmul(dst, src, ident[:], start=start, stop=stop, is_transpose=True)
 
-        def product(b, j, vt_mx, h_mx, bank, tag=None):
-            place = j % 2 if b == 0 else j
-            cols = slice(place * P, (place + 1) * P)
-            sums = bank_tile([P, R], "du_bank", bank)
-            nc.tensor.matmul_mx(
-                sums[:], lhsT=vt_mx[0][:, cols].bitcast(E4), lhsT_scale=vt_mx[1][:, cols],
-                rhs=h_mx[0][:].bitcast(E5), rhs_scale=h_mx[1][:], start=True, stop=True,
-            )
-            du = sb([P, R], F32, "du%d_%d" % (b, j), tag)
-            nc.scalar.copy(du[:], sums[:])
-            return du
+        item_list = keep.tile([P, B * N // 16], U16, name="item_list")
+        user_list = keep.tile([P, B * R // 16], U16, name="user_list")
+        ts_first = sb([1, T], F32, "ts_first")
+        us_first = sb([B * PACK, P], F32, "us_first")
+        nc.sync.dma_start(item_list[:], offs)
+        nc.sync.dma_start(us_first[:], us.rearrange("b (c p) o -> (b c) (p o)", p=P))
+        nc.sync.dma_start(ts_first[:], ts[0:1, :])
+        v_planes = [load_plane(vT, j, "v%d" % j) for j in (0, 1)]
+        nc.sync.dma_start(user_list[:], uoffs)
+        v_planes.extend([load_plane(vT, j, "v%d" % j) for j in (2, 3)])
+        u_planes = [load_plane(uT, j, "u%d" % j) for j in range(PACK)]
+        y_units = []
+        for k in range(UNITS):
+            rows_in = sb([P, BLOCKS, N], F32, "y%d" % k)
+            nc.sync.dma_start(rows_in[:], y.rearrange("b (c p) i -> p (b c) i", p=P)[:, k * BLOCKS : (k + 1) * BLOCKS, :])
+            y_units.append(rows_in)
 
-        round_table(0)
-        pick_items(0)
-        clear_window("raw0_1408")
+        ident = sb([P, P], F32, "ident")
+        make_identity(nc, ident[:])
+        windows = []
 
-        us_bank = bank_tile([P, PACK, P], "us_bank", 3)
-        nc.tensor.transpose(us_bank[:, 0, :], us_rows[:], ident[:])
+        def clear_window(tag):
+            window = sb([P, TU], F32, "window%d" % len(windows), tag)
+            for c0 in range(0, TU, TU // 4):
+                nc.gpsimd.memset(window[:, c0 : c0 + TU // 4], 0.0)
+            windows.append(window)
+
+        clear_window(None)
+        clear_window(None)
+
+        ts_table = sb([P, T], F32, "ts_table")
+        us_rows = sb([P, P], F32, "us_rows")
+        nc.vector.memset(us_rows[:], 0.0)
+        nc.vector.memset(ts_table[:].bitcast(I32), 0)
+        nc.scalar.activation(us_rows[0 : B * PACK, :], us_first[:], COPY)
+        nc.vector.tensor_copy(ts_table[0:1, :], ts_first[:])
+        ts_picked = sb([P, B, N], F32, "ts_picked")
+        gather(nc.vector, ts_picked[:].rearrange("p b i -> p (b i)"), ts_table, item_list[:])
+
+        v_picked = sb([P, PACK * B * N], BF16, "v_picked")
+        vt_mx = []
+
+        def item_plane(j):
+            return v_picked[:, j * B * N : (j + 1) * B * N]
+
+        def turn_items(j, bank, laid):
+            words = item_plane(j).bitcast(F32)
+            turned = bank_tile([P, B, 2, P], "v_bank", bank)
+            for b in range(B):
+                for u in range(2):
+                    nc.tensor.transpose(turned[:, b, u, :], words[:, b * 2 * P + u : (b + 1) * 2 * P : 2], ident[:])
+            nc.scalar.copy(laid.bitcast(F32).rearrange("p (b m u) -> p b m u", b=B, u=2), turned[:].rearrange("p b u m -> p b m u"))
+
+        def quantise_turned(name, laid, planes, tag):
+            mx = mx_tiles(name, planes * B * P, tag)
+            quantise(mx, laid[:], E4)
+            vt_mx.extend([(mx, s * B * P) for s in range(planes)])
+
+        gather(nc.scalar, item_plane(0), v_planes[0], item_list[:])
+        clear_window("v0")
+        gather(nc.vector, item_plane(1), v_planes[1], item_list[:])
+        clear_window("v1")
+        laid01 = sb([P, 2 * B * N], BF16, "v_laid01")
+        turn_items(0, 0, laid01[:, 0 : B * N])
+
+        ts_cols = sb([P, B, PACK], F32, "ts_cols")
+        ts_rows = sb([P, B, N], F32, "ts_rows")
+        for b in range(B):
+            turned = bank_tile([P, PACK, P], "ts_turned", 4 + b)
+            for t in range(PACK):
+                nc.tensor.transpose(turned[:, t, :], ts_picked[:, b, t::PACK], ident[:])
+            nc.scalar.copy(ts_cols[:, b, :], turned[:, :, 0])
+            spread = bank_tile([P, PACK, P], "ts_spread", 6 + b)
+            for t in range(PACK):
+                nc.tensor.transpose(spread[:, t, :], ts_cols[:, b, t : t + 1].to_broadcast([P, P]), ident[:])
+            nc.scalar.copy(ts_rows[:, b, :], spread[:].rearrange("p t q -> p (t q)"))
+
+        def pick_items_by_group(j):
+            for b, engine in enumerate((nc.vector, nc.scalar)):
+                gather(engine, item_plane(j)[:, b * N : (b + 1) * N], v_planes[j], entries(item_list, b * N, (b + 1) * N))
+
+        turn_items(1, 1, laid01[:, B * N :])
+        gather(nc.vector, item_plane(2), v_planes[2], item_list[:])
+        quantise_turned("vt01", laid01, 2, "v2")
+        us_bank = bank_tile([P, P], "us_bank", 4)
+        nc.tensor.transpose(us_bank[:], us_rows[:], ident[:])
         us_neg = sb([P, B * PACK], F32, "us_neg")
         us_sq = sb([P, B * PACK], F32, "us_sq")
-        nc.scalar.activation(us_neg[:], us_bank[:, 0, 0 : B * PACK], COPY, scale=-1.0)
-        nc.scalar.activation(us_sq[:], us_bank[:, 0, 0 : B * PACK], SQUARE)
-        ts_cols, ts_spread = [], []
-        ts_cols0 = sb([P, PACK], F32, "ts_cols0")
-        ts_held = sb([P, 2 * N + 8], F32, "ts_held", "raw0_1024")
-        ts_row0, ts_row1 = ts_held[:, 0:N], ts_held[:, N : 2 * N]
+        nc.scalar.activation(us_neg[:], us_bank[:, 0 : B * PACK], COPY, scale=-1.0)
+        nc.scalar.activation(us_sq[:], us_bank[:, 0 : B * PACK], SQUARE)
+        pick_items_by_group(3)
+        laid2 = sb([P, B * N], BF16, "v_laid2", "v3")
+        turn_items(2, 2, laid2[:])
+        v_mx = []
         for b in range(B):
-            turned = bank_tile([P, PACK, P], "ts_turned", 1 + b)
-            for t in range(PACK):
-                nc.tensor.transpose(turned[:, t, :], ts_picked[:, b, t * P : (t + 1) * P], ident[:])
+            woven = sb([P, N * PACK], BF16, "v_woven%d" % b)
+            planes = v_picked[:].rearrange("p (j b q t) -> p b t q j", j=PACK, b=B, t=PACK)[:, b]
+            nc.vector.tensor_copy(woven[:].rearrange("p (t q j) -> p t q j", t=PACK, j=PACK), planes)
             if b == 0:
-                cols = ts_cols0[:]
-                nc.vector.tensor_copy(cols, turned[:, :, 0])
+                quantise_turned("vt2", laid2, 1, None)
+            v_mx.append(mx_tiles("v%d" % b, N))
+            quantise(v_mx[b], woven[:], E4)
+
+        u_picked = sb([P, PACK * B * R], BF16, "u_picked")
+        u_by_plane = u_picked[:].rearrange("p (j r) -> p j r", j=PACK)
+
+        def pick_users(engine, j, r0, r1):
+            gather(engine, u_picked[:, j * B * R + r0 : j * B * R + r1], u_planes[j], entries(user_list, r0, r1))
+
+        pick_users(nc.scalar, 0, 0, B * R)
+        pick_users(nc.scalar, 1, 0, B * R)
+        pick_users(nc.vector, 2, 0, R)
+        pick_users(nc.scalar, 2, R, B * R)
+        first_woven = sb([P, UNIT, PACK], BF16, "u_woven0")
+        nc.vector.tensor_copy(first_woven[:, :, 0:3], u_by_plane[:, 0:3, 0:UNIT].rearrange("p j r -> p r j"))
+        gather(nc.vector, first_woven[:, :, 3], u_planes[3], entries(user_list, 0, UNIT))
+        pick_users(nc.scalar, 3, UNIT, R)
+        pick_users(nc.scalar, 3, R, B * R)
+
+        def weave_users(k, tag):
+            woven = sb([P, UNIT, PACK], BF16, "u_woven%d" % k, tag)
+            nc.vector.tensor_copy(woven[:], u_by_plane[:, :, k * UNIT : (k + 1) * UNIT].rearrange("p j r -> p r j"))
+            return woven
+
+        def quantise_users(k, woven):
+            mx = mx_tiles("u%d" % k, UNIT)
+            quantise(mx, woven[:].rearrange("p r j -> p (r j)"), E4)
+            return mx
+
+        targets = [sb([P, PACK, PACK, P], F32, "target%d" % b, "u%d" % b) for b in range(B)]
+        h_banks = {}
+
+        def scale_targets(k):
+            for c in range(BLOCKS):
+                block = k * BLOCKS + c
+                target = targets[block // PACK][:, block % PACK]
+                rows_in = y_units[k][:, c, :].rearrange("p (q t) -> p q t", t=PACK)
+                nc.scalar.activation(target.rearrange("p t q -> p q t"), rows_in, COPY, scale=us_neg[:, block : block + 1])
+
+        def turn_targets(k):
+            for c in range(BLOCKS):
+                block = k * BLOCKS + c
+                h_banks[block] = bank_tile([P, PACK, P], "h_bank", 4 + block % PACK)
+                for t in range(PACK):
+                    turn_onto(h_banks[block][:, t, :], targets[block // PACK][:, block % PACK, t, :], t == 0, False)
+
+        def score(k, u_mx):
+            banks = []
+            for c in range(BLOCKS):
+                rows = slice(c * P, (c + 1) * P)
+                scores = bank_tile([P, N], "scores", (k * BLOCKS + c) % PACK)
+                b = k * UNIT // R
+                nc.tensor.matmul_mx(
+                    scores[:], lhsT=u_mx[0][:, rows].bitcast(E4), lhsT_scale=u_mx[1][:, rows],
+                    rhs=v_mx[b][0][:].bitcast(E4), rhs_scale=v_mx[b][1][:], start=True, stop=True,
+                )
+                banks.append(scores)
+            return banks
+
+        def model_block(k, c, scores):
+            block = k * BLOCKS + c
+            model = sb([P, N], F32, "model%d" % block)
+            nc.vector.scalar_tensor_tensor(model[:], scores[c][:], us_sq[:, block : block + 1], ts_rows[:, block // PACK, :], MULT, MULT)
+            for t in range(PACK):
+                turn_onto(h_banks[block][:, t, :], model[:, t * P : (t + 1) * P], False, t == PACK - 1)
+
+        def finish_h(k):
+            h = sb([P, UNIT, PACK], BF16, "h%d" % k)
+            places = ts_cols[:, k * UNIT // R, :].unsqueeze(1).to_broadcast([P, P, PACK])
+            for c in range(BLOCKS):
+                nc.vector.tensor_tensor(h[:, c * P : (c + 1) * P, :], h_banks[k * BLOCKS + c][:].rearrange("p t r -> p r t"), places, MULT)
+            return h
+
+        du_halves = [sb([P, 2, B * R], F32, "du%d" % half, ("ts_first", "ts_table")[half]) for half in range(2)]
+
+        def products(k, h):
+            h_mx = mx_tiles("h%d" % k, UNIT)
+            quantise(h_mx, h[:].rearrange("p r t -> p (r t)"), E5)
+            banks = []
+            for half in range(2):
+                sums = bank_tile([P, 2, UNIT], "du_bank", 4 + (k * BLOCKS + half) % PACK)
+                for s in range(2):
+                    vt, first = vt_mx[2 * half + s]
+                    cols = slice(first + k * UNIT // R * P, first + (k * UNIT // R + 1) * P)
+                    nc.tensor.matmul_mx(
+                        sums[:, s, :], lhsT=vt[0][:, cols].bitcast(E4), lhsT_scale=vt[1][:, cols],
+                        rhs=h_mx[0][:].bitcast(E5), rhs_scale=h_mx[1][:], start=True, stop=True,
+                    )
+                banks.append(sums)
+            return banks
+
+        def copy_out(engine, k, half, banks):
+            dst = du_halves[half][:, :, k * UNIT : (k + 1) * UNIT]
+            if engine is nc.vector:
+                nc.vector.tensor_copy(dst, banks[half][:])
             else:
-                cols = ts_held[:, 2 * N : 2 * N + PACK]
-                nc.scalar.activation(cols, turned[:, :, 0], COPY)
-            spread = bank_tile([P, PACK, P], "ts_spread", (0, 3)[b])
-            for t in range(PACK):
-                nc.tensor.transpose(spread[:, t, :], cols[:, t : t + 1].to_broadcast([P, P]), ident[:])
-            ts_cols.append(cols)
-            ts_spread.append(spread)
+                nc.scalar.copy(dst, banks[half][:])
 
-        round_table(1)
-        nc.scalar.copy(ts_row0, ts_spread[0][:].rearrange("p t q -> p (t q)"))
-        nc.scalar.copy(ts_row1, ts_spread[1][:].rearrange("p t q -> p (t q)"))
-        pick_items(1)
-        round_table(2)
-        v_woven0 = sb([P, PACK * N], BF16, "v_woven0")
-        weave_items(0, v_woven0[:])
-        v_mx = [mx_tiles("v0")]
-        quantise(v_mx[0], v_woven0[:], E4, 0, N)
-        u_picked = sb([P, 2, B, R], U32, "u_picked")
-        nc.vector.tensor_copy(u_picked[:, 0].rearrange("p b c -> p (b c)"), user_words[0].indirect(user_list[:]))
-        round_table(3)
-        u_mx0 = mx_tiles("u0")
-        for c0 in range(0, R, R // 2):
-            c1 = c0 + R // 2
-            nc.vector.tensor_copy(u_picked[:, 1, 0, c0:c1], user_words[1].indirect(user_list[:, c0 // 16 : c1 // 16]))
-            woven = sb([P, R // 2, 2], U32, "u_woven0_%d" % c0)
-            nc.scalar.copy(woven[:], u_picked[:, :, 0, c0:c1].rearrange("p u c -> p c u"))
-            quantise(u_mx0, as_values(woven), E4, c0, c1)
-        nc.vector.tensor_copy(u_picked[:, 1, 1, :], user_words[1].indirect(entries(user_list, 1)))
-
-
-        vt_mx0 = [half_tiles("vt0_0", "u_woven0_256")]
-        first_pairs = sb([P, B, 2 * N], BF16, "first_pairs", "raw1_1024")
-        behind_users = sb([P, 6 * N], BF16, "behind_users", "raw2_1024")
-        last_pair0, v_woven1 = behind_users[:, 0 : 2 * N], behind_users[:, 2 * N :]
-        weave_items(1, v_woven1)
-        for u, laid in enumerate((first_pairs[:, 0, :], last_pair0)):
-            turn_items(0, u, 4 + u, laid)
-        turn_items(1, 0, 6, first_pairs[:, 1, :])
-
-        clear_window("raw3_1664")
-        model0 = sb([P, PACK, PACK, P], F32, "model0", "raw2_0")
-        target0 = [sb([P, 2, PACK, P], F32, "target0_%d" % half, ("raw3_1024", None)[half]) for half in range(2)]
-        for c in range(2):
-            nc.scalar.activation(*dealt_targets(target0[0][:, c], 0, c), COPY, scale=us_neg[:, c : c + 1])
-        for c in range(2, PACK):
-            nc.scalar.activation(*dealt_targets(target0[1][:, c - 2], 0, c), COPY, scale=us_neg[:, c : c + 1])
-        u_woven1 = weave_users(1)
-        last_pair1 = sb([P, 2 * N], BF16, "last_pair1", "y0_2")
-        turn_items(1, 1, 7, last_pair1[:])
-        v_mx.append(mx_tiles("v1", "u_woven0_0"))
-        quantise(v_mx[1], v_woven1, E4, 0, N)
-        quantise(vt_mx0[0], first_pairs[:, 0, :], E4, 0, 2 * P)
-        score_banks = [score(0, c, u_mx0, c) for c in range(PACK)]
-        h_banks = [bank_tile([P, PACK, P], "h_bank", 4 + c) for c in range(PACK)]
-        h_mx0 = mx_tiles("h0")
-        h0 = [sb([P, rows, PACK], BF16, "h0_%d" % c0) for c0, rows in ((0, 2 * P), (2, 2 * P))]
-        h0_rows = [h0[c // 2][:, c % 2 * P : (c % 2 + 1) * P, :] for c in range(PACK)]
-        ts_places0 = ts_cols[0].unsqueeze(1).to_broadcast([P, P, PACK])
-
-        def model_rows0(c):
-            nc.vector.scalar_tensor_tensor(
-                model0[:, c].rearrange("p t q -> p (t q)"), score_banks[c][:], us_sq[:, c : c + 1], ts_row0, MULT, MULT
-            )
-            for t in range(PACK):
-                turn_onto(h_banks[c][:, t, :], target0[c // 2][:, c % 2, t, :], t == 0, False)
-            for t in range(PACK):
-                turn_onto(h_banks[c][:, t, :], model0[:, c, t, :], False, t == PACK - 1)
-
-        for c in range(PACK):
-            model_rows0(c)
-        u_mx1 = quantise_users(1, u_woven1)
-        for c in range(PACK):
-            nc.vector.tensor_tensor(h0_rows[c], h_banks[c][:].rearrange("p t r -> p r t"), ts_places0, MULT)
-        for part, (c0, c1) in enumerate(((0, 2), (2, 4))):
-            quantise(h_mx0, h0[part][:].rearrange("p r t -> p (r t)"), E5, c0 * P, c1 * P)
-        du0 = [product(0, 0, vt_mx0[0], h_mx0, 4)]
-
-        vt_mx1 = mx_tiles("vt1", "h0_0")
-        for u, laid in enumerate((first_pairs[:, 1, :], last_pair1[:])):
-            quantise(vt_mx1, laid, E4, 2 * P * u, 2 * P * (u + 1))
-        vt_mx0.append(half_tiles("vt0_1", "h0_2"))
-        quantise(vt_mx0[1], last_pair0, E4, 0, 2 * P)
-        model1 = [sb([P, rows, PACK, P], F32, "model1_%d" % c0, tag) for c0, rows, tag in ((0, 1, "y0_2"), (1, 3, "raw2_1024"))]
-        model1_rows = [model1[0][:, 0]] + [model1[1][:, c] for c in range(PACK - 1)]
-        scaled1 = sb([P, PACK - 1, N], F32, "scaled1", "raw1_0")
-        for c in range(PACK):
-            scores = score(1, c, u_mx1, c)
-            row = model1_rows[c].rearrange("p t q -> p (t q)")
-            if c == 0:
-                nc.vector.scalar_tensor_tensor(row, scores[:], us_sq[:, PACK : PACK + 1], ts_row1, MULT, MULT)
+        def scatter(engine, j, r0, r1):
+            dst, src = windows[j][:].indirect(entries(user_list, r0, r1)), du_halves[j // 2][:, j % 2, r0:r1]
+            if engine is nc.vector:
+                nc.vector.tensor_copy(dst, src)
             else:
-                nc.scalar.activation(scaled1[:, c - 1, :], scores[:], COPY, scale=us_sq[:, PACK + c : PACK + c + 1])
-                nc.gpsimd.tensor_tensor(row, scaled1[:, c - 1, :], ts_row1, MULT)
-        du0.extend([product(0, j, vt_mx0[j // 2], h_mx0, 4 + j) for j in (1, 2)])
-        target1 = sb([P, PACK, PACK, P], F32, "target1", "pair1")
-        for c in range(PACK):
-            nc.scalar.activation(*dealt_targets(target1[:, c], 1, c), COPY, scale=us_neg[:, PACK + c : PACK + c + 1])
-        place_banks = [bank_tile([P, PACK, P], "place_bank", bank) for bank in (7, 0, 4, 5)]
-        for t in range(PACK):
-            for c in range(PACK):
-                turn_onto(place_banks[t][:, c, :], target1[:, c, t, :], c == 0, False)
-        for c in range(PACK):
-            for t in range(PACK):
-                turn_onto(place_banks[t][:, c, :], model1_rows[c][:, t, :], False, c == PACK - 1)
-        h1 = sb([P, R, PACK], BF16, "h1", "ts_table")
-        places1 = sb([P, PACK, R], BF16, "places1")
-        for t in range(PACK):
-            nc.scalar.activation(places1[:, t, :], place_banks[t][:].rearrange("p c r -> p (c r)"), COPY, scale=ts_cols[1][:, t : t + 1])
-        nc.scalar.copy(h1[:], places1[:].rearrange("p t r -> p r t"))
-        h_mx1 = mx_tiles("h1")
-        quantise(h_mx1, h1[:].rearrange("p r t -> p (r t)"), E5, 0, R)
-        du0.append(product(0, PACK - 1, vt_mx0[1], h_mx0, 6, "places1"))
+                nc.scalar.activation(dst, src, COPY)
 
-        nc.vector.tensor_copy(windows[0][:].indirect(entries(user_list, 0)), du0[0][:])
-        clear_window("raw2_1024")
-        for j in range(1, PACK):
-            nc.vector.tensor_copy(windows[j][:].indirect(entries(user_list, 0)), du0[j][:])
-        du1 = [product(1, j, vt_mx1, h_mx1, 1 + j % 2, tag) for j, tag in enumerate(("ts_picked", "pair2", "raw3_0", "v_picked"))]
-        for j in range(PACK):
-            nc.vector.tensor_copy(windows[j][:].indirect(entries(user_list, 1)), du1[j][:])
-            nc.sync.dma_start(out.rearrange("(m j) c -> m j c", j=PACK)[:, j, :], windows[j][:])
+        def scatter_unit(j, k):
+            scatter(nc.scalar, j, k * UNIT, (k + 1) * UNIT)
+
+        def store(queue, j):
+            queue.dma_start(out.rearrange("(m j) c -> m j c", j=PACK)[:, j, :], windows[j][:])
+
+        u_mx0 = quantise_users(0, first_woven)
+        scores0 = score(0, u_mx0)
+        scale_targets(0)
+        turn_targets(0)
+        laid3 = sb([P, B * N], BF16, "v_laid3", "y0")
+        turn_items(3, 3, laid3[:])
+        u_mx1 = quantise_users(1, weave_users(1, None))
+        for c in range(BLOCKS):
+            model_block(0, c, scores0)
+        scores1 = score(1, u_mx1)
+        scale_targets(1)
+        turn_targets(1)
+        woven2 = weave_users(2, "u0_codes")
+        quantise_turned("vt3", laid3, 1, None)
+        h0 = finish_h(0)
+        model_block(1, 0, scores1)
+        sums0 = products(0, h0)
+        model_block(1, 1, scores1)
+        u_mx2 = quantise_users(2, woven2)
+        scores2 = score(2, u_mx2)
+        scale_targets(2)
+        scale_targets(3)
+        copy_out(nc.scalar, 0, 0, sums0)
+        copy_out(nc.scalar, 0, 1, sums0)
+        turn_targets(2)
+        woven3 = weave_users(3, "model1")
+        h1 = finish_h(1)
+        u_mx3 = quantise_users(3, woven3)
+        sums1 = products(1, h1)
+        scores3 = score(3, u_mx3)
+        scatter_unit(0, 0)
+        copy_out(nc.scalar, 1, 0, sums1)
+        copy_out(nc.scalar, 1, 1, sums1)
+        for c in range(BLOCKS):
+            model_block(2, c, scores2)
+        turn_targets(3)
+        for c in range(BLOCKS):
+            model_block(3, c, scores3)
+        sums2 = products(2, finish_h(2))
+        scatter_unit(0, 1)
+        scatter_unit(1, 1)
+        copy_out(nc.scalar, 2, 0, sums2)
+        scatter_unit(0, 2)
+        h3 = finish_h(3)
+        copy_out(nc.vector, 2, 1, sums2)
+        sums3 = products(3, h3)
+        copy_out(nc.scalar, 3, 0, sums3)
+        copy_out(nc.scalar, 3, 1, sums3)
+        scatter_unit(0, 3)
+        store(nc.sync, 0)
+        scatter(nc.vector, 2, 0, 3 * UNIT)
+        scatter(nc.vector, 2, 3 * UNIT, 4 * UNIT)
+        store(nc.sync, 2)
+        for k in (3, 0, 2):
+            scatter_unit(1, k)
+        store(nc.scalar, 1)
+        scatter(nc.vector, 3, 0, B * R)
+        store(nc.sync, 3)

@@ -24,6 +24,7 @@ UNIT = 256
 UNITS = B * R // UNIT
 BLOCKS = UNIT // P
 ALIGN = 256
+H_BANKS = (4, 6, 4, 0)
 
 
 def tile_attend_gmf_sq_u_kernel(tc, uT, vT, y, us, ts, offs, uoffs, out):
@@ -72,24 +73,22 @@ def tile_attend_gmf_sq_u_kernel(tc, uT, vT, y, us, ts, offs, uoffs, out):
         nc.sync.dma_start(user_list[:], uoffs)
         v_planes.extend([load_plane(vT, j, "v%d" % j) for j in (2, 3)])
         u_planes = [load_plane(uT, j, "u%d" % j) for j in range(PACK)]
-        y_units = []
-        for k in range(UNITS):
-            rows_in = sb([P, BLOCKS, N], F32, "y%d" % k)
-            nc.sync.dma_start(rows_in[:], y.rearrange("b (c p) i -> p (b c) i", p=P)[:, k * BLOCKS : (k + 1) * BLOCKS, :])
-            y_units.append(rows_in)
+        y_blocks = []
+        for c0, c1 in ((0, 1), (1, 2), (2, 4), (4, 6), (6, 8)):
+            rows_in = sb([P, c1 - c0, N], F32, "y%d" % c0)
+            nc.sync.dma_start(rows_in[:], y.rearrange("b (c p) i -> p (b c) i", p=P)[:, c0:c1, :])
+            y_blocks.extend([rows_in[:, c, :] for c in range(c1 - c0)])
 
         ident = sb([P, P], F32, "ident")
         make_identity(nc, ident[:])
         windows = []
 
-        def clear_window(tag):
+        def clear_window(engine, pieces, tag):
             window = sb([P, TU], F32, "window%d" % len(windows), tag)
-            for c0 in range(0, TU, TU // 4):
-                nc.gpsimd.memset(window[:, c0 : c0 + TU // 4], 0.0)
+            for c0 in range(0, TU, TU // pieces):
+                engine.memset(window[:, c0 : c0 + TU // pieces], 0.0)
             windows.append(window)
 
-        clear_window(None)
-        clear_window(None)
 
         ts_table = sb([P, T], F32, "ts_table")
         us_rows = sb([P, P], F32, "us_rows")
@@ -98,87 +97,111 @@ def tile_attend_gmf_sq_u_kernel(tc, uT, vT, y, us, ts, offs, uoffs, out):
         nc.scalar.activation(us_rows[0 : B * PACK, :], us_first[:], COPY)
         nc.vector.tensor_copy(ts_table[0:1, :], ts_first[:])
         ts_picked = sb([P, B, N], F32, "ts_picked")
-        gather(nc.vector, ts_picked[:].rearrange("p b i -> p (b i)"), ts_table, item_list[:])
+        ts_dealt = ts_picked[:].bitcast(U32).rearrange("p b (t q) -> p b q t", t=PACK)
+        nc.vector.tensor_copy(ts_dealt, ts_table[:].bitcast(U32).indirect(item_list[:]))
 
-        v_picked = sb([P, PACK * B * N], BF16, "v_picked")
+        clear_window(nc.gpsimd, 4, "ts_first")
+
+        v_rounded = sb([P, PACK * B * N], BF16, "v_rounded")
+        v_picked = [sb([P, B * N], F32, "v_picked%d" % j) for j in range(PACK)]
         vt_mx = []
 
-        def item_plane(j):
-            return v_picked[:, j * B * N : (j + 1) * B * N]
+        def pick_items(engine, j, i0, i1):
+            gather(engine, v_picked[j][:, i0:i1], v_planes[j], entries(item_list, i0, i1))
+
+        def round_items(engine, j, i0, i1):
+            plane = v_rounded[:, j * B * N + i0 : j * B * N + i1]
+            dst = plane.rearrange("p (b u q e) -> p b q u e", u=2, q=P, e=2)
+            src = v_picked[j][:, i0:i1].rearrange("p (b q u e) -> p b q u e", u=2, q=P, e=2)
+            if engine is nc.vector:
+                nc.vector.tensor_copy(dst, src)
+            else:
+                nc.scalar.copy(dst, src)
 
         def turn_items(j, bank, laid):
-            words = item_plane(j).bitcast(F32)
+            words = v_rounded[:, j * B * N : (j + 1) * B * N].bitcast(F32)
             turned = bank_tile([P, B, 2, P], "v_bank", bank)
             for b in range(B):
                 for u in range(2):
-                    nc.tensor.transpose(turned[:, b, u, :], words[:, b * 2 * P + u : (b + 1) * 2 * P : 2], ident[:])
+                    nc.tensor.transpose(turned[:, b, u, :], words[:, (2 * b + u) * P : (2 * b + u + 1) * P], ident[:])
             nc.scalar.copy(laid.bitcast(F32).rearrange("p (b m u) -> p b m u", b=B, u=2), turned[:].rearrange("p b u m -> p b m u"))
 
-        def quantise_turned(name, laid, planes, tag):
-            mx = mx_tiles(name, planes * B * P, tag)
+        def quantise_turned(name, laid, tag):
+            mx = mx_tiles(name, 2 * B * P, tag)
             quantise(mx, laid[:], E4)
-            vt_mx.extend([(mx, s * B * P) for s in range(planes)])
+            vt_mx.extend([(mx, s * B * P) for s in range(2)])
 
-        gather(nc.scalar, item_plane(0), v_planes[0], item_list[:])
-        clear_window("v0")
-        gather(nc.vector, item_plane(1), v_planes[1], item_list[:])
-        clear_window("v1")
-        laid01 = sb([P, 2 * B * N], BF16, "v_laid01")
-        turn_items(0, 0, laid01[:, 0 : B * N])
-
+        pick_items(nc.scalar, 0, 0, B * N)
+        pick_items(nc.vector, 1, 0, B * N)
+        clear_window(nc.gpsimd, 4, "v0")
         ts_cols = sb([P, B, PACK], F32, "ts_cols")
-        ts_rows = sb([P, B, N], F32, "ts_rows")
+        ts_spread = []
         for b in range(B):
             turned = bank_tile([P, PACK, P], "ts_turned", 4 + b)
             for t in range(PACK):
-                nc.tensor.transpose(turned[:, t, :], ts_picked[:, b, t::PACK], ident[:])
+                nc.tensor.transpose(turned[:, t, :], ts_picked[:, b, t * P : (t + 1) * P], ident[:])
             nc.scalar.copy(ts_cols[:, b, :], turned[:, :, 0])
+        for b in range(B):
             spread = bank_tile([P, PACK, P], "ts_spread", 6 + b)
             for t in range(PACK):
                 nc.tensor.transpose(spread[:, t, :], ts_cols[:, b, t : t + 1].to_broadcast([P, P]), ident[:])
-            nc.scalar.copy(ts_rows[:, b, :], spread[:].rearrange("p t q -> p (t q)"))
+            ts_spread.append(spread)
+        round_items(nc.scalar, 0, 0, B * N)
+        ts_rows = []
 
-        def pick_items_by_group(j):
-            for b, engine in enumerate((nc.vector, nc.scalar)):
-                gather(engine, item_plane(j)[:, b * N : (b + 1) * N], v_planes[j], entries(item_list, b * N, (b + 1) * N))
+        def copy_ts_row(b, tag):
+            row = sb([P, N], F32, "ts_row%d" % b, tag)
+            nc.scalar.copy(row[:], ts_spread[b][:].rearrange("p t q -> p (t q)"))
+            ts_rows.append(row)
 
-        turn_items(1, 1, laid01[:, B * N :])
-        gather(nc.vector, item_plane(2), v_planes[2], item_list[:])
-        quantise_turned("vt01", laid01, 2, "v2")
+        copy_ts_row(0, None)
+        round_items(nc.vector, 1, 0, B * N)
         us_bank = bank_tile([P, P], "us_bank", 4)
         nc.tensor.transpose(us_bank[:], us_rows[:], ident[:])
         us_neg = sb([P, B * PACK], F32, "us_neg")
         us_sq = sb([P, B * PACK], F32, "us_sq")
         nc.scalar.activation(us_neg[:], us_bank[:, 0 : B * PACK], COPY, scale=-1.0)
         nc.scalar.activation(us_sq[:], us_bank[:, 0 : B * PACK], SQUARE)
-        pick_items_by_group(3)
-        laid2 = sb([P, B * N], BF16, "v_laid2", "v3")
-        turn_items(2, 2, laid2[:])
+        pick_items(nc.vector, 2, 0, N)
+        pick_items(nc.scalar, 2, N, B * N)
+        round_items(nc.vector, 2, 0, B * N)
+        laid01 = sb([P, 2 * B * N], BF16, "v_laid01", "v2")
+        for j in range(2):
+            turn_items(j, j, laid01[:, j * B * N : (j + 1) * B * N])
+        pick_items(nc.vector, 3, 0, N)
+        pick_items(nc.scalar, 3, N, B * N)
+        round_items(nc.vector, 3, 0, N)
         v_mx = []
         for b in range(B):
             woven = sb([P, N * PACK], BF16, "v_woven%d" % b)
-            planes = v_picked[:].rearrange("p (j b q t) -> p b t q j", j=PACK, b=B, t=PACK)[:, b]
-            nc.vector.tensor_copy(woven[:].rearrange("p (t q j) -> p t q j", t=PACK, j=PACK), planes)
+            planes = v_rounded[:].rearrange("p (j b u q e) -> p b u e q j", j=PACK, b=B, u=2, e=2)[:, b]
+            nc.vector.tensor_copy(woven[:].rearrange("p (u e q j) -> p u e q j", u=2, e=2, j=PACK), planes)
             if b == 0:
-                quantise_turned("vt2", laid2, 1, None)
+                round_items(nc.vector, 3, N, B * N)
+            else:
+                quantise_turned("vt01", laid01, "v_woven0")
             v_mx.append(mx_tiles("v%d" % b, N))
             quantise(v_mx[b], woven[:], E4)
 
-        u_picked = sb([P, PACK * B * R], BF16, "u_picked")
+        u_picked = sb([P, PACK * B * R], F32, "u_picked")
         u_by_plane = u_picked[:].rearrange("p (j r) -> p j r", j=PACK)
 
         def pick_users(engine, j, r0, r1):
             gather(engine, u_picked[:, j * B * R + r0 : j * B * R + r1], u_planes[j], entries(user_list, r0, r1))
 
         pick_users(nc.scalar, 0, 0, B * R)
+        laid23 = sb([P, 2 * B * N], BF16, "v_laid23", "u0")
+        for j in range(2):
+            turn_items(2 + j, 2 + j, laid23[:, j * B * N : (j + 1) * B * N])
+        quantise_turned("vt23", laid23, "v_woven1")
         pick_users(nc.scalar, 1, 0, B * R)
-        pick_users(nc.vector, 2, 0, R)
-        pick_users(nc.scalar, 2, R, B * R)
+        pick_users(nc.vector, 2, 0, UNIT)
+        pick_users(nc.scalar, 2, UNIT, B * R)
         first_woven = sb([P, UNIT, PACK], BF16, "u_woven0")
         nc.vector.tensor_copy(first_woven[:, :, 0:3], u_by_plane[:, 0:3, 0:UNIT].rearrange("p j r -> p r j"))
         gather(nc.vector, first_woven[:, :, 3], u_planes[3], entries(user_list, 0, UNIT))
         pick_users(nc.scalar, 3, UNIT, R)
-        pick_users(nc.scalar, 3, R, B * R)
+        pick_users(nc.scalar, 3, 2 * UNIT, 3 * UNIT)
 
         def weave_users(k, tag):
             woven = sb([P, UNIT, PACK], BF16, "u_woven%d" % k, tag)
@@ -190,20 +213,20 @@ def tile_attend_gmf_sq_u_kernel(tc, uT, vT, y, us, ts, offs, uoffs, out):
             quantise(mx, woven[:].rearrange("p r j -> p (r j)"), E4)
             return mx
 
-        targets = [sb([P, PACK, PACK, P], F32, "target%d" % b, "u%d" % b) for b in range(B)]
+        targets = [sb([P, PACK, PACK, P], F32, "target%d" % b, ("v_rounded", "u1")[b]) for b in range(B)]
         h_banks = {}
 
         def scale_targets(k):
             for c in range(BLOCKS):
                 block = k * BLOCKS + c
                 target = targets[block // PACK][:, block % PACK]
-                rows_in = y_units[k][:, c, :].rearrange("p (q t) -> p q t", t=PACK)
+                rows_in = y_blocks[block].rearrange("p (q t) -> p q t", t=PACK)
                 nc.scalar.activation(target.rearrange("p t q -> p q t"), rows_in, COPY, scale=us_neg[:, block : block + 1])
 
         def turn_targets(k):
             for c in range(BLOCKS):
                 block = k * BLOCKS + c
-                h_banks[block] = bank_tile([P, PACK, P], "h_bank", 4 + block % PACK)
+                h_banks[block] = bank_tile([P, PACK, P], "h_bank", H_BANKS[k] + c)
                 for t in range(PACK):
                     turn_onto(h_banks[block][:, t, :], targets[block // PACK][:, block % PACK, t, :], t == 0, False)
 
@@ -223,7 +246,7 @@ def tile_attend_gmf_sq_u_kernel(tc, uT, vT, y, us, ts, offs, uoffs, out):
         def model_block(k, c, scores):
             block = k * BLOCKS + c
             model = sb([P, N], F32, "model%d" % block)
-            nc.vector.scalar_tensor_tensor(model[:], scores[c][:], us_sq[:, block : block + 1], ts_rows[:, block // PACK, :], MULT, MULT)
+            nc.vector.scalar_tensor_tensor(model[:], scores[c][:], us_sq[:, block : block + 1], ts_rows[block // PACK][:], MULT, MULT)
             for t in range(PACK):
                 turn_onto(h_banks[block][:, t, :], model[:, t * P : (t + 1) * P], False, t == PACK - 1)
 
@@ -234,14 +257,14 @@ def tile_attend_gmf_sq_u_kernel(tc, uT, vT, y, us, ts, offs, uoffs, out):
                 nc.vector.tensor_tensor(h[:, c * P : (c + 1) * P, :], h_banks[k * BLOCKS + c][:].rearrange("p t r -> p r t"), places, MULT)
             return h
 
-        du_halves = [sb([P, 2, B * R], F32, "du%d" % half, ("ts_first", "ts_table")[half]) for half in range(2)]
+        du_halves = [sb([P, 2, B * R], F32, "du%d" % half, ("v2", "v3")[half]) for half in range(2)]
 
         def products(k, h):
             h_mx = mx_tiles("h%d" % k, UNIT)
             quantise(h_mx, h[:].rearrange("p r t -> p (r t)"), E5)
             banks = []
             for half in range(2):
-                sums = bank_tile([P, 2, UNIT], "du_bank", 4 + (k * BLOCKS + half) % PACK)
+                sums = bank_tile([P, 2, UNIT], "du_bank", H_BANKS[k] + half)
                 for s in range(2):
                     vt, first = vt_mx[2 * half + s]
                     cols = slice(first + k * UNIT // R * P, first + (k * UNIT // R + 1) * P)
@@ -276,8 +299,8 @@ def tile_attend_gmf_sq_u_kernel(tc, uT, vT, y, us, ts, offs, uoffs, out):
         scores0 = score(0, u_mx0)
         scale_targets(0)
         turn_targets(0)
-        laid3 = sb([P, B * N], BF16, "v_laid3", "y0")
-        turn_items(3, 3, laid3[:])
+        copy_ts_row(1, "y0")
+        pick_users(nc.scalar, 3, 3 * UNIT, 4 * UNIT)
         u_mx1 = quantise_users(1, weave_users(1, None))
         for c in range(BLOCKS):
             model_block(0, c, scores0)
@@ -285,7 +308,6 @@ def tile_attend_gmf_sq_u_kernel(tc, uT, vT, y, us, ts, offs, uoffs, out):
         scale_targets(1)
         turn_targets(1)
         woven2 = weave_users(2, "u0_codes")
-        quantise_turned("vt3", laid3, 1, None)
         h0 = finish_h(0)
         model_block(1, 0, scores1)
         sums0 = products(0, h0)
@@ -301,6 +323,7 @@ def tile_attend_gmf_sq_u_kernel(tc, uT, vT, y, us, ts, offs, uoffs, out):
         h1 = finish_h(1)
         u_mx3 = quantise_users(3, woven3)
         sums1 = products(1, h1)
+        clear_window(nc.gpsimd, 4, "h1")
         scores3 = score(3, u_mx3)
         scatter_unit(0, 0)
         copy_out(nc.scalar, 1, 0, sums1)
@@ -318,6 +341,7 @@ def tile_attend_gmf_sq_u_kernel(tc, uT, vT, y, us, ts, offs, uoffs, out):
         h3 = finish_h(3)
         copy_out(nc.vector, 2, 1, sums2)
         sums3 = products(3, h3)
+        clear_window(nc.gpsimd, 4, "h3")
         copy_out(nc.scalar, 3, 0, sums3)
         copy_out(nc.scalar, 3, 1, sums3)
         scatter_unit(0, 3)

@@ -25,6 +25,10 @@ UNITS = B * R // UNIT
 BLOCKS = UNIT // P
 ALIGN = 256
 H_BANKS = (4, 6, 4, 0)
+LOADS = (
+    ((0, 512, 0), (512, 1024, 0), (1024, 1408, 0), (1408, 2048, 640)),
+    ((0, 1024, 384), (1024, 1664, 640), (1664, 2048, 384)),
+)
 
 
 def tile_attend_gmf_sq_u_kernel(tc, uT, vT, y, us, ts, offs, uoffs, out):
@@ -53,6 +57,32 @@ def tile_attend_gmf_sq_u_kernel(tc, uT, vT, y, us, ts, offs, uoffs, out):
             else:
                 nc.scalar.activation(dst, plane[:].indirect(offsets), COPY)
 
+        def copy(engine, dst, src):
+            if engine is nc.vector:
+                nc.vector.tensor_copy(dst, src)
+            else:
+                nc.scalar.copy(dst, src)
+
+        def load_pair(n, table, u):
+            planes = table.rearrange("(p t) c -> p t c", t=PACK)[:, 2 * u : 2 * u + 2, :]
+            pieces = []
+            for c0, c1, share in LOADS[n]:
+                raw = sb([P, 2, c1 - c0], F32, "raw%d_%d" % (n, c0))
+                nc.sync.dma_start(raw[:], planes[:, :, c0:c1])
+                pieces.append((c0, c1, share, raw))
+            return pieces
+
+        def round_pair(n):
+            pair = sb([P, T, 2], BF16, "pair%d" % n)
+            for c0, c1, share, raw in loaded[n]:
+                cut = c1 - c0 - share
+                side_by_side = raw[:].rearrange("p e c -> p c e")
+                if cut:
+                    nc.scalar.activation(pair[:, c0 : c0 + cut, :], side_by_side[:, 0:cut, :], COPY)
+                if share:
+                    nc.vector.tensor_copy(pair[:, c0 + cut : c1, :], side_by_side[:, cut:, :])
+            return pair[:].rearrange("p c e -> p (c e)").bitcast(U32)
+
         def mx_tiles(name, width, tag=None):
             return sb([P, width], U32, name + "_codes", tag), sb([P, width], U8, name + "_scales")
 
@@ -69,9 +99,9 @@ def tile_attend_gmf_sq_u_kernel(tc, uT, vT, y, us, ts, offs, uoffs, out):
         nc.sync.dma_start(item_list[:], offs)
         nc.sync.dma_start(us_first[:], us.rearrange("b (c p) o -> (b c) (p o)", p=P))
         nc.sync.dma_start(ts_first[:], ts[0:1, :])
-        v_planes = [load_plane(vT, j, "v%d" % j) for j in (0, 1)]
+        loaded = [load_pair(0, vT, 0)]
         nc.sync.dma_start(user_list[:], uoffs)
-        v_planes.extend([load_plane(vT, j, "v%d" % j) for j in (2, 3)])
+        loaded.append(load_pair(1, vT, 1))
         u_planes = [load_plane(uT, j, "u%d" % j) for j in range(PACK)]
         y_blocks = []
         for c0, c1 in ((0, 1), (1, 2), (2, 4), (4, 6), (6, 8)):
@@ -96,130 +126,120 @@ def tile_attend_gmf_sq_u_kernel(tc, uT, vT, y, us, ts, offs, uoffs, out):
         nc.vector.memset(ts_table[:].bitcast(I32), 0)
         nc.scalar.activation(us_rows[0 : B * PACK, :], us_first[:], COPY)
         nc.vector.tensor_copy(ts_table[0:1, :], ts_first[:])
-        ts_picked = sb([P, B, N], F32, "ts_picked")
-        ts_dealt = ts_picked[:].bitcast(U32).rearrange("p b (t q) -> p b q t", t=PACK)
-        nc.vector.tensor_copy(ts_dealt, ts_table[:].bitcast(U32).indirect(item_list[:]))
-
-        clear_window(nc.gpsimd, 4, "ts_first")
-
-        v_rounded = sb([P, PACK * B * N], BF16, "v_rounded")
-        v_picked = [sb([P, B * N], F32, "v_picked%d" % j) for j in range(PACK)]
-        vt_mx = []
-
-        def pick_items(engine, j, i0, i1):
-            gather(engine, v_picked[j][:, i0:i1], v_planes[j], entries(item_list, i0, i1))
-
-        def round_items(engine, j, i0, i1):
-            plane = v_rounded[:, j * B * N + i0 : j * B * N + i1]
-            dst = plane.rearrange("p (b u q e) -> p b q u e", u=2, q=P, e=2)
-            src = v_picked[j][:, i0:i1].rearrange("p (b q u e) -> p b q u e", u=2, q=P, e=2)
-            if engine is nc.vector:
-                nc.vector.tensor_copy(dst, src)
-            else:
-                nc.scalar.copy(dst, src)
-
-        def turn_items(j, bank, laid):
-            words = v_rounded[:, j * B * N : (j + 1) * B * N].bitcast(F32)
-            turned = bank_tile([P, B, 2, P], "v_bank", bank)
-            for b in range(B):
-                for u in range(2):
-                    nc.tensor.transpose(turned[:, b, u, :], words[:, (2 * b + u) * P : (2 * b + u + 1) * P], ident[:])
-            nc.scalar.copy(laid.bitcast(F32).rearrange("p (b m u) -> p b m u", b=B, u=2), turned[:].rearrange("p b u m -> p b m u"))
-
-        def quantise_turned(name, laid, tag):
-            mx = mx_tiles(name, 2 * B * P, tag)
-            quantise(mx, laid[:], E4)
-            vt_mx.extend([(mx, s * B * P) for s in range(2)])
-
-        pick_items(nc.scalar, 0, 0, B * N)
-        pick_items(nc.vector, 1, 0, B * N)
-        clear_window(nc.gpsimd, 4, "v0")
-        ts_cols = sb([P, B, PACK], F32, "ts_cols")
-        ts_spread = []
-        for b in range(B):
-            turned = bank_tile([P, PACK, P], "ts_turned", 4 + b)
-            for t in range(PACK):
-                nc.tensor.transpose(turned[:, t, :], ts_picked[:, b, t * P : (t + 1) * P], ident[:])
-            nc.scalar.copy(ts_cols[:, b, :], turned[:, :, 0])
-        for b in range(B):
-            spread = bank_tile([P, PACK, P], "ts_spread", 6 + b)
-            for t in range(PACK):
-                nc.tensor.transpose(spread[:, t, :], ts_cols[:, b, t : t + 1].to_broadcast([P, P]), ident[:])
-            ts_spread.append(spread)
-        round_items(nc.scalar, 0, 0, B * N)
-        ts_rows = []
-
-        def copy_ts_row(b, tag):
-            row = sb([P, N], F32, "ts_row%d" % b, tag)
-            nc.scalar.copy(row[:], ts_spread[b][:].rearrange("p t q -> p (t q)"))
-            ts_rows.append(row)
-
-        copy_ts_row(0, None)
-        round_items(nc.vector, 1, 0, B * N)
-        us_bank = bank_tile([P, P], "us_bank", 4)
+        us_bank = bank_tile([P, P], "us_bank", 3)
         nc.tensor.transpose(us_bank[:], us_rows[:], ident[:])
         us_neg = sb([P, B * PACK], F32, "us_neg")
         us_sq = sb([P, B * PACK], F32, "us_sq")
         nc.scalar.activation(us_neg[:], us_bank[:, 0 : B * PACK], COPY, scale=-1.0)
         nc.scalar.activation(us_sq[:], us_bank[:, 0 : B * PACK], SQUARE)
-        pick_items(nc.vector, 2, 0, N)
-        pick_items(nc.scalar, 2, N, B * N)
-        round_items(nc.vector, 2, 0, B * N)
-        laid01 = sb([P, 2 * B * N], BF16, "v_laid01", "v2")
-        for j in range(2):
-            turn_items(j, j, laid01[:, j * B * N : (j + 1) * B * N])
-        pick_items(nc.vector, 3, 0, N)
-        pick_items(nc.scalar, 3, N, B * N)
-        round_items(nc.vector, 3, 0, N)
-        v_mx = []
+        ts_picked = sb([P, B, N], F32, "ts_picked")
         for b in range(B):
-            woven = sb([P, N * PACK], BF16, "v_woven%d" % b)
-            planes = v_rounded[:].rearrange("p (j b u q e) -> p b u e q j", j=PACK, b=B, u=2, e=2)[:, b]
-            nc.vector.tensor_copy(woven[:].rearrange("p (u e q j) -> p u e q j", u=2, e=2, j=PACK), planes)
-            if b == 0:
-                round_items(nc.vector, 3, N, B * N)
-            else:
-                quantise_turned("vt01", laid01, "v_woven0")
-            v_mx.append(mx_tiles("v%d" % b, N))
-            quantise(v_mx[b], woven[:], E4)
+            ts_dealt = ts_picked[:, b, :].bitcast(U32).rearrange("p (t q) -> p q t", t=PACK)
+            nc.vector.tensor_copy(ts_dealt, ts_table[:].bitcast(U32).indirect(entries(item_list, b * N, (b + 1) * N)))
 
-        u_picked = sb([P, PACK * B * R], F32, "u_picked")
-        u_by_plane = u_picked[:].rearrange("p (j r) -> p j r", j=PACK)
+        clear_window(nc.gpsimd, 2, "ts_first")
+
+        v_picked = sb([P, 2, B, N], U32, "v_picked")
+
+        def pick_items(u, words):
+            nc.vector.tensor_copy(v_picked[:, u].rearrange("p b (t q) -> p b q t", t=PACK), words.indirect(item_list[:]))
+
+        def turn_items(engine, b, u, bank, laid):
+            words = v_picked[:, u, b, :].bitcast(F32)
+            turned = bank_tile([P, PACK, P], "v_bank", bank)
+            for t in range(PACK):
+                nc.tensor.transpose(turned[:, t, :], words[:, t * P : (t + 1) * P], ident[:])
+            halves = turned[:].rearrange("p t m -> p (t m)").bitcast(BF16)
+            copy(engine, laid.rearrange("p (e m t) -> p e m t", t=PACK, e=2), halves.rearrange("p (t m e) -> p e m t", t=PACK, e=2))
+
+        vt_mx = {}
+
+        def quantise_turned(b, u, laid, tag):
+            vt_mx[b, u] = mx_tiles("vt%d_%d" % (b, u), 2 * P, tag)
+            quantise(vt_mx[b, u], laid, E4)
+
+        def weave(engine, name, tag, picked):
+            width = picked.shape[2]
+            woven = sb([P, width, 2], U32, name, tag)
+            if engine is nc.vector:
+                nc.vector.tensor_copy(woven[:].bitcast(I32), picked.rearrange("p u c -> p c u").bitcast(I32))
+            else:
+                nc.scalar.copy(woven[:], picked.rearrange("p u c -> p c u"))
+            return woven
+
+        def quantise_woven(name, woven):
+            mx = mx_tiles(name, woven.shape[1])
+            quantise(mx, woven[:].rearrange("p c u -> p (c u)").bitcast(BF16), E4)
+            return mx
+
+        pick_items(0, round_pair(0))
+        clear_window(nc.gpsimd, 2, "raw0_1408")
+        ts_cols = [sb([P, PACK], F32, "ts_cols0")]
+        ts_held = sb([P, B * N + 8], F32, "ts_held", "raw0_1024")
+        ts_cols.append(ts_held[:, B * N : B * N + PACK])
+        ts_rows = [ts_held[:, b * N : (b + 1) * N] for b in range(B)]
+        for b in range(B):
+            turned = bank_tile([P, PACK, P], "ts_turned", 4 + b)
+            for t in range(PACK):
+                nc.tensor.transpose(turned[:, t, :], ts_picked[:, b, t * P : (t + 1) * P], ident[:])
+            if b == 0:
+                nc.vector.tensor_copy(ts_cols[0][:], turned[:, :, 0])
+            else:
+                nc.scalar.copy(ts_cols[1], turned[:, :, 0])
+        for b in range(B):
+            spread = bank_tile([P, PACK, P], "ts_spread", 6 + b)
+            for t in range(PACK):
+                nc.tensor.transpose(spread[:, t, :], ts_cols[b][:, t : t + 1].to_broadcast([P, P]), ident[:])
+            nc.scalar.copy(ts_rows[b], spread[:].rearrange("p t q -> p (t q)"))
+        last_words = round_pair(1)
+        first_laid = sb([P, B, 2 * N], BF16, "first_laid", "raw1_0")
+        for b in range(B):
+            turn_items(nc.scalar, b, 0, b, first_laid[:, b, :])
+        pick_items(1, last_words)
+        v_woven0 = weave(nc.vector, "v_woven0", None, v_picked[:, :, 0, :])
+        quantise_turned(0, 0, first_laid[:, 0, :], "pair1")
+        v_mx = [quantise_woven("v0", v_woven0)]
+
+        u_picked0 = sb([P, PACK, R], F32, "u_picked0")
+        u_picked1 = [sb([P, 2, R], F32, "u_picked1_0")]
 
         def pick_users(engine, j, r0, r1):
-            gather(engine, u_picked[:, j * B * R + r0 : j * B * R + r1], u_planes[j], entries(user_list, r0, r1))
+            dst = u_picked0[:, j, r0:r1] if r0 < R else u_picked1[j // 2][:, j % 2, r0 - R : r1 - R]
+            gather(engine, dst, u_planes[j], entries(user_list, r0, r1))
 
-        pick_users(nc.scalar, 0, 0, B * R)
-        laid23 = sb([P, 2 * B * N], BF16, "v_laid23", "u0")
-        for j in range(2):
-            turn_items(2 + j, 2 + j, laid23[:, j * B * N : (j + 1) * B * N])
-        quantise_turned("vt23", laid23, "v_woven1")
-        pick_users(nc.scalar, 1, 0, B * R)
+        pick_users(nc.scalar, 0, 0, R)
+        pick_users(nc.scalar, 0, R, B * R)
+        v_woven1 = weave(nc.vector, "v_woven1", None, v_picked[:, :, 1, :])
+        quantise_turned(1, 0, first_laid[:, 1, :], "v_woven0")
+        v_mx.append(quantise_woven("v1", v_woven1))
+        laid01 = sb([P, 2 * N], BF16, "laid01")
+        turn_items(nc.vector, 0, 1, 2, laid01[:])
+        pick_users(nc.scalar, 1, 0, R)
+        pick_users(nc.scalar, 1, R, B * R)
         pick_users(nc.vector, 2, 0, UNIT)
-        pick_users(nc.scalar, 2, UNIT, B * R)
+        pick_users(nc.scalar, 2, UNIT, R)
+        quantise_turned(0, 1, laid01[:], None)
         first_woven = sb([P, UNIT, PACK], BF16, "u_woven0")
-        nc.vector.tensor_copy(first_woven[:, :, 0:3], u_by_plane[:, 0:3, 0:UNIT].rearrange("p j r -> p r j"))
+        nc.vector.tensor_copy(first_woven[:, :, 0:3], u_picked0[:, 0:3, 0:UNIT].rearrange("p j r -> p r j"))
         gather(nc.vector, first_woven[:, :, 3], u_planes[3], entries(user_list, 0, UNIT))
         pick_users(nc.scalar, 3, UNIT, R)
-        pick_users(nc.scalar, 3, 2 * UNIT, 3 * UNIT)
 
-        def weave_users(k, tag):
-            woven = sb([P, UNIT, PACK], BF16, "u_woven%d" % k, tag)
-            nc.vector.tensor_copy(woven[:], u_by_plane[:, :, k * UNIT : (k + 1) * UNIT].rearrange("p j r -> p r j"))
-            return woven
+        def weave_users(woven, picked):
+            nc.vector.tensor_copy(woven, picked.rearrange("p j r -> p r j"))
 
         def quantise_users(k, woven):
             mx = mx_tiles("u%d" % k, UNIT)
-            quantise(mx, woven[:].rearrange("p r j -> p (r j)"), E4)
+            quantise(mx, woven.rearrange("p r j -> p (r j)"), E4)
             return mx
 
-        targets = [sb([P, PACK, PACK, P], F32, "target%d" % b, ("v_rounded", "u1")[b]) for b in range(B)]
+        targets = {}
         h_banks = {}
 
-        def scale_targets(k):
+        def scale_targets(k, tag):
+            targets[k] = sb([P, BLOCKS, PACK, P], F32, "target%d" % k, tag)
             for c in range(BLOCKS):
                 block = k * BLOCKS + c
-                target = targets[block // PACK][:, block % PACK]
+                target = targets[k][:, c]
                 rows_in = y_blocks[block].rearrange("p (q t) -> p q t", t=PACK)
                 nc.scalar.activation(target.rearrange("p t q -> p q t"), rows_in, COPY, scale=us_neg[:, block : block + 1])
 
@@ -228,7 +248,7 @@ def tile_attend_gmf_sq_u_kernel(tc, uT, vT, y, us, ts, offs, uoffs, out):
                 block = k * BLOCKS + c
                 h_banks[block] = bank_tile([P, PACK, P], "h_bank", H_BANKS[k] + c)
                 for t in range(PACK):
-                    turn_onto(h_banks[block][:, t, :], targets[block // PACK][:, block % PACK, t, :], t == 0, False)
+                    turn_onto(h_banks[block][:, t, :], targets[k][:, c, t, :], t == 0, False)
 
         def score(k, u_mx):
             banks = []
@@ -246,18 +266,18 @@ def tile_attend_gmf_sq_u_kernel(tc, uT, vT, y, us, ts, offs, uoffs, out):
         def model_block(k, c, scores):
             block = k * BLOCKS + c
             model = sb([P, N], F32, "model%d" % block)
-            nc.vector.scalar_tensor_tensor(model[:], scores[c][:], us_sq[:, block : block + 1], ts_rows[block // PACK][:], MULT, MULT)
+            nc.vector.scalar_tensor_tensor(model[:], scores[c][:], us_sq[:, block : block + 1], ts_rows[block // PACK], MULT, MULT)
             for t in range(PACK):
                 turn_onto(h_banks[block][:, t, :], model[:, t * P : (t + 1) * P], False, t == PACK - 1)
 
         def finish_h(k):
             h = sb([P, UNIT, PACK], BF16, "h%d" % k)
-            places = ts_cols[:, k * UNIT // R, :].unsqueeze(1).to_broadcast([P, P, PACK])
+            places = ts_cols[k * UNIT // R][:].unsqueeze(1).to_broadcast([P, P, PACK])
             for c in range(BLOCKS):
                 nc.vector.tensor_tensor(h[:, c * P : (c + 1) * P, :], h_banks[k * BLOCKS + c][:].rearrange("p t r -> p r t"), places, MULT)
             return h
 
-        du_halves = [sb([P, 2, B * R], F32, "du%d" % half, ("v2", "v3")[half]) for half in range(2)]
+        du_halves = [sb([P, 2, B * R], F32, "du%d" % half, ("pair0", "ts_table")[half]) for half in range(2)]
 
         def products(k, h):
             h_mx = mx_tiles("h%d" % k, UNIT)
@@ -266,8 +286,8 @@ def tile_attend_gmf_sq_u_kernel(tc, uT, vT, y, us, ts, offs, uoffs, out):
             for half in range(2):
                 sums = bank_tile([P, 2, UNIT], "du_bank", H_BANKS[k] + half)
                 for s in range(2):
-                    vt, first = vt_mx[2 * half + s]
-                    cols = slice(first + k * UNIT // R * P, first + (k * UNIT // R + 1) * P)
+                    vt = vt_mx[k * UNIT // R, half]
+                    cols = slice(s * P, (s + 1) * P)
                     nc.tensor.matmul_mx(
                         sums[:, s, :], lhsT=vt[0][:, cols].bitcast(E4), lhsT_scale=vt[1][:, cols],
                         rhs=h_mx[0][:].bitcast(E5), rhs_scale=h_mx[1][:], start=True, stop=True,
@@ -295,33 +315,43 @@ def tile_attend_gmf_sq_u_kernel(tc, uT, vT, y, us, ts, offs, uoffs, out):
         def store(queue, j):
             queue.dma_start(out.rearrange("(m j) c -> m j c", j=PACK)[:, j, :], windows[j][:])
 
-        u_mx0 = quantise_users(0, first_woven)
+        u_mx0 = quantise_users(0, first_woven[:])
         scores0 = score(0, u_mx0)
-        scale_targets(0)
+        scale_targets(0, "raw0_0")
         turn_targets(0)
-        copy_ts_row(1, "y0")
-        pick_users(nc.scalar, 3, 3 * UNIT, 4 * UNIT)
-        u_mx1 = quantise_users(1, weave_users(1, None))
+        u_picked1.append(sb([P, 2, R], F32, "u_picked1_1", "y1"))
+        for j in (2, 3):
+            pick_users(nc.scalar, j, 2 * UNIT, 3 * UNIT)
+        woven1 = sb([P, UNIT, PACK], BF16, "u_woven1")
+        weave_users(woven1[:], u_picked0[:, :, UNIT:R])
+        late_woven = sb([P, R, PACK], BF16, "late_woven", "u0_codes")
+        u_mx1 = quantise_users(1, woven1[:])
         for c in range(BLOCKS):
             model_block(0, c, scores0)
         scores1 = score(1, u_mx1)
-        scale_targets(1)
+        scale_targets(1, "raw1_1024")
+        for j in (2, 3):
+            pick_users(nc.scalar, j, 3 * UNIT, 4 * UNIT)
         turn_targets(1)
-        woven2 = weave_users(2, "u0_codes")
+        laid11 = sb([P, 2 * N], BF16, "laid11", "y2")
+        turn_items(nc.scalar, 1, 1, 0, laid11[:])
+        weave_users(late_woven[:, :, 0:2], u_picked1[0][:])
         h0 = finish_h(0)
+        weave_users(late_woven[:, 0:UNIT, 2:4], u_picked1[1][:, :, 0:UNIT])
         model_block(1, 0, scores1)
         sums0 = products(0, h0)
         model_block(1, 1, scores1)
-        u_mx2 = quantise_users(2, woven2)
+        u_mx2 = quantise_users(2, late_woven[:, 0:UNIT, :])
         scores2 = score(2, u_mx2)
-        scale_targets(2)
-        scale_targets(3)
+        scale_targets(2, "raw1_1664")
         copy_out(nc.scalar, 0, 0, sums0)
         copy_out(nc.scalar, 0, 1, sums0)
         turn_targets(2)
-        woven3 = weave_users(3, "model1")
+        scale_targets(3, "h0_codes")
+        weave_users(late_woven[:, UNIT:R, 2:4], u_picked1[1][:, :, UNIT:R])
         h1 = finish_h(1)
-        u_mx3 = quantise_users(3, woven3)
+        u_mx3 = quantise_users(3, late_woven[:, UNIT:R, :])
+        quantise_turned(1, 1, laid11[:], None)
         sums1 = products(1, h1)
         clear_window(nc.gpsimd, 4, "h1")
         scores3 = score(3, u_mx3)
@@ -333,7 +363,8 @@ def tile_attend_gmf_sq_u_kernel(tc, uT, vT, y, us, ts, offs, uoffs, out):
         turn_targets(3)
         for c in range(BLOCKS):
             model_block(3, c, scores3)
-        sums2 = products(2, finish_h(2))
+        h2 = finish_h(2)
+        sums2 = products(2, h2)
         scatter_unit(0, 1)
         scatter_unit(1, 1)
         copy_out(nc.scalar, 2, 0, sums2)

@@ -201,11 +201,17 @@ def tile_attend_gmf_sq_u_kernel(tc, uT, vT, y, us, ts, offs, uoffs, out):
         v_mx = [quantise_woven("v0", v_woven0)]
 
         u_picked0 = sb([P, PACK, R], F32, "u_picked0")
-        u_picked1 = [sb([P, 2, R], F32, "u_picked1_0")]
+        u_picked1 = sb([P, 2, R], F32, "u_picked1")
 
         def pick_users(engine, j, r0, r1):
-            dst = u_picked0[:, j, r0:r1] if r0 < R else u_picked1[j // 2][:, j % 2, r0 - R : r1 - R]
+            dst = u_picked0[:, j, r0:r1] if r0 < R else u_picked1[:, j, :]
             gather(engine, dst, u_planes[j], entries(user_list, r0, r1))
+
+        def pick_late_users(k, tag):
+            picked = sb([P, 2, UNIT], F32, "u_late%d" % k, tag)
+            for j in range(2):
+                gather(nc.scalar, picked[:, j, :], u_planes[2 + j], entries(user_list, k * UNIT, (k + 1) * UNIT))
+            return picked
 
         pick_users(nc.scalar, 0, 0, R)
         pick_users(nc.scalar, 0, R, B * R)
@@ -216,6 +222,8 @@ def tile_attend_gmf_sq_u_kernel(tc, uT, vT, y, us, ts, offs, uoffs, out):
         turn_items(nc.vector, 0, 1, 2, laid01[:])
         pick_users(nc.scalar, 1, 0, R)
         pick_users(nc.scalar, 1, R, B * R)
+        laid11 = sb([P, 2 * N], BF16, "laid11", "u1")
+        turn_items(nc.scalar, 1, 1, 3, laid11[:])
         pick_users(nc.vector, 2, 0, UNIT)
         pick_users(nc.scalar, 2, UNIT, R)
         quantise_turned(0, 1, laid01[:], None)
@@ -243,13 +251,6 @@ def tile_attend_gmf_sq_u_kernel(tc, uT, vT, y, us, ts, offs, uoffs, out):
                 rows_in = y_blocks[block].rearrange("p (q t) -> p q t", t=PACK)
                 nc.scalar.activation(target.rearrange("p t q -> p q t"), rows_in, COPY, scale=us_neg[:, block : block + 1])
 
-        def turn_targets(k):
-            for c in range(BLOCKS):
-                block = k * BLOCKS + c
-                h_banks[block] = bank_tile([P, PACK, P], "h_bank", H_BANKS[k] + c)
-                for t in range(PACK):
-                    turn_onto(h_banks[block][:, t, :], targets[k][:, c, t, :], t == 0, False)
-
         def score(k, u_mx):
             banks = []
             for c in range(BLOCKS):
@@ -267,23 +268,23 @@ def tile_attend_gmf_sq_u_kernel(tc, uT, vT, y, us, ts, offs, uoffs, out):
             block = k * BLOCKS + c
             model = sb([P, N], F32, "model%d" % block)
             nc.vector.scalar_tensor_tensor(model[:], scores[c][:], us_sq[:, block : block + 1], ts_rows[block // PACK], MULT, MULT)
+            h_banks[block] = bank_tile([P, PACK, P], "h_bank", H_BANKS[k] + c)
             for t in range(PACK):
-                turn_onto(h_banks[block][:, t, :], model[:, t * P : (t + 1) * P], False, t == PACK - 1)
+                turn_onto(h_banks[block][:, t, :], model[:, t * P : (t + 1) * P], t == 0, False)
+            for t in range(PACK):
+                turn_onto(h_banks[block][:, t, :], targets[k][:, c, t, :], False, t == PACK - 1)
 
-        def finish_h(k):
-            h = sb([P, UNIT, PACK], BF16, "h%d" % k)
+        def finish_h(k, c, h):
             places = ts_cols[k * UNIT // R][:].unsqueeze(1).to_broadcast([P, P, PACK])
-            for c in range(BLOCKS):
-                nc.vector.tensor_tensor(h[:, c * P : (c + 1) * P, :], h_banks[k * BLOCKS + c][:].rearrange("p t r -> p r t"), places, MULT)
-            return h
+            nc.vector.tensor_tensor(h[:, c * P : (c + 1) * P, :], h_banks[k * BLOCKS + c][:].rearrange("p t r -> p r t"), places, MULT)
 
         du_halves = [sb([P, 2, B * R], F32, "du%d" % half, ("pair0", "ts_table")[half]) for half in range(2)]
 
-        def products(k, h):
+        def products(k, h, halves=(0, 1)):
             h_mx = mx_tiles("h%d" % k, UNIT)
             quantise(h_mx, h[:].rearrange("p r t -> p (r t)"), E5)
-            banks = []
-            for half in range(2):
+            banks = {}
+            for half in halves:
                 sums = bank_tile([P, 2, UNIT], "du_bank", H_BANKS[k] + half)
                 for s in range(2):
                     vt = vt_mx[k * UNIT // R, half]
@@ -292,7 +293,7 @@ def tile_attend_gmf_sq_u_kernel(tc, uT, vT, y, us, ts, offs, uoffs, out):
                         sums[:, s, :], lhsT=vt[0][:, cols].bitcast(E4), lhsT_scale=vt[1][:, cols],
                         rhs=h_mx[0][:].bitcast(E5), rhs_scale=h_mx[1][:], start=True, stop=True,
                     )
-                banks.append(sums)
+                banks[half] = sums
             return banks
 
         def copy_out(engine, k, half, banks):
@@ -317,62 +318,61 @@ def tile_attend_gmf_sq_u_kernel(tc, uT, vT, y, us, ts, offs, uoffs, out):
 
         u_mx0 = quantise_users(0, first_woven[:])
         scores0 = score(0, u_mx0)
-        scale_targets(0, "raw0_0")
-        turn_targets(0)
-        u_picked1.append(sb([P, 2, R], F32, "u_picked1_1", "y1"))
-        for j in (2, 3):
-            pick_users(nc.scalar, j, 2 * UNIT, 3 * UNIT)
         woven1 = sb([P, UNIT, PACK], BF16, "u_woven1")
         weave_users(woven1[:], u_picked0[:, :, UNIT:R])
-        late_woven = sb([P, R, PACK], BF16, "late_woven", "u0_codes")
+        quantise_turned(1, 1, laid11[:], "u_woven0")
         u_mx1 = quantise_users(1, woven1[:])
+        scores1 = score(1, u_mx1)
+        scale_targets(0, "raw0_0")
+        scale_targets(1, "raw1_1024")
+        late2 = pick_late_users(2, "y1")
+        late3 = pick_late_users(3, "y2")
         for c in range(BLOCKS):
             model_block(0, c, scores0)
-        scores1 = score(1, u_mx1)
-        scale_targets(1, "raw1_1024")
-        for j in (2, 3):
-            pick_users(nc.scalar, j, 3 * UNIT, 4 * UNIT)
-        turn_targets(1)
-        laid11 = sb([P, 2 * N], BF16, "laid11", "y2")
-        turn_items(nc.scalar, 1, 1, 0, laid11[:])
-        weave_users(late_woven[:, :, 0:2], u_picked1[0][:])
-        h0 = finish_h(0)
-        weave_users(late_woven[:, 0:UNIT, 2:4], u_picked1[1][:, :, 0:UNIT])
-        model_block(1, 0, scores1)
+        for c in range(BLOCKS):
+            model_block(1, c, scores1)
+        late_woven = sb([P, R, PACK], BF16, "late_woven", "u1_codes")
+        weave_users(late_woven[:, :, 0:2], u_picked1[:])
+        h0 = sb([P, UNIT, PACK], BF16, "h0")
+        for c in range(BLOCKS):
+            finish_h(0, c, h0)
+        weave_users(late_woven[:, 0:UNIT, 2:4], late2[:])
         sums0 = products(0, h0)
-        model_block(1, 1, scores1)
         u_mx2 = quantise_users(2, late_woven[:, 0:UNIT, :])
         scores2 = score(2, u_mx2)
         scale_targets(2, "raw1_1664")
         copy_out(nc.scalar, 0, 0, sums0)
         copy_out(nc.scalar, 0, 1, sums0)
-        turn_targets(2)
         scale_targets(3, "h0_codes")
-        weave_users(late_woven[:, UNIT:R, 2:4], u_picked1[1][:, :, UNIT:R])
-        h1 = finish_h(1)
-        u_mx3 = quantise_users(3, late_woven[:, UNIT:R, :])
-        quantise_turned(1, 1, laid11[:], None)
+        h1 = sb([P, UNIT, PACK], BF16, "h1")
+        for c in range(BLOCKS):
+            finish_h(1, c, h1)
+        weave_users(late_woven[:, UNIT:R, 2:4], late3[:])
         sums1 = products(1, h1)
-        clear_window(nc.gpsimd, 4, "h1")
+        u_mx3 = quantise_users(3, late_woven[:, UNIT:R, :])
         scores3 = score(3, u_mx3)
+        clear_window(nc.gpsimd, 2, "u1_codes")
         scatter_unit(0, 0)
         copy_out(nc.scalar, 1, 0, sums1)
         copy_out(nc.scalar, 1, 1, sums1)
         for c in range(BLOCKS):
             model_block(2, c, scores2)
-        turn_targets(3)
         for c in range(BLOCKS):
             model_block(3, c, scores3)
-        h2 = finish_h(2)
-        sums2 = products(2, h2)
+        h2 = sb([P, UNIT, PACK], BF16, "h2")
+        for c in range(BLOCKS):
+            finish_h(2, c, h2)
+        sums2 = products(2, h2, (1, 0))
         scatter_unit(0, 1)
         scatter_unit(1, 1)
         copy_out(nc.scalar, 2, 0, sums2)
         scatter_unit(0, 2)
-        h3 = finish_h(3)
+        h3 = sb([P, UNIT, PACK], BF16, "h3")
+        for c in range(BLOCKS):
+            finish_h(3, c, h3)
         copy_out(nc.vector, 2, 1, sums2)
         sums3 = products(3, h3)
-        clear_window(nc.gpsimd, 4, "h3")
+        clear_window(nc.gpsimd, 2, "h3")
         copy_out(nc.scalar, 3, 0, sums3)
         copy_out(nc.scalar, 3, 1, sums3)
         scatter_unit(0, 3)

@@ -196,6 +196,7 @@ def tile_attend_gmf_sq_u_kernel(tc, uT, vT, y, us, ts, offs, uoffs, out):
         for b in range(B):
             turn_items(nc.scalar, b, 0, b, first_laid[:, b, :])
         pick_items(1, last_words)
+        clear_window(nc.gpsimd, 2, "raw1_1664")
         v_woven0 = weave(nc.vector, "v_woven0", None, v_picked[:, :, 0, :])
         quantise_turned(0, 0, first_laid[:, 0, :], "pair1")
         v_mx = [quantise_woven("v0", v_woven0)]
@@ -340,7 +341,7 @@ def tile_attend_gmf_sq_u_kernel(tc, uT, vT, y, us, ts, offs, uoffs, out):
         sums0 = products(0, h0)
         u_mx2 = quantise_users(2, late_woven[:, 0:UNIT, :])
         scores2 = score(2, u_mx2)
-        scale_targets(2, "raw1_1664")
+        scale_targets(2, "raw0_512")
         copy_out(nc.scalar, 0, 0, sums0)
         copy_out(nc.scalar, 0, 1, sums0)
         scale_targets(3, "h0_codes")
@@ -351,7 +352,6 @@ def tile_attend_gmf_sq_u_kernel(tc, uT, vT, y, us, ts, offs, uoffs, out):
         sums1 = products(1, h1)
         u_mx3 = quantise_users(3, late_woven[:, UNIT:R, :])
         scores3 = score(3, u_mx3)
-        clear_window(nc.gpsimd, 2, "u1_codes")
         scatter_unit(0, 0)
         copy_out(nc.scalar, 1, 0, sums1)
         copy_out(nc.scalar, 1, 1, sums1)

@@ -372,7 +372,7 @@ def tile_attend_gmf_sq_u_kernel(tc, uT, vT, y, us, ts, offs, uoffs, out):
             finish_h(3, c, h3)
         copy_out(nc.vector, 2, 1, sums2)
         sums3 = products(3, h3)
-        clear_window(nc.gpsimd, 2, "h3")
+        clear_window(nc.gpsimd, 2, "h3_codes")
         copy_out(nc.scalar, 3, 0, sums3)
         copy_out(nc.scalar, 3, 1, sums3)
         scatter_unit(0, 3)

@@ -236,6 +236,9 @@ def tile_attend_gmf_sq_u_kernel(tc, uT, vT, y, us, ts, offs, uoffs, out):
         def weave_users(woven, picked):
             nc.vector.tensor_copy(woven, picked.rearrange("p j r -> p r j"))
 
+        def pair_users(engine, words, picked):
+            copy(engine, words.bitcast(BF16).rearrange("p (r e) -> p r e", e=2), picked.rearrange("p e r -> p r e"))
+
         def quantise_users(k, woven):
             mx = mx_tiles("u%d" % k, UNIT)
             quantise(mx, woven.rearrange("p r j -> p (r j)"), E4)
@@ -327,30 +330,32 @@ def tile_attend_gmf_sq_u_kernel(tc, uT, vT, y, us, ts, offs, uoffs, out):
         scale_targets(0, "raw0_0")
         scale_targets(1, "raw1_1024")
         late2 = pick_late_users(2, "y1")
-        late3 = pick_late_users(3, "y2")
+        words1 = sb([P, 2, R], U32, "u_words1", "y2")
+        pair_users(nc.scalar, words1[:, 0, :], u_picked1[:])
+        late3 = pick_late_users(3, "raw0_0")
         for c in range(BLOCKS):
             model_block(0, c, scores0)
         for c in range(BLOCKS):
             model_block(1, c, scores1)
-        late_woven = sb([P, R, PACK], BF16, "late_woven", "u1_codes")
-        weave_users(late_woven[:, :, 0:2], u_picked1[:])
         h0 = sb([P, UNIT, PACK], BF16, "h0")
-        for c in range(BLOCKS):
-            finish_h(0, c, h0)
-        weave_users(late_woven[:, 0:UNIT, 2:4], late2[:])
+        finish_h(0, 0, h0)
+        pair_users(nc.vector, words1[:, 1, 0:UNIT], late2[:])
+        finish_h(0, 1, h0)
+        woven2 = weave(nc.vector, "u_woven2", None, words1[:, :, 0:UNIT])
         sums0 = products(0, h0)
-        u_mx2 = quantise_users(2, late_woven[:, 0:UNIT, :])
+        u_mx2 = quantise_woven("u2", woven2)
         scores2 = score(2, u_mx2)
         scale_targets(2, "raw0_512")
         copy_out(nc.scalar, 0, 0, sums0)
         copy_out(nc.scalar, 0, 1, sums0)
         scale_targets(3, "h0_codes")
         h1 = sb([P, UNIT, PACK], BF16, "h1")
-        for c in range(BLOCKS):
-            finish_h(1, c, h1)
-        weave_users(late_woven[:, UNIT:R, 2:4], late3[:])
+        finish_h(1, 0, h1)
+        pair_users(nc.vector, words1[:, 1, UNIT:R], late3[:])
+        finish_h(1, 1, h1)
+        woven3 = weave(nc.vector, "u_woven3", None, words1[:, :, UNIT:R])
         sums1 = products(1, h1)
-        u_mx3 = quantise_users(3, late_woven[:, UNIT:R, :])
+        u_mx3 = quantise_woven("u3", woven3)
         scores3 = score(3, u_mx3)
         scatter_unit(0, 0)
         copy_out(nc.scalar, 1, 0, sums1)

@@ -15,6 +15,7 @@ U8 = mybir.dt.uint8
 E4 = mybir.dt.float8_e4m3fn_x4
 E5 = mybir.dt.float8_e5m2_x4
 MULT = mybir.AluOpType.mult
+ADD = mybir.AluOpType.add
 SQUARE = mybir.ActivationFunctionType.Square
 COPY = mybir.ActivationFunctionType.Copy
 
@@ -23,6 +24,7 @@ PACK = 4
 UNIT = 256
 UNITS = B * R // UNIT
 BLOCKS = UNIT // P
+WIDE = 384
 ALIGN = 256
 H_BANKS = (4, 6, 4, 0)
 LOADS = (
@@ -144,27 +146,25 @@ def tile_attend_gmf_sq_u_kernel(tc, uT, vT, y, us, ts, offs, uoffs, out):
         def pick_items(u, words):
             nc.vector.tensor_copy(v_picked[:, u].rearrange("p b (t q) -> p b q t", t=PACK), words.indirect(item_list[:]))
 
-        def turn_items(engine, b, u, bank, laid):
+        def turn_items(b, u, bank, laid):
             words = v_picked[:, u, b, :].bitcast(F32)
             turned = bank_tile([P, PACK, P], "v_bank", bank)
             for t in range(PACK):
                 nc.tensor.transpose(turned[:, t, :], words[:, t * P : (t + 1) * P], ident[:])
             halves = turned[:].rearrange("p t m -> p (t m)").bitcast(BF16)
-            copy(engine, laid.rearrange("p (e m t) -> p e m t", t=PACK, e=2), halves.rearrange("p (t m e) -> p e m t", t=PACK, e=2))
+            nc.scalar.copy(laid.rearrange("p (e m t) -> p e m t", t=PACK, e=2), halves.rearrange("p (t m e) -> p e m t", t=PACK, e=2))
 
         vt_mx = {}
 
-        def quantise_turned(b, u, laid, tag):
-            vt_mx[b, u] = mx_tiles("vt%d_%d" % (b, u), 2 * P, tag)
-            quantise(vt_mx[b, u], laid, E4)
+        def quantise_turned(u, groups, laid, tag):
+            mx = mx_tiles("vt%d_%d" % (u, groups[0]), len(groups) * 2 * P, tag)
+            quantise(mx, laid.rearrange("p b c -> p (b c)"), E4)
+            for place, b in enumerate(groups):
+                vt_mx[b, u] = (mx, place * 2 * P)
 
-        def weave(engine, name, tag, picked):
-            width = picked.shape[2]
-            woven = sb([P, width, 2], U32, name, tag)
-            if engine is nc.vector:
-                nc.vector.tensor_copy(woven[:].bitcast(I32), picked.rearrange("p u c -> p c u").bitcast(I32))
-            else:
-                nc.scalar.copy(woven[:], picked.rearrange("p u c -> p c u"))
+        def weave(name, picked):
+            woven = sb([P, picked.shape[2], 2], U32, name)
+            nc.vector.tensor_copy(woven[:].bitcast(I32), picked.rearrange("p u c -> p c u").bitcast(I32))
             return woven
 
         def quantise_woven(name, woven):
@@ -194,12 +194,12 @@ def tile_attend_gmf_sq_u_kernel(tc, uT, vT, y, us, ts, offs, uoffs, out):
         last_words = round_pair(1)
         first_laid = sb([P, B, 2 * N], BF16, "first_laid", "raw1_0")
         for b in range(B):
-            turn_items(nc.scalar, b, 0, b, first_laid[:, b, :])
+            turn_items(b, 0, b, first_laid[:, b, :])
         pick_items(1, last_words)
         clear_window(nc.gpsimd, 2, "raw1_1664")
-        v_woven0 = weave(nc.vector, "v_woven0", None, v_picked[:, :, 0, :])
-        quantise_turned(0, 0, first_laid[:, 0, :], "pair1")
-        v_mx = [quantise_woven("v0", v_woven0)]
+        v_woven = weave("v_woven", v_picked[:].rearrange("p u b i -> p u (b i)"))
+        quantise_turned(0, (0, 1), first_laid[:], "pair1")
+        v_mx = quantise_woven("v", v_woven)
 
         u_picked0 = sb([P, PACK, R], F32, "u_picked0")
         u_picked1 = sb([P, 2, R], F32, "u_picked1")
@@ -216,18 +216,16 @@ def tile_attend_gmf_sq_u_kernel(tc, uT, vT, y, us, ts, offs, uoffs, out):
 
         pick_users(nc.scalar, 0, 0, R)
         pick_users(nc.scalar, 0, R, B * R)
-        v_woven1 = weave(nc.vector, "v_woven1", None, v_picked[:, :, 1, :])
-        quantise_turned(1, 0, first_laid[:, 1, :], "v_woven0")
-        v_mx.append(quantise_woven("v1", v_woven1))
-        laid01 = sb([P, 2 * N], BF16, "laid01")
-        turn_items(nc.vector, 0, 1, 2, laid01[:])
-        pick_users(nc.scalar, 1, 0, R)
+        last_laid = sb([P, B, 2 * N], BF16, "last_laid", "u0")
+        for b in range(B):
+            turn_items(b, 1, 2 + b, last_laid[:, b, :])
+        pick_users(nc.vector, 1, 0, UNIT)
         pick_users(nc.scalar, 1, R, B * R)
-        laid11 = sb([P, 2 * N], BF16, "laid11", "u1")
-        turn_items(nc.scalar, 1, 1, 3, laid11[:])
-        pick_users(nc.vector, 2, 0, UNIT)
-        pick_users(nc.scalar, 2, UNIT, R)
-        quantise_turned(0, 1, laid01[:], None)
+        pick_users(nc.scalar, 1, UNIT, R)
+        words1 = sb([P, 2, R], U32, "u_words1")
+        first_pairs = words1[:, 0, :].bitcast(BF16).rearrange("p (r e) -> p r e", e=2)
+        nc.gpsimd.tensor_scalar(first_pairs, u_picked1[:].rearrange("p e r -> p r e"), 1.0, 0.0, op0=MULT, op1=ADD)
+        pick_users(nc.vector, 2, 0, R)
         first_woven = sb([P, UNIT, PACK], BF16, "u_woven0")
         nc.vector.tensor_copy(first_woven[:, :, 0:3], u_picked0[:, 0:3, 0:UNIT].rearrange("p j r -> p r j"))
         gather(nc.vector, first_woven[:, :, 3], u_planes[3], entries(user_list, 0, UNIT))
@@ -236,8 +234,8 @@ def tile_attend_gmf_sq_u_kernel(tc, uT, vT, y, us, ts, offs, uoffs, out):
         def weave_users(woven, picked):
             nc.vector.tensor_copy(woven, picked.rearrange("p j r -> p r j"))
 
-        def pair_users(engine, words, picked):
-            copy(engine, words.bitcast(BF16).rearrange("p (r e) -> p r e", e=2), picked.rearrange("p e r -> p r e"))
+        def pair_users(words, picked):
+            nc.scalar.copy(words.bitcast(BF16).rearrange("p (r e) -> p r e", e=2), picked.rearrange("p e r -> p r e"))
 
         def quantise_users(k, woven):
             mx = mx_tiles("u%d" % k, UNIT)
@@ -260,10 +258,10 @@ def tile_attend_gmf_sq_u_kernel(tc, uT, vT, y, us, ts, offs, uoffs, out):
             for c in range(BLOCKS):
                 rows = slice(c * P, (c + 1) * P)
                 scores = bank_tile([P, N], "scores", (k * BLOCKS + c) % PACK)
-                b = k * UNIT // R
+                slots = slice(k * UNIT // R * N, (k * UNIT // R + 1) * N)
                 nc.tensor.matmul_mx(
                     scores[:], lhsT=u_mx[0][:, rows].bitcast(E4), lhsT_scale=u_mx[1][:, rows],
-                    rhs=v_mx[b][0][:].bitcast(E4), rhs_scale=v_mx[b][1][:], start=True, stop=True,
+                    rhs=v_mx[0][:, slots].bitcast(E4), rhs_scale=v_mx[1][:, slots], start=True, stop=True,
                 )
                 banks.append(scores)
             return banks
@@ -291,8 +289,8 @@ def tile_attend_gmf_sq_u_kernel(tc, uT, vT, y, us, ts, offs, uoffs, out):
             for half in halves:
                 sums = bank_tile([P, 2, UNIT], "du_bank", H_BANKS[k] + half)
                 for s in range(2):
-                    vt = vt_mx[k * UNIT // R, half]
-                    cols = slice(s * P, (s + 1) * P)
+                    vt, first = vt_mx[k * UNIT // R, half]
+                    cols = slice(first + s * P, first + (s + 1) * P)
                     nc.tensor.matmul_mx(
                         sums[:, s, :], lhsT=vt[0][:, cols].bitcast(E4), lhsT_scale=vt[1][:, cols],
                         rhs=h_mx[0][:].bitcast(E5), rhs_scale=h_mx[1][:], start=True, stop=True,
@@ -324,36 +322,35 @@ def tile_attend_gmf_sq_u_kernel(tc, uT, vT, y, us, ts, offs, uoffs, out):
         scores0 = score(0, u_mx0)
         woven1 = sb([P, UNIT, PACK], BF16, "u_woven1")
         weave_users(woven1[:], u_picked0[:, :, UNIT:R])
-        quantise_turned(1, 1, laid11[:], "u_woven0")
+        quantise_turned(1, (0,), last_laid[:, 0:1, :], "u_woven0")
         u_mx1 = quantise_users(1, woven1[:])
         scores1 = score(1, u_mx1)
         scale_targets(0, "raw0_0")
         scale_targets(1, "raw1_1024")
-        late2 = pick_late_users(2, "y1")
-        words1 = sb([P, 2, R], U32, "u_words1", "y2")
-        pair_users(nc.scalar, words1[:, 0, :], u_picked1[:])
-        late3 = pick_late_users(3, "raw0_0")
+        late2 = pick_late_users(2, "y0")
+        pair_users(words1[:, 1, 0:UNIT], late2[:])
+        late3 = pick_late_users(3, "y2")
         for c in range(BLOCKS):
             model_block(0, c, scores0)
         for c in range(BLOCKS):
             model_block(1, c, scores1)
+        quantise_turned(1, (1,), last_laid[:, 1:2, :], "u1_codes")
         h0 = sb([P, UNIT, PACK], BF16, "h0")
-        finish_h(0, 0, h0)
-        pair_users(nc.vector, words1[:, 1, 0:UNIT], late2[:])
-        finish_h(0, 1, h0)
-        woven2 = weave(nc.vector, "u_woven2", None, words1[:, :, 0:UNIT])
+        for c in range(BLOCKS):
+            finish_h(0, c, h0)
+        woven2 = weave("u_woven2", words1[:, :, 0:UNIT])
+        pair_users(words1[:, 1, UNIT:R], late3[:])
         sums0 = products(0, h0)
         u_mx2 = quantise_woven("u2", woven2)
         scores2 = score(2, u_mx2)
         scale_targets(2, "raw0_512")
         copy_out(nc.scalar, 0, 0, sums0)
         copy_out(nc.scalar, 0, 1, sums0)
-        scale_targets(3, "h0_codes")
+        scale_targets(3, "y0")
         h1 = sb([P, UNIT, PACK], BF16, "h1")
-        finish_h(1, 0, h1)
-        pair_users(nc.vector, words1[:, 1, UNIT:R], late3[:])
-        finish_h(1, 1, h1)
-        woven3 = weave(nc.vector, "u_woven3", None, words1[:, :, UNIT:R])
+        for c in range(BLOCKS):
+            finish_h(1, c, h1)
+        woven3 = weave("u_woven3", words1[:, :, UNIT:R])
         sums1 = products(1, h1)
         u_mx3 = quantise_woven("u3", woven3)
         scores3 = score(3, u_mx3)
@@ -382,11 +379,12 @@ def tile_attend_gmf_sq_u_kernel(tc, uT, vT, y, us, ts, offs, uoffs, out):
         copy_out(nc.scalar, 3, 1, sums3)
         scatter_unit(0, 3)
         store(nc.sync, 0)
-        scatter(nc.vector, 2, 0, 3 * UNIT)
-        scatter(nc.vector, 2, 3 * UNIT, 4 * UNIT)
+        scatter(nc.vector, 2, 0, B * R - WIDE)
+        scatter(nc.scalar, 2, B * R - WIDE, B * R)
         store(nc.sync, 2)
         for k in (3, 0, 2):
             scatter_unit(1, k)
         store(nc.scalar, 1)
-        scatter(nc.vector, 3, 0, B * R)
+        scatter(nc.vector, 3, 0, 3 * UNIT)
+        scatter(nc.vector, 3, 3 * UNIT, 4 * UNIT)
         store(nc.sync, 3)

@@ -366,7 +366,7 @@ def tile_attend_gmf_sq_u_kernel(tc, uT, vT, y, us, ts, offs, uoffs, out):
             finish_h(2, c, h2)
         sums2 = products(2, h2, (1, 0))
         scatter_unit(0, 1)
-        scatter_unit(1, 1)
+        scatter(nc.scalar, 1, 0, WIDE)
         copy_out(nc.scalar, 2, 0, sums2)
         scatter_unit(0, 2)
         h3 = sb([P, UNIT, PACK], BF16, "h3")
@@ -382,8 +382,8 @@ def tile_attend_gmf_sq_u_kernel(tc, uT, vT, y, us, ts, offs, uoffs, out):
         scatter(nc.vector, 2, 0, B * R - WIDE)
         scatter(nc.scalar, 2, B * R - WIDE, B * R)
         store(nc.sync, 2)
-        for k in (3, 0, 2):
-            scatter_unit(1, k)
+        scatter_unit(1, 3)
+        scatter(nc.scalar, 1, WIDE, 2 * WIDE)
         store(nc.scalar, 1)
         scatter(nc.vector, 3, 0, 3 * UNIT)
         scatter(nc.vector, 3, 3 * UNIT, 4 * UNIT)

@@ -9,7 +9,6 @@ FLOPS = 2 * 2 * B * N * R * D
 F32 = mybir.dt.float32
 BF16 = mybir.dt.bfloat16
 U32 = mybir.dt.uint32
-I32 = mybir.dt.int32
 U16 = mybir.dt.uint16
 U8 = mybir.dt.uint8
 E4 = mybir.dt.float8_e4m3fn_x4
@@ -22,25 +21,29 @@ COPY = mybir.ActivationFunctionType.Copy
 P = 128
 PACK = 4
 UNIT = 256
-UNITS = B * R // UNIT
 BLOCKS = UNIT // P
 WIDE = 384
 ALIGN = 256
+KB = 1024
+PLANE = 8 * KB
 H_BANKS = (4, 6, 4, 0)
-LOADS = (
-    ((0, 512, 0), (512, 1024, 0), (1024, 1408, 0), (1408, 2048, 640)),
-    ((0, 1024, 384), (1024, 1664, 640), (1664, 2048, 384)),
-)
+V_AT = 0
+U_AT = 4 * PLANE
+PICKED_AT = 8 * PLANE
+LATE_AT = 10 * PLANE
 
 
 def tile_attend_gmf_sq_u_kernel(tc, uT, vT, y, us, ts, offs, uoffs, out):
     nc = tc.nc
     with ExitStack() as ctx:
         keep = ctx.enter_context(tc.tile_pool(name="keep", bufs=1))
+        shared = ctx.enter_context(tc.tile_pool(name="shared", bufs=1))
         psum = ctx.enter_context(tc.psum_pool(name="psum", bufs=1))
 
-        def sb(shape, dtype, name, tag=None):
-            return keep.tile(shape, dtype, name=name, tag=tag or name, align_bytes=ALIGN)
+        def sb(shape, dtype, name, at=None):
+            if at is None:
+                return keep.tile(shape, dtype, name=name, align_bytes=ALIGN)
+            return shared.tile(shape, dtype, name=name, align_bytes=ALIGN, offset=at)
 
         def bank_tile(shape, name, bank):
             return psum.tile(shape, F32, name=name, tag="bank%d" % bank)
@@ -48,249 +51,217 @@ def tile_attend_gmf_sq_u_kernel(tc, uT, vT, y, us, ts, offs, uoffs, out):
         def entries(offsets, e0, e1):
             return offsets[:, e0 // 16 : e1 // 16]
 
-        def load_plane(table, j, name):
-            plane = sb([P, T], F32, name)
-            nc.sync.dma_start(plane[:], table.rearrange("(p j) c -> p j c", j=PACK)[:, j, :])
-            return plane
-
-        def gather(engine, dst, plane, offsets):
-            if engine is nc.vector:
-                nc.vector.tensor_copy(dst, plane[:].indirect(offsets))
-            else:
-                nc.scalar.activation(dst, plane[:].indirect(offsets), COPY)
-
-        def copy(engine, dst, src):
+        def move(engine, dst, src):
             if engine is nc.vector:
                 nc.vector.tensor_copy(dst, src)
             else:
-                nc.scalar.copy(dst, src)
+                nc.scalar.activation(dst, src, COPY)
 
-        def load_pair(n, table, u):
-            planes = table.rearrange("(p t) c -> p t c", t=PACK)[:, 2 * u : 2 * u + 2, :]
-            pieces = []
-            for c0, c1, share in LOADS[n]:
-                raw = sb([P, 2, c1 - c0], F32, "raw%d_%d" % (n, c0))
-                nc.sync.dma_start(raw[:], planes[:, :, c0:c1])
-                pieces.append((c0, c1, share, raw))
-            return pieces
+        def load_plane(table, j, name, at):
+            plane = sb([P, T], F32, name, at + j * PLANE)
+            nc.sync.dma_start(plane[:], table.rearrange("(p j) c -> p j c", j=PACK)[:, j, :])
+            return plane
 
-        def round_pair(n):
-            pair = sb([P, T, 2], BF16, "pair%d" % n)
-            for c0, c1, share, raw in loaded[n]:
-                cut = c1 - c0 - share
-                side_by_side = raw[:].rearrange("p e c -> p c e")
-                if cut:
-                    nc.scalar.activation(pair[:, c0 : c0 + cut, :], side_by_side[:, 0:cut, :], COPY)
-                if share:
-                    nc.vector.tensor_copy(pair[:, c0 + cut : c1, :], side_by_side[:, cut:, :])
-            return pair[:].rearrange("p c e -> p (c e)").bitcast(U32)
-
-        def mx_tiles(name, width, tag=None):
-            return sb([P, width], U32, name + "_codes", tag), sb([P, width], U8, name + "_scales")
-
-        def quantise(mx, src, fmt):
-            nc.vector.quantize_mx(mx[0][:].bitcast(fmt), mx[1][:], src)
+        def quantise(name, src, fmt, at=None):
+            width = src.shape[1] // PACK
+            codes = sb([P, width], U32, name + "_codes", at)
+            scales = sb([P, width], U8, name + "_scales")
+            nc.vector.quantize_mx(codes[:].bitcast(fmt), scales[:], src)
+            return codes, scales
 
         def turn_onto(dst, src, start, stop):
             nc.tensor.matmul(dst, src, ident[:], start=start, stop=stop, is_transpose=True)
 
+        def by_place(slots, dealt):
+            return slots.rearrange("p (t q) -> p t q" if dealt else "p (q t) -> p t q", t=PACK)
+
         item_list = keep.tile([P, B * N // 16], U16, name="item_list")
         user_list = keep.tile([P, B * R // 16], U16, name="user_list")
-        ts_first = sb([1, T], F32, "ts_first")
-        us_first = sb([B * PACK, P], F32, "us_first")
+        ts_table = sb([P, T], F32, "ts_table")
+        us_rows = sb([P, P], F32, "us_rows")
+        us_at = P - B * PACK
         nc.sync.dma_start(item_list[:], offs)
-        nc.sync.dma_start(us_first[:], us.rearrange("b (c p) o -> (b c) (p o)", p=P))
-        nc.sync.dma_start(ts_first[:], ts[0:1, :])
-        loaded = [load_pair(0, vT, 0)]
+        nc.sync.dma_start(ts_table[P - 1 : P, :], ts[0:1, :])
+        nc.sync.dma_start(us_rows[us_at:P, :], us.rearrange("b (c p) o -> (b c) (p o)", p=P))
+        v_planes = [load_plane(vT, j, "v%d" % j, V_AT) for j in range(PACK)]
         nc.sync.dma_start(user_list[:], uoffs)
-        loaded.append(load_pair(1, vT, 1))
-        u_planes = [load_plane(uT, j, "u%d" % j) for j in range(PACK)]
+        u_planes = [load_plane(uT, j, "u%d" % j, U_AT) for j in range(PACK)]
+        u_first = sb([P, PACK, R], F32, "u_first")
+        u_late = [sb([P, PACK, UNIT], F32, "u_late%d" % k) for k in range(2)]
+        y_rows = y.rearrange("b (c p) i -> p (b c) i", p=P)
         y_blocks = []
         for c0, c1 in ((0, 1), (1, 2), (2, 4), (4, 6), (6, 8)):
             rows_in = sb([P, c1 - c0, N], F32, "y%d" % c0)
-            nc.sync.dma_start(rows_in[:], y.rearrange("b (c p) i -> p (b c) i", p=P)[:, c0:c1, :])
+            nc.sync.dma_start(rows_in[:], y_rows[:, c0:c1, :])
             y_blocks.extend([rows_in[:, c, :] for c in range(c1 - c0)])
 
+        nc.vector.memset(ts_table[0 : P - 1, :], 0.0)
+        nc.vector.memset(us_rows[0:us_at, :], 0.0)
         ident = sb([P, P], F32, "ident")
         make_identity(nc, ident[:])
-        windows = []
+        windows = [sb([P, TU], F32, "window%d" % j) for j in range(PACK)]
+        for window in windows:
+            for c0 in (0, TU // 2):
+                nc.gpsimd.memset(window[:, c0 : c0 + TU // 2], 0.0)
 
-        def clear_window(engine, pieces, tag):
-            window = sb([P, TU], F32, "window%d" % len(windows), tag)
-            for c0 in range(0, TU, TU // pieces):
-                engine.memset(window[:, c0 : c0 + TU // pieces], 0.0)
-            windows.append(window)
-
-
-        ts_table = sb([P, T], F32, "ts_table")
-        us_rows = sb([P, P], F32, "us_rows")
-        nc.vector.memset(us_rows[:], 0.0)
-        nc.vector.memset(ts_table[:].bitcast(I32), 0)
-        nc.scalar.activation(us_rows[0 : B * PACK, :], us_first[:], COPY)
-        nc.vector.tensor_copy(ts_table[0:1, :], ts_first[:])
+        ts_picked = [sb([P, N], F32, "ts_picked%d" % b) for b in range(B)]
+        nc.vector.tensor_copy(
+            ts_picked[0][:].bitcast(U32).rearrange("p (t q) -> p q t", t=PACK),
+            ts_table[:].bitcast(U32).indirect(entries(item_list, 0, N)),
+        )
+        move(nc.scalar, ts_picked[1][:], ts_table[:].indirect(entries(item_list, N, B * N)))
         us_bank = bank_tile([P, P], "us_bank", 3)
         nc.tensor.transpose(us_bank[:], us_rows[:], ident[:])
         us_neg = sb([P, B * PACK], F32, "us_neg")
         us_sq = sb([P, B * PACK], F32, "us_sq")
-        nc.scalar.activation(us_neg[:], us_bank[:, 0 : B * PACK], COPY, scale=-1.0)
-        nc.scalar.activation(us_sq[:], us_bank[:, 0 : B * PACK], SQUARE)
-        ts_picked = sb([P, B, N], F32, "ts_picked")
-        for b in range(B):
-            ts_dealt = ts_picked[:, b, :].bitcast(U32).rearrange("p (t q) -> p q t", t=PACK)
-            nc.vector.tensor_copy(ts_dealt, ts_table[:].bitcast(U32).indirect(entries(item_list, b * N, (b + 1) * N)))
+        nc.scalar.activation(us_neg[:], us_bank[:, us_at:P], COPY, scale=-1.0)
+        nc.scalar.activation(us_sq[:], us_bank[:, us_at:P], SQUARE)
+        ts_cols = [sb([P, PACK], F32, "ts_cols0"), sb([P, PACK], F32, "ts_cols1", V_AT)]
+        ts_rows = [sb([P, N], F32, "ts_rows0", V_AT + KB), sb([P, N], F32, "ts_rows1", V_AT + PLANE + 2 * KB)]
+        engines = (nc.vector, nc.scalar)
 
-        clear_window(nc.gpsimd, 2, "ts_first")
-
-        v_picked = sb([P, 2, B, N], U32, "v_picked")
-
-        def pick_items(u, words):
-            nc.vector.tensor_copy(v_picked[:, u].rearrange("p b (t q) -> p b q t", t=PACK), words.indirect(item_list[:]))
-
-        def turn_items(b, u, bank, laid):
-            words = v_picked[:, u, b, :].bitcast(F32)
-            turned = bank_tile([P, PACK, P], "v_bank", bank)
-            for t in range(PACK):
-                nc.tensor.transpose(turned[:, t, :], words[:, t * P : (t + 1) * P], ident[:])
-            halves = turned[:].rearrange("p t m -> p (t m)").bitcast(BF16)
-            nc.scalar.copy(laid.rearrange("p (e m t) -> p e m t", t=PACK, e=2), halves.rearrange("p (t m e) -> p e m t", t=PACK, e=2))
-
-        vt_mx = {}
-
-        def quantise_turned(u, groups, laid, tag):
-            mx = mx_tiles("vt%d_%d" % (u, groups[0]), len(groups) * 2 * P, tag)
-            quantise(mx, laid.rearrange("p b c -> p (b c)"), E4)
-            for place, b in enumerate(groups):
-                vt_mx[b, u] = (mx, place * 2 * P)
-
-        def weave(name, picked):
-            woven = sb([P, picked.shape[2], 2], U32, name)
-            nc.vector.tensor_copy(woven[:].bitcast(I32), picked.rearrange("p u c -> p c u").bitcast(I32))
-            return woven
-
-        def quantise_woven(name, woven):
-            mx = mx_tiles(name, woven.shape[1])
-            quantise(mx, woven[:].rearrange("p c u -> p (c u)").bitcast(BF16), E4)
-            return mx
-
-        pick_items(0, round_pair(0))
-        clear_window(nc.gpsimd, 2, "raw0_1408")
-        ts_cols = [sb([P, PACK], F32, "ts_cols0")]
-        ts_held = sb([P, B * N + 8], F32, "ts_held", "raw0_1024")
-        ts_cols.append(ts_held[:, B * N : B * N + PACK])
-        ts_rows = [ts_held[:, b * N : (b + 1) * N] for b in range(B)]
-        for b in range(B):
+        def ts_columns(b):
             turned = bank_tile([P, PACK, P], "ts_turned", 4 + b)
             for t in range(PACK):
-                nc.tensor.transpose(turned[:, t, :], ts_picked[:, b, t * P : (t + 1) * P], ident[:])
-            if b == 0:
-                nc.vector.tensor_copy(ts_cols[0][:], turned[:, :, 0])
-            else:
-                nc.scalar.copy(ts_cols[1], turned[:, :, 0])
-        for b in range(B):
+                nc.tensor.transpose(turned[:, t, :], by_place(ts_picked[b][:], b == 0)[:, t, :], ident[:])
+            move(engines[b], ts_cols[b][:], turned[:, :, P - 1])
+
+        def ts_spread(b):
             spread = bank_tile([P, PACK, P], "ts_spread", 6 + b)
             for t in range(PACK):
                 nc.tensor.transpose(spread[:, t, :], ts_cols[b][:, t : t + 1].to_broadcast([P, P]), ident[:])
-            nc.scalar.copy(ts_rows[b], spread[:].rearrange("p t q -> p (t q)"))
-        last_words = round_pair(1)
-        first_laid = sb([P, B, 2 * N], BF16, "first_laid", "raw1_0")
-        for b in range(B):
-            turn_items(b, 0, b, first_laid[:, b, :])
-        pick_items(1, last_words)
-        clear_window(nc.gpsimd, 2, "raw1_1664")
-        v_woven = weave("v_woven", v_picked[:].rearrange("p u b i -> p u (b i)"))
-        quantise_turned(0, (0, 1), first_laid[:], "pair1")
-        v_mx = quantise_woven("v", v_woven)
+            move(engines[b], ts_rows[b][:], spread[:].rearrange("p t q -> p (t q)"))
 
-        u_picked0 = sb([P, PACK, R], F32, "u_picked0")
-        u_picked1 = sb([P, 2, R], F32, "u_picked1")
+        v_picked = [sb([P, PACK, N], F32, "v_picked%d" % b, PICKED_AT + b * PLANE) for b in range(B)]
+        laid, vt_mx, v_mx = {}, {}, {}
+
+        def pick_items(j):
+            dealt = v_picked[0][:, j, :].rearrange("p (t q) -> p q t", t=PACK)
+            move(nc.vector, dealt, v_planes[j][:].indirect(entries(item_list, 0, N)))
+            move(nc.scalar, v_picked[1][:, j, :], v_planes[j][:].indirect(entries(item_list, N, B * N)))
+
+        def turn_items(j, at):
+            laid[j] = sb([P, B, P, PACK], BF16, "laid%d" % j, at)
+            for b in range(B):
+                turned = bank_tile([P, PACK, P], "v_bank", (B * j + b) % PACK)
+                for t in range(PACK):
+                    nc.tensor.transpose(turned[:, t, :], by_place(v_picked[b][:, j, :], b == 0)[:, t, :], ident[:])
+                move(engines[b], laid[j][:, b], turned[:].rearrange("p t m -> p m t"))
+
+        def quantise_turned(j, at=None):
+            vt_mx[j] = quantise("vt%d" % j, laid[j][:].rearrange("p b m t -> p (b m t)"), E4, at)
+
+        def weave(engine, woven, picked):
+            side_by_side = picked.rearrange("p j c -> p c j")
+            if engine is nc.gpsimd:
+                nc.gpsimd.tensor_scalar(woven, side_by_side, 1.0, 0.0, op0=MULT, op1=ADD)
+            else:
+                move(engine, woven, side_by_side)
+
+        def weave_items(engine, b, pieces):
+            woven = sb([P, N, PACK], BF16, "v_woven%d" % b, LATE_AT + 10 * KB)
+            for c0 in range(0, N, N // pieces):
+                weave(engine, woven[:, c0 : c0 + N // pieces, :], v_picked[b][:, :, c0 : c0 + N // pieces])
+            return woven
+
+        def quantise_woven(name, woven, fmt, at=None):
+            return quantise(name, woven[:].rearrange("p c j -> p (c j)"), fmt, at)
+
+        ts_columns(0)
+        pick_items(0)
+        ts_columns(1)
+        ts_spread(0)
+        pick_items(1)
+        turn_items(0, V_AT + PLANE)
+        ts_spread(1)
+        pick_items(2)
+        quantise_turned(0, V_AT + 2 * PLANE + 2 * KB)
+        turn_items(1, V_AT + 2 * PLANE)
+        pick_items(3)
+        quantise_turned(1, V_AT + 3 * PLANE + 2 * KB)
+        turn_items(2, V_AT + 3 * PLANE)
+        v_woven0 = weave_items(nc.vector, 0, 1)
 
         def pick_users(engine, j, r0, r1):
-            dst = u_picked0[:, j, r0:r1] if r0 < R else u_picked1[:, j, :]
-            gather(engine, dst, u_planes[j], entries(user_list, r0, r1))
-
-        def pick_late_users(k, tag):
-            picked = sb([P, 2, UNIT], F32, "u_late%d" % k, tag)
-            for j in range(2):
-                gather(nc.scalar, picked[:, j, :], u_planes[2 + j], entries(user_list, k * UNIT, (k + 1) * UNIT))
-            return picked
+            dst = u_first[:, j, r0:r1] if r0 < R else u_late[r0 // UNIT - 2][:, j, :]
+            move(engine, dst, u_planes[j][:].indirect(entries(user_list, r0, r1)))
 
         pick_users(nc.scalar, 0, 0, R)
-        pick_users(nc.scalar, 0, R, B * R)
-        last_laid = sb([P, B, 2 * N], BF16, "last_laid", "u0")
-        for b in range(B):
-            turn_items(b, 1, 2 + b, last_laid[:, b, :])
-        pick_users(nc.vector, 1, 0, UNIT)
-        pick_users(nc.scalar, 1, R, B * R)
-        pick_users(nc.scalar, 1, UNIT, R)
-        words1 = sb([P, 2, R], U32, "u_words1")
-        first_pairs = words1[:, 0, :].bitcast(BF16).rearrange("p (r e) -> p r e", e=2)
-        nc.gpsimd.tensor_scalar(first_pairs, u_picked1[:].rearrange("p e r -> p r e"), 1.0, 0.0, op0=MULT, op1=ADD)
-        pick_users(nc.vector, 2, 0, R)
-        first_woven = sb([P, UNIT, PACK], BF16, "u_woven0")
-        nc.vector.tensor_copy(first_woven[:, :, 0:3], u_picked0[:, 0:3, 0:UNIT].rearrange("p j r -> p r j"))
-        gather(nc.vector, first_woven[:, :, 3], u_planes[3], entries(user_list, 0, UNIT))
+        pick_users(nc.scalar, 0, 2 * UNIT, 3 * UNIT)
+        pick_users(nc.scalar, 0, 3 * UNIT, 4 * UNIT)
+        quantise_turned(2)
+        v_mx[0] = quantise_woven("v0", v_woven0, E4)
+        turn_items(3, PICKED_AT)
+        v_woven1 = weave_items(nc.gpsimd, 1, 2)
+        for j in (1, 2):
+            pick_users(nc.vector, j, 0, R)
+            pick_users(nc.scalar, j, 2 * UNIT, 3 * UNIT)
+            pick_users(nc.scalar, j, 3 * UNIT, 4 * UNIT)
+        woven0 = sb([P, UNIT, PACK], BF16, "u_woven0", LATE_AT + 2 * KB)
+        weave(nc.vector, woven0[:, :, 0:3], u_first[:, 0:3, 0:UNIT])
+        move(nc.vector, woven0[:, :, 3], u_planes[3][:].indirect(entries(user_list, 0, UNIT)))
         pick_users(nc.scalar, 3, UNIT, R)
-
-        def weave_users(woven, picked):
-            nc.vector.tensor_copy(woven, picked.rearrange("p j r -> p r j"))
-
-        def pair_users(words, picked):
-            nc.scalar.copy(words.bitcast(BF16).rearrange("p (r e) -> p r e", e=2), picked.rearrange("p e r -> p r e"))
-
-        def quantise_users(k, woven):
-            mx = mx_tiles("u%d" % k, UNIT)
-            quantise(mx, woven.rearrange("p r j -> p (r j)"), E4)
-            return mx
 
         targets = {}
         h_banks = {}
 
-        def scale_targets(k, tag):
-            targets[k] = sb([P, BLOCKS, PACK, P], F32, "target%d" % k, tag)
+        def scale_targets(k):
+            targets[k] = sb([P, BLOCKS, PACK, P], F32, "target%d" % k)
             for c in range(BLOCKS):
                 block = k * BLOCKS + c
-                target = targets[k][:, c]
                 rows_in = y_blocks[block].rearrange("p (q t) -> p q t", t=PACK)
-                nc.scalar.activation(target.rearrange("p t q -> p q t"), rows_in, COPY, scale=us_neg[:, block : block + 1])
+                nc.scalar.activation(targets[k][:, c].rearrange("p t q -> p q t"), rows_in, COPY, scale=us_neg[:, block : block + 1])
+
+        def weave_late_users(k, at=None):
+            woven = sb([P, UNIT, PACK], BF16, "u_woven%d" % k, at)
+            for c in range(BLOCKS):
+                weave(nc.gpsimd, woven[:, c * P : (c + 1) * P, :], u_late[k - 2][:, :, c * P : (c + 1) * P])
+            return woven
 
         def score(k, u_mx):
             banks = []
             for c in range(BLOCKS):
                 rows = slice(c * P, (c + 1) * P)
                 scores = bank_tile([P, N], "scores", (k * BLOCKS + c) % PACK)
-                slots = slice(k * UNIT // R * N, (k * UNIT // R + 1) * N)
+                items = v_mx[k * UNIT // R]
                 nc.tensor.matmul_mx(
                     scores[:], lhsT=u_mx[0][:, rows].bitcast(E4), lhsT_scale=u_mx[1][:, rows],
-                    rhs=v_mx[0][:, slots].bitcast(E4), rhs_scale=v_mx[1][:, slots], start=True, stop=True,
+                    rhs=items[0][:].bitcast(E4), rhs_scale=items[1][:], start=True, stop=True,
                 )
                 banks.append(scores)
             return banks
 
-        def model_block(k, c, scores):
+        def turn_targets(k):
+            for c in range(BLOCKS):
+                block = k * BLOCKS + c
+                h_banks[block] = bank_tile([P, PACK, P], "h_bank", H_BANKS[k] + c)
+                for t in range(PACK):
+                    turn_onto(h_banks[block][:, t, :], targets[k][:, c, t, :], t == 0, False)
+
+        def model_term(k, c, scores):
+            b = k * UNIT // R
             block = k * BLOCKS + c
             model = sb([P, N], F32, "model%d" % block)
-            nc.vector.scalar_tensor_tensor(model[:], scores[c][:], us_sq[:, block : block + 1], ts_rows[block // PACK], MULT, MULT)
-            h_banks[block] = bank_tile([P, PACK, P], "h_bank", H_BANKS[k] + c)
+            nc.vector.scalar_tensor_tensor(
+                by_place(model[:], True), by_place(scores[c][:], b == 0), us_sq[:, block : block + 1], by_place(ts_rows[b][:], True), MULT, MULT
+            )
             for t in range(PACK):
-                turn_onto(h_banks[block][:, t, :], model[:, t * P : (t + 1) * P], t == 0, False)
-            for t in range(PACK):
-                turn_onto(h_banks[block][:, t, :], targets[k][:, c, t, :], False, t == PACK - 1)
+                turn_onto(h_banks[block][:, t, :], model[:, t * P : (t + 1) * P], False, t == PACK - 1)
 
-        def finish_h(k, c, h):
+        def finish_h(k, c):
             places = ts_cols[k * UNIT // R][:].unsqueeze(1).to_broadcast([P, P, PACK])
-            nc.vector.tensor_tensor(h[:, c * P : (c + 1) * P, :], h_banks[k * BLOCKS + c][:].rearrange("p t r -> p r t"), places, MULT)
+            nc.vector.tensor_tensor(hs[k][:, c * P : (c + 1) * P, :], h_banks[k * BLOCKS + c][:].rearrange("p t r -> p r t"), places, MULT)
 
-        du_halves = [sb([P, 2, B * R], F32, "du%d" % half, ("pair0", "ts_table")[half]) for half in range(2)]
+        du_halves = [sb([P, 2, B * R], F32, "du%d" % half, U_AT + half * PLANE) for half in range(2)]
 
-        def products(k, h, halves=(0, 1)):
-            h_mx = mx_tiles("h%d" % k, UNIT)
-            quantise(h_mx, h[:].rearrange("p r t -> p (r t)"), E5)
+        def products(k, halves=(0, 1)):
+            h_mx = quantise_woven("h%d" % k, hs[k], E5)
+            cols = slice(k * UNIT // R * P, (k * UNIT // R + 1) * P)
             banks = {}
             for half in halves:
                 sums = bank_tile([P, 2, UNIT], "du_bank", H_BANKS[k] + half)
                 for s in range(2):
-                    vt, first = vt_mx[k * UNIT // R, half]
-                    cols = slice(first + s * P, first + (s + 1) * P)
+                    vt = vt_mx[2 * half + s]
                     nc.tensor.matmul_mx(
                         sums[:, s, :], lhsT=vt[0][:, cols].bitcast(E4), lhsT_scale=vt[1][:, cols],
                         rhs=h_mx[0][:].bitcast(E5), rhs_scale=h_mx[1][:], start=True, stop=True,
@@ -299,18 +270,10 @@ def tile_attend_gmf_sq_u_kernel(tc, uT, vT, y, us, ts, offs, uoffs, out):
             return banks
 
         def copy_out(engine, k, half, banks):
-            dst = du_halves[half][:, :, k * UNIT : (k + 1) * UNIT]
-            if engine is nc.vector:
-                nc.vector.tensor_copy(dst, banks[half][:])
-            else:
-                nc.scalar.copy(dst, banks[half][:])
+            move(engine, du_halves[half][:, :, k * UNIT : (k + 1) * UNIT], banks[half][:])
 
         def scatter(engine, j, r0, r1):
-            dst, src = windows[j][:].indirect(entries(user_list, r0, r1)), du_halves[j // 2][:, j % 2, r0:r1]
-            if engine is nc.vector:
-                nc.vector.tensor_copy(dst, src)
-            else:
-                nc.scalar.activation(dst, src, COPY)
+            move(engine, windows[j][:].indirect(entries(user_list, r0, r1)), du_halves[j // 2][:, j % 2, r0:r1])
 
         def scatter_unit(j, k):
             scatter(nc.scalar, j, k * UNIT, (k + 1) * UNIT)
@@ -318,73 +281,67 @@ def tile_attend_gmf_sq_u_kernel(tc, uT, vT, y, us, ts, offs, uoffs, out):
         def store(queue, j):
             queue.dma_start(out.rearrange("(m j) c -> m j c", j=PACK)[:, j, :], windows[j][:])
 
-        u_mx0 = quantise_users(0, first_woven[:])
-        scores0 = score(0, u_mx0)
-        woven1 = sb([P, UNIT, PACK], BF16, "u_woven1")
-        weave_users(woven1[:], u_picked0[:, :, UNIT:R])
-        quantise_turned(1, (0,), last_laid[:, 0:1, :], "u_woven0")
-        u_mx1 = quantise_users(1, woven1[:])
-        scores1 = score(1, u_mx1)
-        scale_targets(0, "raw0_0")
-        scale_targets(1, "raw1_1024")
-        late2 = pick_late_users(2, "y0")
-        pair_users(words1[:, 1, 0:UNIT], late2[:])
-        late3 = pick_late_users(3, "y2")
-        for c in range(BLOCKS):
-            model_block(0, c, scores0)
-        for c in range(BLOCKS):
-            model_block(1, c, scores1)
-        quantise_turned(1, (1,), last_laid[:, 1:2, :], "u1_codes")
-        h0 = sb([P, UNIT, PACK], BF16, "h0")
-        for c in range(BLOCKS):
-            finish_h(0, c, h0)
-        woven2 = weave("u_woven2", words1[:, :, 0:UNIT])
-        pair_users(words1[:, 1, UNIT:R], late3[:])
-        sums0 = products(0, h0)
-        u_mx2 = quantise_woven("u2", woven2)
-        scores2 = score(2, u_mx2)
-        scale_targets(2, "raw0_512")
+        scores0 = score(0, quantise_woven("u0", woven0, E4))
+        v_mx[1] = quantise_woven("v1", v_woven1, E4, LATE_AT + KB)
+        quantise_turned(3, LATE_AT + 3 * KB)
+        woven1 = sb([P, UNIT, PACK], BF16, "u_woven1", LATE_AT + 5 * KB)
+        weave(nc.vector, woven1[:], u_first[:, :, UNIT:R])
+        scores1 = score(1, quantise_woven("u1", woven1, E4))
+        scale_targets(0)
+        pick_users(nc.scalar, 3, 2 * UNIT, 3 * UNIT)
+        pick_users(nc.scalar, 3, 3 * UNIT, 4 * UNIT)
+        for k in (1, 2, 3):
+            scale_targets(k)
+        woven2 = weave_late_users(2, LATE_AT + 4 * KB)
+        woven3 = weave_late_users(3, LATE_AT + 6 * KB)
+        turn_targets(0)
+        model_term(0, 0, scores0)
+        model_term(0, 1, scores0)
+        turn_targets(1)
+        model_term(1, 0, scores1)
+        hs = [sb([P, UNIT, PACK], BF16, "h%d" % k, None if k else LATE_AT + 8 * KB) for k in range(PACK)]
+        finish_h(0, 0)
+        finish_h(0, 1)
+        sums0 = products(0)
+        scores2 = score(2, quantise_woven("u2", woven2, E4, LATE_AT + 8 * KB))
+        u_mx3 = quantise_woven("u3", woven3, E4, LATE_AT + 9 * KB)
         copy_out(nc.scalar, 0, 0, sums0)
         copy_out(nc.scalar, 0, 1, sums0)
-        scale_targets(3, "y0")
-        h1 = sb([P, UNIT, PACK], BF16, "h1")
-        for c in range(BLOCKS):
-            finish_h(1, c, h1)
-        woven3 = weave("u_woven3", words1[:, :, UNIT:R])
-        sums1 = products(1, h1)
-        u_mx3 = quantise_woven("u3", woven3)
+        model_term(1, 1, scores1)
         scores3 = score(3, u_mx3)
+        turn_targets(2)
+        finish_h(1, 0)
+        model_term(2, 0, scores2)
+        finish_h(1, 1)
+        model_term(2, 1, scores2)
+        sums1 = products(1)
+        turn_targets(3)
         scatter_unit(0, 0)
+        scatter_unit(2, 0)
         copy_out(nc.scalar, 1, 0, sums1)
         copy_out(nc.scalar, 1, 1, sums1)
-        for c in range(BLOCKS):
-            model_block(2, c, scores2)
-        for c in range(BLOCKS):
-            model_block(3, c, scores3)
-        h2 = sb([P, UNIT, PACK], BF16, "h2")
-        for c in range(BLOCKS):
-            finish_h(2, c, h2)
-        sums2 = products(2, h2, (1, 0))
+        model_term(3, 0, scores3)
+        finish_h(2, 0)
+        model_term(3, 1, scores3)
+        finish_h(2, 1)
+        finish_h(3, 0)
+        sums2 = products(2, (1, 0))
         scatter_unit(0, 1)
-        scatter(nc.scalar, 1, 0, WIDE)
         copy_out(nc.scalar, 2, 0, sums2)
         scatter_unit(0, 2)
-        h3 = sb([P, UNIT, PACK], BF16, "h3")
-        for c in range(BLOCKS):
-            finish_h(3, c, h3)
+        finish_h(3, 1)
         copy_out(nc.vector, 2, 1, sums2)
-        sums3 = products(3, h3)
-        clear_window(nc.gpsimd, 2, "h3_codes")
+        sums3 = products(3)
+        scatter(nc.vector, 2, UNIT, 3 * UNIT)
         copy_out(nc.scalar, 3, 0, sums3)
-        copy_out(nc.scalar, 3, 1, sums3)
+        copy_out(nc.vector, 3, 1, sums3)
         scatter_unit(0, 3)
         store(nc.sync, 0)
-        scatter(nc.vector, 2, 0, B * R - WIDE)
-        scatter(nc.scalar, 2, B * R - WIDE, B * R)
+        scatter_unit(2, 3)
         store(nc.sync, 2)
-        scatter_unit(1, 3)
-        scatter(nc.scalar, 1, WIDE, 2 * WIDE)
-        store(nc.scalar, 1)
-        scatter(nc.vector, 3, 0, 3 * UNIT)
-        scatter(nc.vector, 3, 3 * UNIT, 4 * UNIT)
+        scatter(nc.vector, 3, 0, B * R)
         store(nc.sync, 3)
+        scatter(nc.scalar, 1, B * R - WIDE, B * R)
+        scatter(nc.scalar, 1, 0, (B * R - WIDE) // 2)
+        scatter(nc.scalar, 1, (B * R - WIDE) // 2, B * R - WIDE)
+        store(nc.scalar, 1)

@@ -205,12 +205,18 @@ def tile_attend_gmf_sq_u_kernel(tc, uT, vT, y, us, ts, offs, uoffs, out):
         targets = {}
         h_banks = {}
 
-        def scale_targets(k):
-            targets[k] = sb([P, BLOCKS, PACK, P], F32, "target%d" % k)
+        def scale_targets(engine, k, at=None):
+            targets[k] = sb([P, BLOCKS, PACK, P], F32, "target%d" % k, at)
             for c in range(BLOCKS):
                 block = k * BLOCKS + c
-                rows_in = y_blocks[block].rearrange("p (q t) -> p q t", t=PACK)
-                nc.scalar.activation(targets[k][:, c].rearrange("p t q -> p q t"), rows_in, COPY, scale=us_neg[:, block : block + 1])
+                target = targets[k][:, c]
+                factor = us_neg[:, block : block + 1]
+                if engine is nc.scalar:
+                    rows_in = y_blocks[block].rearrange("p (q t) -> p q t", t=PACK)
+                    nc.scalar.activation(target.rearrange("p t q -> p q t"), rows_in, COPY, scale=factor)
+                else:
+                    rows_in = y_blocks[block].rearrange("p (l i t) -> p l t i", t=PACK, i=PACK)
+                    nc.gpsimd.tensor_scalar(target.rearrange("p t (l i) -> p l t i", i=PACK), rows_in, factor, 0.0, op0=MULT, op1=ADD)
 
         def weave_late_users(k, at=None):
             woven = sb([P, UNIT, PACK], BF16, "u_woven%d" % k, at)
@@ -254,14 +260,14 @@ def tile_attend_gmf_sq_u_kernel(tc, uT, vT, y, us, ts, offs, uoffs, out):
 
         du_halves = [sb([P, 2, B * R], F32, "du%d" % half, U_AT + half * PLANE) for half in range(2)]
 
-        def products(k, halves=(0, 1)):
+        def products(k):
             h_mx = quantise_woven("h%d" % k, hs[k], E5)
             cols = slice(k * UNIT // R * P, (k * UNIT // R + 1) * P)
             banks = {}
-            for half in halves:
+            for half in range(2):
                 sums = bank_tile([P, 2, UNIT], "du_bank", H_BANKS[k] + half)
                 for s in range(2):
-                    vt = vt_mx[2 * half + s]
+                    vt = vt_mx[2 * s + half]
                     nc.tensor.matmul_mx(
                         sums[:, s, :], lhsT=vt[0][:, cols].bitcast(E4), lhsT_scale=vt[1][:, cols],
                         rhs=h_mx[0][:].bitcast(E5), rhs_scale=h_mx[1][:], start=True, stop=True,
@@ -273,7 +279,7 @@ def tile_attend_gmf_sq_u_kernel(tc, uT, vT, y, us, ts, offs, uoffs, out):
             move(engine, du_halves[half][:, :, k * UNIT : (k + 1) * UNIT], banks[half][:])
 
         def scatter(engine, j, r0, r1):
-            move(engine, windows[j][:].indirect(entries(user_list, r0, r1)), du_halves[j // 2][:, j % 2, r0:r1])
+            move(engine, windows[j][:].indirect(entries(user_list, r0, r1)), du_halves[j % 2][:, j // 2, r0:r1])
 
         def scatter_unit(j, k):
             scatter(nc.scalar, j, k * UNIT, (k + 1) * UNIT)
@@ -287,11 +293,11 @@ def tile_attend_gmf_sq_u_kernel(tc, uT, vT, y, us, ts, offs, uoffs, out):
         woven1 = sb([P, UNIT, PACK], BF16, "u_woven1", LATE_AT + 5 * KB)
         weave(nc.vector, woven1[:], u_first[:, :, UNIT:R])
         scores1 = score(1, quantise_woven("u1", woven1, E4))
-        scale_targets(0)
+        scale_targets(nc.scalar, 0)
         pick_users(nc.scalar, 3, 2 * UNIT, 3 * UNIT)
         pick_users(nc.scalar, 3, 3 * UNIT, 4 * UNIT)
-        for k in (1, 2, 3):
-            scale_targets(k)
+        for k in (1, 2):
+            scale_targets(nc.scalar, k)
         woven2 = weave_late_users(2, LATE_AT + 4 * KB)
         woven3 = weave_late_users(3, LATE_AT + 6 * KB)
         turn_targets(0)
@@ -305,6 +311,7 @@ def tile_attend_gmf_sq_u_kernel(tc, uT, vT, y, us, ts, offs, uoffs, out):
         sums0 = products(0)
         scores2 = score(2, quantise_woven("u2", woven2, E4, LATE_AT + 8 * KB))
         u_mx3 = quantise_woven("u3", woven3, E4, LATE_AT + 9 * KB)
+        scale_targets(nc.gpsimd, 3, LATE_AT + 4 * KB)
         copy_out(nc.scalar, 0, 0, sums0)
         copy_out(nc.scalar, 0, 1, sums0)
         model_term(1, 1, scores1)
@@ -325,23 +332,24 @@ def tile_attend_gmf_sq_u_kernel(tc, uT, vT, y, us, ts, offs, uoffs, out):
         model_term(3, 1, scores3)
         finish_h(2, 1)
         finish_h(3, 0)
-        sums2 = products(2, (1, 0))
+        sums2 = products(2)
         scatter_unit(0, 1)
-        copy_out(nc.scalar, 2, 0, sums2)
-        scatter_unit(0, 2)
+        scatter(nc.scalar, 1, 0, WIDE)
         finish_h(3, 1)
+        copy_out(nc.vector, 2, 0, sums2)
         copy_out(nc.vector, 2, 1, sums2)
+        scatter_unit(0, 2)
         sums3 = products(3)
-        scatter(nc.vector, 2, UNIT, 3 * UNIT)
+        scatter(nc.vector, 2, UNIT, B * R - WIDE)
         copy_out(nc.scalar, 3, 0, sums3)
         copy_out(nc.vector, 3, 1, sums3)
         scatter_unit(0, 3)
         store(nc.sync, 0)
-        scatter_unit(2, 3)
+        scatter(nc.scalar, 2, B * R - WIDE, B * R)
         store(nc.sync, 2)
-        scatter(nc.vector, 3, 0, B * R)
+        scatter(nc.vector, 3, UNIT, B * R)
+        scatter(nc.vector, 3, 0, UNIT)
         store(nc.sync, 3)
-        scatter(nc.scalar, 1, B * R - WIDE, B * R)
-        scatter(nc.scalar, 1, 0, (B * R - WIDE) // 2)
-        scatter(nc.scalar, 1, (B * R - WIDE) // 2, B * R - WIDE)
+        scatter(nc.scalar, 1, (B * R + WIDE) // 2, B * R)
+        scatter(nc.scalar, 1, WIDE, (B * R + WIDE) // 2)
         store(nc.scalar, 1)

@@ -91,8 +91,11 @@ def tile_attend_gmf_sq_u_kernel(tc, uT, vT, y, us, ts, offs, uoffs, out):
         y_rows = y.rearrange("b (c p) i -> p (b c) i", p=P)
         y_blocks = []
         for c0, c1 in ((0, 1), (1, 2), (2, 4), (4, 6), (6, 8)):
-            rows_in = sb([P, c1 - c0, N], F32, "y%d" % c0)
-            nc.sync.dma_start(rows_in[:], y_rows[:, c0:c1, :])
+            if c0 == 1:
+                rows_in = u_late[0][:, 2:4, :].rearrange("p (c j) r -> p c (j r)", c=1)
+            else:
+                rows_in = sb([P, c1 - c0, N], F32, "y%d" % c0)[:]
+            nc.sync.dma_start(rows_in, y_rows[:, c0:c1, :])
             y_blocks.extend([rows_in[:, c, :] for c in range(c1 - c0)])
 
         nc.vector.memset(ts_table[0 : P - 1, :], 0.0)
@@ -152,11 +155,10 @@ def tile_attend_gmf_sq_u_kernel(tc, uT, vT, y, us, ts, offs, uoffs, out):
             vt_mx[j] = quantise("vt%d" % j, laid[j][:].rearrange("p b m t -> p (b m t)"), E4, at)
 
         def weave(engine, woven, picked):
-            side_by_side = picked.rearrange("p j c -> p c j")
             if engine is nc.gpsimd:
-                nc.gpsimd.tensor_scalar(woven, side_by_side, 1.0, 0.0, op0=MULT, op1=ADD)
+                nc.gpsimd.tensor_scalar(woven, picked.rearrange("p j c -> p c j"), 1.0, 0.0, op0=MULT, op1=ADD)
             else:
-                move(engine, woven, side_by_side)
+                nc.vector.tensor_copy(woven.rearrange("p (c i) j -> p c j i", i=PACK), picked.rearrange("p j (c i) -> p c j i", i=PACK))
 
         def weave_items(engine, b, pieces):
             woven = sb([P, N, PACK], BF16, "v_woven%d" % b, LATE_AT + 10 * KB)
@@ -193,10 +195,12 @@ def tile_attend_gmf_sq_u_kernel(tc, uT, vT, y, us, ts, offs, uoffs, out):
         v_mx[0] = quantise_woven("v0", v_woven0, E4)
         turn_items(3, PICKED_AT)
         v_woven1 = weave_items(nc.gpsimd, 1, 2)
-        for j in (1, 2):
-            pick_users(nc.vector, j, 0, R)
-            pick_users(nc.scalar, j, 2 * UNIT, 3 * UNIT)
-            pick_users(nc.scalar, j, 3 * UNIT, 4 * UNIT)
+        pick_users(nc.vector, 1, 0, R)
+        pick_users(nc.scalar, 1, 2 * UNIT, 3 * UNIT)
+        pick_users(nc.scalar, 1, 3 * UNIT, 4 * UNIT)
+        pick_users(nc.vector, 2, 0, UNIT)
+        pick_users(nc.scalar, 2, UNIT, R)
+        pick_users(nc.scalar, 2, 3 * UNIT, 4 * UNIT)
         woven0 = sb([P, UNIT, PACK], BF16, "u_woven0", LATE_AT + 2 * KB)
         weave(nc.vector, woven0[:, :, 0:3], u_first[:, 0:3, 0:UNIT])
         move(nc.vector, woven0[:, :, 3], u_planes[3][:].indirect(entries(user_list, 0, UNIT)))
@@ -294,6 +298,7 @@ def tile_attend_gmf_sq_u_kernel(tc, uT, vT, y, us, ts, offs, uoffs, out):
         weave(nc.vector, woven1[:], u_first[:, :, UNIT:R])
         scores1 = score(1, quantise_woven("u1", woven1, E4))
         scale_targets(nc.scalar, 0)
+        pick_users(nc.scalar, 2, 2 * UNIT, 3 * UNIT)
         pick_users(nc.scalar, 3, 2 * UNIT, 3 * UNIT)
         pick_users(nc.scalar, 3, 3 * UNIT, 4 * UNIT)
         for k in (1, 2):

@@ -120,7 +120,7 @@ def tile_attend_gmf_sq_u_kernel(tc, uT, vT, y, us, ts, offs, uoffs, out):
         nc.scalar.activation(us_neg[:], us_bank[:, us_at:P], COPY, scale=-1.0)
         nc.scalar.activation(us_sq[:], us_bank[:, us_at:P], SQUARE)
         ts_cols = [sb([P, PACK], F32, "ts_cols0"), sb([P, PACK], F32, "ts_cols1", V_AT)]
-        ts_rows = [sb([P, N], F32, "ts_rows0", V_AT + KB), sb([P, N], F32, "ts_rows1", V_AT + PLANE + 2 * KB)]
+        ts_rows = [sb([P, N], F32, "ts_rows0", V_AT + KB), sb([P, N], F32, "ts_rows1", U_AT + 3 * PLANE)]
         engines = (nc.vector, nc.scalar)
 
         def ts_columns(b):
@@ -143,13 +143,13 @@ def tile_attend_gmf_sq_u_kernel(tc, uT, vT, y, us, ts, offs, uoffs, out):
             move(nc.vector, dealt, v_planes[j][:].indirect(entries(item_list, 0, N)))
             move(nc.scalar, v_picked[1][:, j, :], v_planes[j][:].indirect(entries(item_list, N, B * N)))
 
-        def turn_items(j, at):
+        def turn_items(j, at, movers=engines):
             laid[j] = sb([P, B, P, PACK], BF16, "laid%d" % j, at)
             for b in range(B):
                 turned = bank_tile([P, PACK, P], "v_bank", (B * j + b) % PACK)
                 for t in range(PACK):
                     nc.tensor.transpose(turned[:, t, :], by_place(v_picked[b][:, j, :], b == 0)[:, t, :], ident[:])
-                move(engines[b], laid[j][:, b], turned[:].rearrange("p t m -> p m t"))
+                move(movers[b], laid[j][:, b], turned[:].rearrange("p t m -> p m t"))
 
         def quantise_turned(j, at=None):
             vt_mx[j] = quantise("vt%d" % j, laid[j][:].rearrange("p b m t -> p (b m t)"), E4, at)
@@ -161,7 +161,7 @@ def tile_attend_gmf_sq_u_kernel(tc, uT, vT, y, us, ts, offs, uoffs, out):
                 nc.vector.tensor_copy(woven.rearrange("p (c i) j -> p c j i", i=PACK), picked.rearrange("p j (c i) -> p c j i", i=PACK))
 
         def weave_items(engine, b, pieces):
-            woven = sb([P, N, PACK], BF16, "v_woven%d" % b, LATE_AT + 10 * KB)
+            woven = sb([P, N, PACK], BF16, "v_woven%d" % b, LATE_AT + 14 * KB)
             for c0 in range(0, N, N // pieces):
                 weave(engine, woven[:, c0 : c0 + N // pieces, :], v_picked[b][:, :, c0 : c0 + N // pieces])
             return woven
@@ -175,10 +175,9 @@ def tile_attend_gmf_sq_u_kernel(tc, uT, vT, y, us, ts, offs, uoffs, out):
         ts_spread(0)
         pick_items(1)
         turn_items(0, V_AT + PLANE)
-        ts_spread(1)
         pick_items(2)
         quantise_turned(0, V_AT + 2 * PLANE + 2 * KB)
-        turn_items(1, V_AT + 2 * PLANE)
+        turn_items(1, V_AT + 2 * PLANE, (nc.scalar, nc.scalar))
         pick_items(3)
         quantise_turned(1, V_AT + 3 * PLANE + 2 * KB)
         turn_items(2, V_AT + 3 * PLANE)
@@ -262,28 +261,37 @@ def tile_attend_gmf_sq_u_kernel(tc, uT, vT, y, us, ts, offs, uoffs, out):
             places = ts_cols[k * UNIT // R][:].unsqueeze(1).to_broadcast([P, P, PACK])
             nc.vector.tensor_tensor(hs[k][:, c * P : (c + 1) * P, :], h_banks[k * BLOCKS + c][:].rearrange("p t r -> p r t"), places, MULT)
 
-        du_halves = [sb([P, 2, B * R], F32, "du%d" % half, U_AT + half * PLANE) for half in range(2)]
+        du = sb([P, 2, 2, B * R], F32, "du", U_AT)
+
+        def multiply(sums, j, b, h_mx):
+            vt, cols = vt_mx[j], slice(b * P, (b + 1) * P)
+            nc.tensor.matmul_mx(
+                sums, lhsT=vt[0][:, cols].bitcast(E4), lhsT_scale=vt[1][:, cols],
+                rhs=h_mx[0][:].bitcast(E5), rhs_scale=h_mx[1][:], start=True, stop=True,
+            )
+
+        def first_products(c):
+            h_mx = quantise("h0_%d" % c, hs[0][:, c * P : (c + 1) * P, :].rearrange("p r t -> p (r t)"), E5)
+            sums = bank_tile([P, 2, 2, P], "du_bank", H_BANKS[0] + c)
+            for j in range(PACK):
+                multiply(sums[:, j % 2, j // 2, :], j, 0, h_mx)
+            nc.scalar.activation(du[:, :, :, c * P : (c + 1) * P], sums[:], COPY)
 
         def products(k):
             h_mx = quantise_woven("h%d" % k, hs[k], E5)
-            cols = slice(k * UNIT // R * P, (k * UNIT // R + 1) * P)
             banks = {}
             for half in range(2):
                 sums = bank_tile([P, 2, UNIT], "du_bank", H_BANKS[k] + half)
                 for s in range(2):
-                    vt = vt_mx[2 * s + half]
-                    nc.tensor.matmul_mx(
-                        sums[:, s, :], lhsT=vt[0][:, cols].bitcast(E4), lhsT_scale=vt[1][:, cols],
-                        rhs=h_mx[0][:].bitcast(E5), rhs_scale=h_mx[1][:], start=True, stop=True,
-                    )
+                    multiply(sums[:, s, :], 2 * s + half, k * UNIT // R, h_mx)
                 banks[half] = sums
             return banks
 
         def copy_out(engine, k, half, banks):
-            move(engine, du_halves[half][:, :, k * UNIT : (k + 1) * UNIT], banks[half][:])
+            move(engine, du[:, half, :, k * UNIT : (k + 1) * UNIT], banks[half][:])
 
         def scatter(engine, j, r0, r1):
-            move(engine, windows[j][:].indirect(entries(user_list, r0, r1)), du_halves[j % 2][:, j // 2, r0:r1])
+            move(engine, windows[j][:].indirect(entries(user_list, r0, r1)), du[:, j % 2, j // 2, r0:r1])
 
         def scatter_unit(j, k):
             scatter(nc.scalar, j, k * UNIT, (k + 1) * UNIT)
@@ -294,31 +302,31 @@ def tile_attend_gmf_sq_u_kernel(tc, uT, vT, y, us, ts, offs, uoffs, out):
         scores0 = score(0, quantise_woven("u0", woven0, E4))
         v_mx[1] = quantise_woven("v1", v_woven1, E4, LATE_AT + KB)
         quantise_turned(3, LATE_AT + 3 * KB)
-        woven1 = sb([P, UNIT, PACK], BF16, "u_woven1", LATE_AT + 5 * KB)
+        woven1 = sb([P, UNIT, PACK], BF16, "u_woven1", LATE_AT + 6 * KB)
         weave(nc.vector, woven1[:], u_first[:, :, UNIT:R])
         scores1 = score(1, quantise_woven("u1", woven1, E4))
         scale_targets(nc.scalar, 0)
         pick_users(nc.scalar, 2, 2 * UNIT, 3 * UNIT)
         pick_users(nc.scalar, 3, 2 * UNIT, 3 * UNIT)
         pick_users(nc.scalar, 3, 3 * UNIT, 4 * UNIT)
-        for k in (1, 2):
-            scale_targets(nc.scalar, k)
-        woven2 = weave_late_users(2, LATE_AT + 4 * KB)
-        woven3 = weave_late_users(3, LATE_AT + 6 * KB)
+        ts_spread(1)
+        scale_targets(nc.scalar, 1)
+        woven2 = weave_late_users(2, LATE_AT + 5 * KB)
+        woven3 = weave_late_users(3, LATE_AT + 7 * KB)
         turn_targets(0)
         model_term(0, 0, scores0)
         model_term(0, 1, scores0)
         turn_targets(1)
         model_term(1, 0, scores1)
-        hs = [sb([P, UNIT, PACK], BF16, "h%d" % k, None if k else LATE_AT + 8 * KB) for k in range(PACK)]
+        hs = [sb([P, UNIT, PACK], BF16, "h%d" % k, None if k else LATE_AT + 12 * KB) for k in range(PACK)]
         finish_h(0, 0)
         finish_h(0, 1)
-        sums0 = products(0)
-        scores2 = score(2, quantise_woven("u2", woven2, E4, LATE_AT + 8 * KB))
-        u_mx3 = quantise_woven("u3", woven3, E4, LATE_AT + 9 * KB)
-        scale_targets(nc.gpsimd, 3, LATE_AT + 4 * KB)
-        copy_out(nc.scalar, 0, 0, sums0)
-        copy_out(nc.scalar, 0, 1, sums0)
+        first_products(0)
+        first_products(1)
+        scores2 = score(2, quantise_woven("u2", woven2, E4, LATE_AT + 12 * KB))
+        u_mx3 = quantise_woven("u3", woven3, E4, LATE_AT + 13 * KB)
+        scale_targets(nc.gpsimd, 2, LATE_AT + 4 * KB)
+        scale_targets(nc.gpsimd, 3, LATE_AT + 8 * KB)
         model_term(1, 1, scores1)
         scores3 = score(3, u_mx3)
         turn_targets(2)

@@ -23,6 +23,8 @@ PACK = 4
 UNIT = 256
 BLOCKS = UNIT // P
 WIDE = 384
+FIRST_PIECE = UNIT + 32
+LAST_SHARE = FIRST_PIECE + WIDE
 ALIGN = 256
 KB = 1024
 PLANE = 8 * KB
@@ -75,6 +77,10 @@ def tile_attend_gmf_sq_u_kernel(tc, uT, vT, y, us, ts, offs, uoffs, out):
         def by_place(slots, dealt):
             return slots.rearrange("p (t q) -> p t q" if dealt else "p (q t) -> p t q", t=PACK)
 
+        def in_score_order(slots, dealt, b):
+            places = by_place(slots, dealt)
+            return places if b == 0 else places.rearrange("p t q -> p q t")
+
         item_list = keep.tile([P, B * N // 16], U16, name="item_list")
         user_list = keep.tile([P, B * R // 16], U16, name="user_list")
         ts_table = sb([P, T], F32, "ts_table")
@@ -120,7 +126,7 @@ def tile_attend_gmf_sq_u_kernel(tc, uT, vT, y, us, ts, offs, uoffs, out):
         nc.scalar.activation(us_neg[:], us_bank[:, us_at:P], COPY, scale=-1.0)
         nc.scalar.activation(us_sq[:], us_bank[:, us_at:P], SQUARE)
         ts_cols = [sb([P, PACK], F32, "ts_cols0"), sb([P, PACK], F32, "ts_cols1", V_AT)]
-        ts_rows = [sb([P, N], F32, "ts_rows0", V_AT + KB), sb([P, N], F32, "ts_rows1", U_AT + 3 * PLANE)]
+        ts_rows = [sb([P, N], F32, "ts_rows0", V_AT + KB), sb([P, N], F32, "ts_rows1", V_AT + PLANE + 2 * KB)]
         engines = (nc.vector, nc.scalar)
 
         def ts_columns(b):
@@ -133,7 +139,7 @@ def tile_attend_gmf_sq_u_kernel(tc, uT, vT, y, us, ts, offs, uoffs, out):
             spread = bank_tile([P, PACK, P], "ts_spread", 6 + b)
             for t in range(PACK):
                 nc.tensor.transpose(spread[:, t, :], ts_cols[b][:, t : t + 1].to_broadcast([P, P]), ident[:])
-            move(engines[b], ts_rows[b][:], spread[:].rearrange("p t q -> p (t q)"))
+            move(engines[b], in_score_order(ts_rows[b][:], b == 0, b), spread[:].rearrange("p t q -> p t q" if b == 0 else "p t q -> p q t"))
 
         v_picked = [sb([P, PACK, N], F32, "v_picked%d" % b, PICKED_AT + b * PLANE) for b in range(B)]
         laid, vt_mx, v_mx = {}, {}, {}
@@ -143,13 +149,13 @@ def tile_attend_gmf_sq_u_kernel(tc, uT, vT, y, us, ts, offs, uoffs, out):
             move(nc.vector, dealt, v_planes[j][:].indirect(entries(item_list, 0, N)))
             move(nc.scalar, v_picked[1][:, j, :], v_planes[j][:].indirect(entries(item_list, N, B * N)))
 
-        def turn_items(j, at, movers=engines):
+        def turn_items(j, at):
             laid[j] = sb([P, B, P, PACK], BF16, "laid%d" % j, at)
             for b in range(B):
                 turned = bank_tile([P, PACK, P], "v_bank", (B * j + b) % PACK)
                 for t in range(PACK):
                     nc.tensor.transpose(turned[:, t, :], by_place(v_picked[b][:, j, :], b == 0)[:, t, :], ident[:])
-                move(movers[b], laid[j][:, b], turned[:].rearrange("p t m -> p m t"))
+                move(engines[b], laid[j][:, b], turned[:].rearrange("p t m -> p m t"))
 
         def quantise_turned(j, at=None):
             vt_mx[j] = quantise("vt%d" % j, laid[j][:].rearrange("p b m t -> p (b m t)"), E4, at)
@@ -175,9 +181,10 @@ def tile_attend_gmf_sq_u_kernel(tc, uT, vT, y, us, ts, offs, uoffs, out):
         ts_spread(0)
         pick_items(1)
         turn_items(0, V_AT + PLANE)
+        ts_spread(1)
         pick_items(2)
         quantise_turned(0, V_AT + 2 * PLANE + 2 * KB)
-        turn_items(1, V_AT + 2 * PLANE, (nc.scalar, nc.scalar))
+        turn_items(1, V_AT + 2 * PLANE)
         pick_items(3)
         quantise_turned(1, V_AT + 3 * PLANE + 2 * KB)
         turn_items(2, V_AT + 3 * PLANE)
@@ -252,7 +259,8 @@ def tile_attend_gmf_sq_u_kernel(tc, uT, vT, y, us, ts, offs, uoffs, out):
             block = k * BLOCKS + c
             model = sb([P, N], F32, "model%d" % block)
             nc.vector.scalar_tensor_tensor(
-                by_place(model[:], True), by_place(scores[c][:], b == 0), us_sq[:, block : block + 1], by_place(ts_rows[b][:], True), MULT, MULT
+                in_score_order(model[:], True, b), in_score_order(scores[c][:], b == 0, b), us_sq[:, block : block + 1],
+                in_score_order(ts_rows[b][:], b == 0, b), MULT, MULT,
             )
             for t in range(PACK):
                 turn_onto(h_banks[block][:, t, :], model[:, t * P : (t + 1) * P], False, t == PACK - 1)
@@ -275,7 +283,8 @@ def tile_attend_gmf_sq_u_kernel(tc, uT, vT, y, us, ts, offs, uoffs, out):
             sums = bank_tile([P, 2, 2, P], "du_bank", H_BANKS[0] + c)
             for j in range(PACK):
                 multiply(sums[:, j % 2, j // 2, :], j, 0, h_mx)
-            nc.scalar.activation(du[:, :, :, c * P : (c + 1) * P], sums[:], COPY)
+            for halves in ((slice(0, 2),), (slice(0, 1), slice(1, 2)))[c]:
+                nc.scalar.activation(du[:, halves, :, c * P : (c + 1) * P], sums[:, halves], COPY)
 
         def products(k):
             h_mx = quantise_woven("h%d" % k, hs[k], E5)
@@ -300,17 +309,17 @@ def tile_attend_gmf_sq_u_kernel(tc, uT, vT, y, us, ts, offs, uoffs, out):
             queue.dma_start(out.rearrange("(m j) c -> m j c", j=PACK)[:, j, :], windows[j][:])
 
         scores0 = score(0, quantise_woven("u0", woven0, E4))
-        v_mx[1] = quantise_woven("v1", v_woven1, E4, LATE_AT + KB)
         quantise_turned(3, LATE_AT + 3 * KB)
         woven1 = sb([P, UNIT, PACK], BF16, "u_woven1", LATE_AT + 6 * KB)
         weave(nc.vector, woven1[:], u_first[:, :, UNIT:R])
+        v_mx[1] = quantise_woven("v1", v_woven1, E4, LATE_AT + KB)
         scores1 = score(1, quantise_woven("u1", woven1, E4))
         scale_targets(nc.scalar, 0)
         pick_users(nc.scalar, 2, 2 * UNIT, 3 * UNIT)
         pick_users(nc.scalar, 3, 2 * UNIT, 3 * UNIT)
         pick_users(nc.scalar, 3, 3 * UNIT, 4 * UNIT)
-        ts_spread(1)
-        scale_targets(nc.scalar, 1)
+        for k in (1, 2):
+            scale_targets(nc.scalar, k)
         woven2 = weave_late_users(2, LATE_AT + 5 * KB)
         woven3 = weave_late_users(3, LATE_AT + 7 * KB)
         turn_targets(0)
@@ -323,18 +332,17 @@ def tile_attend_gmf_sq_u_kernel(tc, uT, vT, y, us, ts, offs, uoffs, out):
         finish_h(0, 1)
         first_products(0)
         first_products(1)
+        model_term(1, 1, scores1)
         scores2 = score(2, quantise_woven("u2", woven2, E4, LATE_AT + 12 * KB))
         u_mx3 = quantise_woven("u3", woven3, E4, LATE_AT + 13 * KB)
-        scale_targets(nc.gpsimd, 2, LATE_AT + 4 * KB)
-        scale_targets(nc.gpsimd, 3, LATE_AT + 8 * KB)
-        model_term(1, 1, scores1)
+        scale_targets(nc.gpsimd, 3, LATE_AT + 5 * KB)
         scores3 = score(3, u_mx3)
         turn_targets(2)
         finish_h(1, 0)
-        model_term(2, 0, scores2)
         finish_h(1, 1)
-        model_term(2, 1, scores2)
+        model_term(2, 0, scores2)
         sums1 = products(1)
+        model_term(2, 1, scores2)
         turn_targets(3)
         scatter_unit(0, 0)
         scatter_unit(2, 0)
@@ -347,22 +355,22 @@ def tile_attend_gmf_sq_u_kernel(tc, uT, vT, y, us, ts, offs, uoffs, out):
         finish_h(3, 0)
         sums2 = products(2)
         scatter_unit(0, 1)
-        scatter(nc.scalar, 1, 0, WIDE)
+        scatter(nc.scalar, 1, 0, FIRST_PIECE)
         finish_h(3, 1)
+        sums3 = products(3)
         copy_out(nc.vector, 2, 0, sums2)
         copy_out(nc.vector, 2, 1, sums2)
         scatter_unit(0, 2)
-        sums3 = products(3)
-        scatter(nc.vector, 2, UNIT, B * R - WIDE)
-        copy_out(nc.scalar, 3, 0, sums3)
-        copy_out(nc.vector, 3, 1, sums3)
+        scatter(nc.vector, 2, UNIT, LAST_SHARE)
+        for engine, half, order in ((nc.scalar, 0, (0, 1)), (nc.vector, 1, (1, 0))):
+            for s in order:
+                move(engine, du[:, half, s, 3 * UNIT : 4 * UNIT], sums3[half][:, s, :])
         scatter_unit(0, 3)
         store(nc.sync, 0)
-        scatter(nc.scalar, 2, B * R - WIDE, B * R)
+        scatter(nc.scalar, 2, LAST_SHARE, B * R)
         store(nc.sync, 2)
-        scatter(nc.vector, 3, UNIT, B * R)
-        scatter(nc.vector, 3, 0, UNIT)
+        scatter(nc.vector, 3, 0, B * R)
         store(nc.sync, 3)
-        scatter(nc.scalar, 1, (B * R + WIDE) // 2, B * R)
-        scatter(nc.scalar, 1, WIDE, (B * R + WIDE) // 2)
+        scatter(nc.scalar, 1, FIRST_PIECE + WIDE, B * R)
+        scatter(nc.scalar, 1, FIRST_PIECE, FIRST_PIECE + WIDE)
         store(nc.scalar, 1)

@@ -93,7 +93,7 @@ def tile_attend_gmf_sq_u_kernel(tc, uT, vT, y, us, ts, offs, uoffs, out):
         nc.sync.dma_start(user_list[:], uoffs)
         u_planes = [load_plane(uT, j, "u%d" % j, U_AT) for j in range(PACK)]
         u_first = sb([P, PACK, R], F32, "u_first")
-        u_late = [sb([P, PACK, UNIT], F32, "u_late%d" % k) for k in range(2)]
+        u_late = [sb([P, PACK, UNIT], F32, "u_late%d" % k, None if k else LATE_AT + 18 * KB) for k in range(2)]
         y_rows = y.rearrange("b (c p) i -> p (b c) i", p=P)
         y_blocks = []
         for c0, c1 in ((0, 1), (1, 2), (2, 4), (4, 6), (6, 8)):
@@ -215,11 +215,10 @@ def tile_attend_gmf_sq_u_kernel(tc, uT, vT, y, us, ts, offs, uoffs, out):
         targets = {}
         h_banks = {}
 
-        def scale_targets(engine, k, at=None):
-            targets[k] = sb([P, BLOCKS, PACK, P], F32, "target%d" % k, at)
-            for c in range(BLOCKS):
-                block = k * BLOCKS + c
-                target = targets[k][:, c]
+        def scale_targets(engine, blocks, at=None):
+            for block in blocks:
+                targets[block] = sb([P, PACK, P], F32, "target%d" % block, at)
+                target = targets[block][:]
                 factor = us_neg[:, block : block + 1]
                 if engine is nc.scalar:
                     rows_in = y_blocks[block].rearrange("p (q t) -> p q t", t=PACK)
@@ -228,20 +227,22 @@ def tile_attend_gmf_sq_u_kernel(tc, uT, vT, y, us, ts, offs, uoffs, out):
                     rows_in = y_blocks[block].rearrange("p (l i t) -> p l t i", t=PACK, i=PACK)
                     nc.gpsimd.tensor_scalar(target.rearrange("p t (l i) -> p l t i", i=PACK), rows_in, factor, 0.0, op0=MULT, op1=ADD)
 
-        def weave_late_users(k, at=None):
-            woven = sb([P, UNIT, PACK], BF16, "u_woven%d" % k, at)
-            for c in range(BLOCKS):
-                weave(nc.gpsimd, woven[:, c * P : (c + 1) * P, :], u_late[k - 2][:, :, c * P : (c + 1) * P])
-            return woven
+        def weave_late_users(k, blocks, at):
+            woven = sb([P, len(blocks), P, PACK], BF16, "u_woven%d_%d" % (k, blocks[0]), at)
+            for n, c in enumerate(blocks):
+                weave(nc.gpsimd, woven[:, n], u_late[k - 2][:, :, c * P : (c + 1) * P])
+            return woven[:].rearrange("p n r j -> p (n r j)")
+
+        def by_block(u_mx):
+            return [(u_mx[0][:, c * P : (c + 1) * P], u_mx[1][:, c * P : (c + 1) * P]) for c in range(BLOCKS)]
 
         def score(k, u_mx):
             banks = []
             for c in range(BLOCKS):
-                rows = slice(c * P, (c + 1) * P)
                 scores = bank_tile([P, N], "scores", (k * BLOCKS + c) % PACK)
                 items = v_mx[k * UNIT // R]
                 nc.tensor.matmul_mx(
-                    scores[:], lhsT=u_mx[0][:, rows].bitcast(E4), lhsT_scale=u_mx[1][:, rows],
+                    scores[:], lhsT=u_mx[c][0].bitcast(E4), lhsT_scale=u_mx[c][1],
                     rhs=items[0][:].bitcast(E4), rhs_scale=items[1][:], start=True, stop=True,
                 )
                 banks.append(scores)
@@ -252,7 +253,7 @@ def tile_attend_gmf_sq_u_kernel(tc, uT, vT, y, us, ts, offs, uoffs, out):
                 block = k * BLOCKS + c
                 h_banks[block] = bank_tile([P, PACK, P], "h_bank", H_BANKS[k] + c)
                 for t in range(PACK):
-                    turn_onto(h_banks[block][:, t, :], targets[k][:, c, t, :], t == 0, False)
+                    turn_onto(h_banks[block][:, t, :], targets[block][:, t, :], t == 0, False)
 
         def model_term(k, c, scores):
             b = k * UNIT // R
@@ -308,41 +309,43 @@ def tile_attend_gmf_sq_u_kernel(tc, uT, vT, y, us, ts, offs, uoffs, out):
         def store(queue, j):
             queue.dma_start(out.rearrange("(m j) c -> m j c", j=PACK)[:, j, :], windows[j][:])
 
-        scores0 = score(0, quantise_woven("u0", woven0, E4))
+        scores0 = score(0, by_block(quantise_woven("u0", woven0, E4)))
         quantise_turned(3, LATE_AT + 3 * KB)
         woven1 = sb([P, UNIT, PACK], BF16, "u_woven1", LATE_AT + 6 * KB)
         weave(nc.vector, woven1[:], u_first[:, :, UNIT:R])
         v_mx[1] = quantise_woven("v1", v_woven1, E4, LATE_AT + KB)
-        scores1 = score(1, quantise_woven("u1", woven1, E4))
-        scale_targets(nc.scalar, 0)
+        scores1 = score(1, by_block(quantise_woven("u1", woven1, E4)))
+        pick_users(nc.scalar, 3, 3 * UNIT, 4 * UNIT)
+        scale_targets(nc.scalar, (0, 1))
         pick_users(nc.scalar, 2, 2 * UNIT, 3 * UNIT)
         pick_users(nc.scalar, 3, 2 * UNIT, 3 * UNIT)
-        pick_users(nc.scalar, 3, 3 * UNIT, 4 * UNIT)
-        for k in (1, 2):
-            scale_targets(nc.scalar, k)
-        woven2 = weave_late_users(2, LATE_AT + 5 * KB)
-        woven3 = weave_late_users(3, LATE_AT + 7 * KB)
+        scale_targets(nc.scalar, (2, 3, 4, 5))
+        woven3 = weave_late_users(3, (0, 1), LATE_AT + 7 * KB)
+        woven2 = [weave_late_users(2, (0,), LATE_AT + 6 * KB)]
         turn_targets(0)
         model_term(0, 0, scores0)
         model_term(0, 1, scores0)
         turn_targets(1)
         model_term(1, 0, scores1)
-        hs = [sb([P, UNIT, PACK], BF16, "h%d" % k, None if k else LATE_AT + 12 * KB) for k in range(PACK)]
+        hs = [sb([P, UNIT, PACK], BF16, "h%d" % k, (LATE_AT + 11 * KB, LATE_AT + 22 * KB, None, None)[k]) for k in range(PACK)]
         finish_h(0, 0)
         finish_h(0, 1)
         first_products(0)
         first_products(1)
+        woven2.append(weave_late_users(2, (1,), LATE_AT + 10 * KB + 2 * ALIGN))
         model_term(1, 1, scores1)
-        scores2 = score(2, quantise_woven("u2", woven2, E4, LATE_AT + 12 * KB))
-        u_mx3 = quantise_woven("u3", woven3, E4, LATE_AT + 13 * KB)
-        scale_targets(nc.gpsimd, 3, LATE_AT + 5 * KB)
+        finish_h(1, 0)
+        u_mx2 = [quantise("u2_%d" % c, woven2[c], E4, None if c else LATE_AT + 18 * KB) for c in range(BLOCKS)]
+        scores2 = score(2, [(codes[:], scales[:]) for codes, scales in u_mx2])
+        u_mx3 = by_block(quantise("u3", woven3, E4, LATE_AT + 19 * KB))
+        scale_targets(nc.gpsimd, (6,), LATE_AT + 8 * KB + 3 * ALIGN)
         scores3 = score(3, u_mx3)
         turn_targets(2)
-        finish_h(1, 0)
         finish_h(1, 1)
         model_term(2, 0, scores2)
-        sums1 = products(1)
         model_term(2, 1, scores2)
+        sums1 = products(1)
+        scale_targets(nc.gpsimd, (7,), LATE_AT + 22 * KB)
         turn_targets(3)
         scatter_unit(0, 0)
         scatter_unit(2, 0)

@@ -93,7 +93,7 @@ def tile_attend_gmf_sq_u_kernel(tc, uT, vT, y, us, ts, offs, uoffs, out):
         nc.sync.dma_start(user_list[:], uoffs)
         u_planes = [load_plane(uT, j, "u%d" % j, U_AT) for j in range(PACK)]
         u_first = sb([P, PACK, R], F32, "u_first")
-        u_late = [sb([P, PACK, UNIT], F32, "u_late%d" % k, None if k else LATE_AT + 18 * KB) for k in range(2)]
+        u_late = [sb([P, PACK, UNIT], F32, "u_late%d" % k) for k in range(2)]
         y_rows = y.rearrange("b (c p) i -> p (b c) i", p=P)
         y_blocks = []
         for c0, c1 in ((0, 1), (1, 2), (2, 4), (4, 6), (6, 8)):
@@ -163,6 +163,8 @@ def tile_attend_gmf_sq_u_kernel(tc, uT, vT, y, us, ts, offs, uoffs, out):
         def weave(engine, woven, picked):
             if engine is nc.gpsimd:
                 nc.gpsimd.tensor_scalar(woven, picked.rearrange("p j c -> p c j"), 1.0, 0.0, op0=MULT, op1=ADD)
+            elif engine is nc.scalar:
+                move(engine, woven, picked.rearrange("p j c -> p c j"))
             else:
                 nc.vector.tensor_copy(woven.rearrange("p (c i) j -> p c j i", i=PACK), picked.rearrange("p j (c i) -> p c j i", i=PACK))
 
@@ -227,11 +229,8 @@ def tile_attend_gmf_sq_u_kernel(tc, uT, vT, y, us, ts, offs, uoffs, out):
                     rows_in = y_blocks[block].rearrange("p (l i t) -> p l t i", t=PACK, i=PACK)
                     nc.gpsimd.tensor_scalar(target.rearrange("p t (l i) -> p l t i", i=PACK), rows_in, factor, 0.0, op0=MULT, op1=ADD)
 
-        def weave_late_users(k, blocks, at):
-            woven = sb([P, len(blocks), P, PACK], BF16, "u_woven%d_%d" % (k, blocks[0]), at)
-            for n, c in enumerate(blocks):
-                weave(nc.gpsimd, woven[:, n], u_late[k - 2][:, :, c * P : (c + 1) * P])
-            return woven[:].rearrange("p n r j -> p (n r j)")
+        def weave_late_users(engine, woven, k, c):
+            weave(engine, woven[:, c * P : (c + 1) * P, :], u_late[k - 2][:, :, c * P : (c + 1) * P])
 
         def by_block(u_mx):
             return [(u_mx[0][:, c * P : (c + 1) * P], u_mx[1][:, c * P : (c + 1) * P]) for c in range(BLOCKS)]
@@ -319,33 +318,37 @@ def tile_attend_gmf_sq_u_kernel(tc, uT, vT, y, us, ts, offs, uoffs, out):
         scale_targets(nc.scalar, (0, 1))
         pick_users(nc.scalar, 2, 2 * UNIT, 3 * UNIT)
         pick_users(nc.scalar, 3, 2 * UNIT, 3 * UNIT)
-        scale_targets(nc.scalar, (2, 3, 4, 5))
-        woven3 = weave_late_users(3, (0, 1), LATE_AT + 7 * KB)
-        woven2 = [weave_late_users(2, (0,), LATE_AT + 6 * KB)]
+        scale_targets(nc.scalar, (2, 3))
+        woven3 = sb([P, UNIT, PACK], BF16, "u_woven3", LATE_AT + 7 * KB)
+        woven2 = sb([P, UNIT, PACK], BF16, "u_woven2", LATE_AT + 5 * KB)
+        for c in range(BLOCKS):
+            weave_late_users(nc.gpsimd, woven3, 3, c)
+        weave_late_users(nc.gpsimd, woven2, 2, 0)
+        weave_late_users(nc.scalar, woven2, 2, 1)
+        scale_targets(nc.scalar, (4,))
         turn_targets(0)
         model_term(0, 0, scores0)
         model_term(0, 1, scores0)
         turn_targets(1)
         model_term(1, 0, scores1)
-        hs = [sb([P, UNIT, PACK], BF16, "h%d" % k, (LATE_AT + 11 * KB, LATE_AT + 22 * KB, None, None)[k]) for k in range(PACK)]
+        hs = [sb([P, UNIT, PACK], BF16, "h%d" % k, (LATE_AT + 11 * KB, LATE_AT + 19 * KB, None, None)[k]) for k in range(PACK)]
         finish_h(0, 0)
         finish_h(0, 1)
         first_products(0)
         first_products(1)
-        woven2.append(weave_late_users(2, (1,), LATE_AT + 10 * KB + 2 * ALIGN))
         model_term(1, 1, scores1)
-        finish_h(1, 0)
-        u_mx2 = [quantise("u2_%d" % c, woven2[c], E4, None if c else LATE_AT + 18 * KB) for c in range(BLOCKS)]
-        scores2 = score(2, [(codes[:], scales[:]) for codes, scales in u_mx2])
-        u_mx3 = by_block(quantise("u3", woven3, E4, LATE_AT + 19 * KB))
-        scale_targets(nc.gpsimd, (6,), LATE_AT + 8 * KB + 3 * ALIGN)
+        scores2 = score(2, by_block(quantise_woven("u2", woven2, E4, LATE_AT + 11 * KB)))
+        u_mx3 = by_block(quantise_woven("u3", woven3, E4, LATE_AT + 12 * KB))
+        scale_targets(nc.gpsimd, (5,), LATE_AT + 6 * KB)
         scores3 = score(3, u_mx3)
         turn_targets(2)
+        finish_h(1, 0)
         finish_h(1, 1)
         model_term(2, 0, scores2)
         model_term(2, 1, scores2)
         sums1 = products(1)
-        scale_targets(nc.gpsimd, (7,), LATE_AT + 22 * KB)
+        scale_targets(nc.gpsimd, (6,), LATE_AT + 18 * KB)
+        scale_targets(nc.gpsimd, (7,), LATE_AT + 20 * KB)
         turn_targets(3)
         scatter_unit(0, 0)
         scatter_unit(2, 0)

from contextlib import ExitStack

import concourse.mybir as mybir
from concourse.masks import make_identity

B, N, T, D, R, TU = 2, 512, 2048, 512, 512, 2048
FLOPS = 2 * 2 * B * N * R * D

F32 = mybir.dt.float32
BF16 = mybir.dt.bfloat16
U32 = mybir.dt.uint32
U16 = mybir.dt.uint16
U8 = mybir.dt.uint8
E4 = mybir.dt.float8_e4m3fn_x4
E5 = mybir.dt.float8_e5m2_x4
MULT = mybir.AluOpType.mult
ADD = mybir.AluOpType.add
SQUARE = mybir.ActivationFunctionType.Square
COPY = mybir.ActivationFunctionType.Copy

P = 128
PACK = 4
UNIT = 256
BLOCKS = UNIT // P
WIDE = 384
FIRST_PIECE = UNIT + 32
LAST_SHARE = FIRST_PIECE + WIDE
ALIGN = 256
KB = 1024
PLANE = 8 * KB
H_BANKS = (4, 6, 4, 0)
V_AT = 0
U_AT = 4 * PLANE
PICKED_AT = 8 * PLANE
LATE_AT = 10 * PLANE


def tile_attend_gmf_sq_u_kernel(tc, uT, vT, y, us, ts, offs, uoffs, out):
    nc = tc.nc
    with ExitStack() as ctx:
        keep = ctx.enter_context(tc.tile_pool(name="keep", bufs=1))
        shared = ctx.enter_context(tc.tile_pool(name="shared", bufs=1))
        psum = ctx.enter_context(tc.psum_pool(name="psum", bufs=1))

        def sb(shape, dtype, name, at=None):
            if at is None:
                return keep.tile(shape, dtype, name=name, align_bytes=ALIGN)
            return shared.tile(shape, dtype, name=name, align_bytes=ALIGN, offset=at)

        def bank_tile(shape, name, bank):
            return psum.tile(shape, F32, name=name, tag="bank%d" % bank)

        def entries(offsets, e0, e1):
            return offsets[:, e0 // 16 : e1 // 16]

        def move(engine, dst, src):
            if engine is nc.vector:
                nc.vector.tensor_copy(dst, src)
            else:
                nc.scalar.activation(dst, src, COPY)

        def load_plane(table, j, name, at):
            plane = sb([P, T], F32, name, at + j * PLANE)
            nc.sync.dma_start(plane[:], table.rearrange("(p j) c -> p j c", j=PACK)[:, j, :])
            return plane

        def quantise(name, src, fmt, at=None):
            width = src.shape[1] // PACK
            codes = sb([P, width], U32, name + "_codes", at)
            scales = sb([P, width], U8, name + "_scales")
            nc.vector.quantize_mx(codes[:].bitcast(fmt), scales[:], src)
            return codes, scales

        def turn_onto(dst, src, start, stop):
            nc.tensor.matmul(dst, src, ident[:], start=start, stop=stop, is_transpose=True)

        def by_place(slots, dealt):
            return slots.rearrange("p (t q) -> p t q" if dealt else "p (q t) -> p t q", t=PACK)

        def in_score_order(slots, dealt, b):
            places = by_place(slots, dealt)
            return places if b == 0 else places.rearrange("p t q -> p q t")

        item_list = keep.tile([P, B * N // 16], U16, name="item_list")
        user_list = keep.tile([P, B * R // 16], U16, name="user_list")
        ts_table = sb([P, T], F32, "ts_table")
        us_rows = sb([P, P], F32, "us_rows")
        us_at = P - B * PACK
        nc.sync.dma_start(item_list[:], offs)
        nc.sync.dma_start(ts_table[P - 1 : P, :], ts[0:1, :])
        nc.sync.dma_start(us_rows[us_at:P, :], us.rearrange("b (c p) o -> (b c) (p o)", p=P))
        v_planes = [load_plane(vT, j, "v%d" % j, V_AT) for j in range(PACK)]
        nc.sync.dma_start(user_list[:], uoffs)
        u_planes = [load_plane(uT, j, "u%d" % j, U_AT) for j in range(PACK)]
        u_first = sb([P, PACK, R], F32, "u_first")
        u_late = [sb([P, PACK, UNIT], F32, "u_late%d" % k) for k in range(2)]
        y_rows = y.rearrange("b (c p) i -> p (b c) i", p=P)
        y_blocks = []
        for c0, c1 in ((0, 1), (1, 2), (2, 4), (4, 6), (6, 8)):
            if c0 == 1:
                rows_in = u_late[0][:, 2:4, :].rearrange("p (c j) r -> p c (j r)", c=1)
            else:
                rows_in = sb([P, c1 - c0, N], F32, "y%d" % c0)[:]
            nc.sync.dma_start(rows_in, y_rows[:, c0:c1, :])
            y_blocks.extend([rows_in[:, c, :] for c in range(c1 - c0)])

        nc.vector.memset(ts_table[0 : P - 1, :], 0.0)
        nc.vector.memset(us_rows[0:us_at, :], 0.0)
        ident = sb([P, P], F32, "ident")
        make_identity(nc, ident[:])
        windows = [sb([P, TU], F32, "window%d" % j) for j in range(PACK)]
        for window in windows:
            for c0 in (0, TU // 2):
                nc.gpsimd.memset(window[:, c0 : c0 + TU // 2], 0.0)

        ts_picked = [sb([P, N], F32, "ts_picked%d" % b) for b in range(B)]
        nc.vector.tensor_copy(
            ts_picked[0][:].bitcast(U32).rearrange("p (t q) -> p q t", t=PACK),
            ts_table[:].bitcast(U32).indirect(entries(item_list, 0, N)),
        )
        move(nc.scalar, ts_picked[1][:], ts_table[:].indirect(entries(item_list, N, B * N)))
        us_bank = bank_tile([P, P], "us_bank", 3)
        nc.tensor.transpose(us_bank[:], us_rows[:], ident[:])
        us_neg = sb([P, B * PACK], F32, "us_neg")
        us_sq = sb([P, B * PACK], F32, "us_sq")
        nc.scalar.activation(us_neg[:], us_bank[:, us_at:P], COPY, scale=-1.0)
        nc.scalar.activation(us_sq[:], us_bank[:, us_at:P], SQUARE)
        ts_cols = [sb([P, PACK], F32, "ts_cols0"), sb([P, PACK], F32, "ts_cols1", V_AT)]
        ts_rows = [sb([P, N], F32, "ts_rows0", V_AT + KB), sb([P, N], F32, "ts_rows1", V_AT + PLANE + 2 * KB)]
        engines = (nc.vector, nc.scalar)

        def ts_columns(b):
            turned = bank_tile([P, PACK, P], "ts_turned", 4 + b)
            for t in range(PACK):
                nc.tensor.transpose(turned[:, t, :], by_place(ts_picked[b][:], b == 0)[:, t, :], ident[:])
            move(engines[b], ts_cols[b][:], turned[:, :, P - 1])

        def ts_spread(b):
            spread = bank_tile([P, PACK, P], "ts_spread", 6 + b)
            for t in range(PACK):
                nc.tensor.transpose(spread[:, t, :], ts_cols[b][:, t : t + 1].to_broadcast([P, P]), ident[:])
            move(engines[b], in_score_order(ts_rows[b][:], b == 0, b), spread[:].rearrange("p t q -> p t q" if b == 0 else "p t q -> p q t"))

        v_picked = [sb([P, PACK, N], F32, "v_picked%d" % b, PICKED_AT + b * PLANE) for b in range(B)]
        laid, vt_mx, v_mx = {}, {}, {}

        def pick_items(j):
            dealt = v_picked[0][:, j, :].rearrange("p (t q) -> p q t", t=PACK)
            move(nc.vector, dealt, v_planes[j][:].indirect(entries(item_list, 0, N)))
            move(nc.scalar, v_picked[1][:, j, :], v_planes[j][:].indirect(entries(item_list, N, B * N)))

        def turn_items(j, at):
            laid[j] = sb([P, B, P, PACK], BF16, "laid%d" % j, at)
            for b in range(B):
                turned = bank_tile([P, PACK, P], "v_bank", (B * j + b) % PACK)
                for t in range(PACK):
                    nc.tensor.transpose(turned[:, t, :], by_place(v_picked[b][:, j, :], b == 0)[:, t, :], ident[:])
                move(engines[b], laid[j][:, b], turned[:].rearrange("p t m -> p m t"))

        def quantise_turned(j, at=None):
            vt_mx[j] = quantise("vt%d" % j, laid[j][:].rearrange("p b m t -> p (b m t)"), E4, at)

        def weave(engine, woven, picked):
            if engine is nc.gpsimd:
                nc.gpsimd.tensor_scalar(woven, picked.rearrange("p j c -> p c j"), 1.0, 0.0, op0=MULT, op1=ADD)
            elif engine is nc.scalar:
                move(engine, woven, picked.rearrange("p j c -> p c j"))
            else:
                nc.vector.tensor_copy(woven.rearrange("p (c i) j -> p c j i", i=PACK), picked.rearrange("p j (c i) -> p c j i", i=PACK))

        def weave_items(engine, b, pieces):
            woven = sb([P, N, PACK], BF16, "v_woven%d" % b, LATE_AT + 14 * KB)
            for c0 in range(0, N, N // pieces):
                weave(engine, woven[:, c0 : c0 + N // pieces, :], v_picked[b][:, :, c0 : c0 + N // pieces])
            return woven

        def quantise_woven(name, woven, fmt, at=None):
            return quantise(name, woven[:].rearrange("p c j -> p (c j)"), fmt, at)

        ts_columns(0)
        pick_items(0)
        ts_columns(1)
        ts_spread(0)
        pick_items(1)
        turn_items(0, V_AT + PLANE)
        ts_spread(1)
        pick_items(2)
        quantise_turned(0, V_AT + 2 * PLANE + 2 * KB)
        turn_items(1, V_AT + 2 * PLANE)
        pick_items(3)
        quantise_turned(1, V_AT + 3 * PLANE + 2 * KB)
        turn_items(2, V_AT + 3 * PLANE)
        v_woven0 = weave_items(nc.vector, 0, 1)

        def pick_users(engine, j, r0, r1):
            dst = u_first[:, j, r0:r1] if r0 < R else u_late[r0 // UNIT - 2][:, j, :]
            move(engine, dst, u_planes[j][:].indirect(entries(user_list, r0, r1)))

        pick_users(nc.scalar, 0, 0, R)
        pick_users(nc.scalar, 0, 2 * UNIT, 3 * UNIT)
        pick_users(nc.scalar, 0, 3 * UNIT, 4 * UNIT)
        quantise_turned(2)
        v_mx[0] = quantise_woven("v0", v_woven0, E4)
        turn_items(3, PICKED_AT)
        v_woven1 = weave_items(nc.gpsimd, 1, 2)
        pick_users(nc.vector, 1, 0, R)
        pick_users(nc.scalar, 1, 2 * UNIT, 3 * UNIT)
        pick_users(nc.scalar, 1, 3 * UNIT, 4 * UNIT)
        pick_users(nc.vector, 2, 0, UNIT)
        pick_users(nc.scalar, 2, UNIT, R)
        pick_users(nc.scalar, 2, 3 * UNIT, 4 * UNIT)
        woven0 = sb([P, UNIT, PACK], BF16, "u_woven0", LATE_AT + 2 * KB)
        weave(nc.vector, woven0[:, :, 0:3], u_first[:, 0:3, 0:UNIT])
        move(nc.vector, woven0[:, :, 3], u_planes[3][:].indirect(entries(user_list, 0, UNIT)))
        pick_users(nc.scalar, 3, UNIT, R)

        targets = {}
        h_banks = {}

        def scale_targets(engine, blocks, at=None):
            for block in blocks:
                targets[block] = sb([P, PACK, P], F32, "target%d" % block, at)
                target = targets[block][:]
                factor = us_neg[:, block : block + 1]
                if engine is nc.scalar:
                    rows_in = y_blocks[block].rearrange("p (q t) -> p q t", t=PACK)
                    nc.scalar.activation(target.rearrange("p t q -> p q t"), rows_in, COPY, scale=factor)
                else:
                    rows_in = y_blocks[block].rearrange("p (l i t) -> p l t i", t=PACK, i=PACK)
                    nc.gpsimd.tensor_scalar(target.rearrange("p t (l i) -> p l t i", i=PACK), rows_in, factor, 0.0, op0=MULT, op1=ADD)

        def weave_late_users(engine, woven, k, c):
            weave(engine, woven[:, c * P : (c + 1) * P, :], u_late[k - 2][:, :, c * P : (c + 1) * P])

        def by_block(u_mx):
            return [(u_mx[0][:, c * P : (c + 1) * P], u_mx[1][:, c * P : (c + 1) * P]) for c in range(BLOCKS)]

        def score(k, u_mx):
            banks = []
            for c in range(BLOCKS):
                scores = bank_tile([P, N], "scores", (k * BLOCKS + c) % PACK)
                items = v_mx[k * UNIT // R]
                nc.tensor.matmul_mx(
                    scores[:], lhsT=u_mx[c][0].bitcast(E4), lhsT_scale=u_mx[c][1],
                    rhs=items[0][:].bitcast(E4), rhs_scale=items[1][:], start=True, stop=True,
                )
                banks.append(scores)
            return banks

        def turn_targets(k):
            for c in range(BLOCKS):
                block = k * BLOCKS + c
                h_banks[block] = bank_tile([P, PACK, P], "h_bank", H_BANKS[k] + c)
                for t in range(PACK):
                    turn_onto(h_banks[block][:, t, :], targets[block][:, t, :], t == 0, False)

        def model_term(k, c, scores):
            b = k * UNIT // R
            block = k * BLOCKS + c
            model = sb([P, N], F32, "model%d" % block)
            nc.vector.scalar_tensor_tensor(
                in_score_order(model[:], True, b), in_score_order(scores[c][:], b == 0, b), us_sq[:, block : block + 1],
                in_score_order(ts_rows[b][:], b == 0, b), MULT, MULT,
            )
            for t in range(PACK):
                turn_onto(h_banks[block][:, t, :], model[:, t * P : (t + 1) * P], False, t == PACK - 1)

        def finish_h(k, c):
            places = ts_cols[k * UNIT // R][:].unsqueeze(1).to_broadcast([P, P, PACK])
            nc.vector.tensor_tensor(hs[k][:, c * P : (c + 1) * P, :], h_banks[k * BLOCKS + c][:].rearrange("p t r -> p r t"), places, MULT)

        du = sb([P, 2, 2, B * R], F32, "du", U_AT)

        def multiply(sums, j, b, h_mx):
            vt, cols = vt_mx[j], slice(b * P, (b + 1) * P)
            nc.tensor.matmul_mx(
                sums, lhsT=vt[0][:, cols].bitcast(E4), lhsT_scale=vt[1][:, cols],
                rhs=h_mx[0][:].bitcast(E5), rhs_scale=h_mx[1][:], start=True, stop=True,
            )

        def first_products(c):
            h_mx = quantise("h0_%d" % c, hs[0][:, c * P : (c + 1) * P, :].rearrange("p r t -> p (r t)"), E5)
            sums = bank_tile([P, 2, 2, P], "du_bank", H_BANKS[0] + c)
            for j in range(PACK):
                multiply(sums[:, j % 2, j // 2, :], j, 0, h_mx)
            for halves in ((slice(0, 2),), (slice(0, 1), slice(1, 2)))[c]:
                nc.scalar.activation(du[:, halves, :, c * P : (c + 1) * P], sums[:, halves], COPY)

        def products(k):
            h_mx = quantise_woven("h%d" % k, hs[k], E5)
            banks = {}
            for half in range(2):
                sums = bank_tile([P, 2, UNIT], "du_bank", H_BANKS[k] + half)
                for s in range(2):
                    multiply(sums[:, s, :], 2 * s + half, k * UNIT // R, h_mx)
                banks[half] = sums
            return banks

        def copy_out(engine, k, half, banks):
            move(engine, du[:, half, :, k * UNIT : (k + 1) * UNIT], banks[half][:])

        def scatter(engine, j, r0, r1):
            move(engine, windows[j][:].indirect(entries(user_list, r0, r1)), du[:, j % 2, j // 2, r0:r1])

        def scatter_unit(j, k):
            scatter(nc.scalar, j, k * UNIT, (k + 1) * UNIT)

        def store(queue, j):
            queue.dma_start(out.rearrange("(m j) c -> m j c", j=PACK)[:, j, :], windows[j][:])

        scores0 = score(0, by_block(quantise_woven("u0", woven0, E4)))
        quantise_turned(3, LATE_AT + 3 * KB)
        woven1 = sb([P, UNIT, PACK], BF16, "u_woven1", LATE_AT + 6 * KB)
        weave(nc.vector, woven1[:], u_first[:, :, UNIT:R])
        v_mx[1] = quantise_woven("v1", v_woven1, E4, LATE_AT + KB)
        scores1 = score(1, by_block(quantise_woven("u1", woven1, E4)))
        pick_users(nc.scalar, 3, 3 * UNIT, 4 * UNIT)
        scale_targets(nc.scalar, (0, 1))
        pick_users(nc.scalar, 2, 2 * UNIT, 3 * UNIT)
        pick_users(nc.scalar, 3, 2 * UNIT, 3 * UNIT)
        scale_targets(nc.scalar, (2, 3))
        woven3 = sb([P, UNIT, PACK], BF16, "u_woven3", LATE_AT + 7 * KB)
        woven2 = sb([P, UNIT, PACK], BF16, "u_woven2", LATE_AT + 5 * KB)
        for c in range(BLOCKS):
            weave_late_users(nc.gpsimd, woven3, 3, c)
        weave_late_users(nc.gpsimd, woven2, 2, 0)
        weave_late_users(nc.scalar, woven2, 2, 1)
        scale_targets(nc.scalar, (4,))
        turn_targets(0)
        model_term(0, 0, scores0)
        model_term(0, 1, scores0)
        turn_targets(1)
        model_term(1, 0, scores1)
        hs = [sb([P, UNIT, PACK], BF16, "h%d" % k, (LATE_AT + 11 * KB, LATE_AT + 19 * KB, None, None)[k]) for k in range(PACK)]
        finish_h(0, 0)
        finish_h(0, 1)
        first_products(0)
        first_products(1)
        model_term(1, 1, scores1)
        scores2 = score(2, by_block(quantise_woven("u2", woven2, E4, LATE_AT + 11 * KB)))
        u_mx3 = by_block(quantise_woven("u3", woven3, E4, LATE_AT + 12 * KB))
        scale_targets(nc.gpsimd, (5,), LATE_AT + 6 * KB)
        scores3 = score(3, u_mx3)
        turn_targets(2)
        finish_h(1, 0)
        finish_h(1, 1)
        model_term(2, 0, scores2)
        model_term(2, 1, scores2)
        sums1 = products(1)
        scale_targets(nc.gpsimd, (6,), LATE_AT + 18 * KB)
        scale_targets(nc.gpsimd, (7,), LATE_AT + 20 * KB)
        turn_targets(3)
        scatter_unit(0, 0)
        scatter_unit(2, 0)
        copy_out(nc.scalar, 1, 0, sums1)
        copy_out(nc.scalar, 1, 1, sums1)
        model_term(3, 0, scores3)
        finish_h(2, 0)
        model_term(3, 1, scores3)
        finish_h(2, 1)
        finish_h(3, 0)
        sums2 = products(2)
        scatter_unit(0, 1)
        scatter(nc.scalar, 1, 0, FIRST_PIECE)
        finish_h(3, 1)
        sums3 = products(3)
        copy_out(nc.vector, 2, 0, sums2)
        copy_out(nc.vector, 2, 1, sums2)
        scatter_unit(0, 2)
        scatter(nc.vector, 2, UNIT, LAST_SHARE)
        for engine, half, order in ((nc.scalar, 0, (0, 1)), (nc.vector, 1, (1, 0))):
            for s in order:
                move(engine, du[:, half, s, 3 * UNIT : 4 * UNIT], sums3[half][:, s, :])
        scatter_unit(0, 3)
        store(nc.sync, 0)
        scatter(nc.scalar, 2, LAST_SHARE, B * R)
        store(nc.sync, 2)
        scatter(nc.vector, 3, 0, B * R)
        store(nc.sync, 3)
        scatter(nc.scalar, 1, FIRST_PIECE + WIDE, B * R)
        scatter(nc.scalar, 1, FIRST_PIECE, FIRST_PIECE + WIDE)
        store(nc.scalar, 1)
